import numpy as np, ml_dtypes
CORES = [40,64,80,88,96,104,120,144]
N = 8
BF = ml_dtypes.bfloat16
NN, P, LN, RO = 384, 2, 192, 6
W = 8 * NN
ACT = (P * np.arange(LN)[None, :] + np.arange(RO)[:, None] % P).reshape(-1)
def states(rng):
    return (0.125 + 1.375 * rng.random((N, 8, 16, W))) * rng.choice(np.array([0.75, 1.0, 1.25]), (N, 8, 16, 1))
def parts(rng, few=(4, 6, 10, 16, 32)):
    o = rng.permutation(NN).reshape(NN // 32, 32); cl = np.empty(NN, np.int64); cl[o.reshape(-1)] = np.arange(NN) // 32
    sz = rng.permutation(np.resize(np.array(few), NN // 32))[cl]
    def member(c, n, shape, stray):
        m = o[c, (rng.random(shape) * n).astype(np.int64)]
        return np.where(rng.random(shape) < stray, rng.integers(0, NN, shape), m)
    ka = member(cl, sz, (N, 8, 16, NN), 0.04)
    for c in range(5):
        e = member(cl, sz, (N, 8, NN), 0.0); np.put_along_axis(ka, (e & 3)[:, :, None], e[:, :, None], 2)
    nm = 8 * member(cl, 32, (N, 8, 8, NN), 0.2) + rng.integers(0, 8, (N, 8, 8, NN))
    own = np.take_along_axis(ka, rng.integers(0, 4, (N, 8, 1, NN)), 2)[:, :, 0]
    wide_ = np.where(rng.random((N, 8, NN)) < 0.2, 32, sz)
    pv = np.where(rng.random((N, 8, NN)) < 0.35, own, member(cl, wide_, (N, 8, NN), 0.03))
    own = np.take_along_axis(ka[..., ACT], rng.integers(0, 4, (N, 8, 1, RO * LN)), 2)[:, :, 0]
    sp = np.where(rng.random((N, 8, RO * LN)) < 0.6, own, member(cl[ACT], 32, (N, 8, RO * LN), 0.1))
    proto = rng.integers(0, 4, (N, 8, 16, NN // 32))[..., cl]
    xa = np.where(rng.random((N, 8, 16, NN)) < 0.3, proto, rng.integers(0, 4, (N, 8, 16, NN)))
    return ka, nm, xa, pv, sp
def pack(ka, nm, xa, s, pv, sp):
    return {"ka": np.ascontiguousarray(ka).reshape(N, 128, NN).astype(np.int32), "nm": np.ascontiguousarray(nm).reshape(N, 64, NN).astype(np.int32),
            "xa": np.ascontiguousarray(xa).reshape(N, 128, NN).astype(np.float32).astype(BF), "s0": np.ascontiguousarray(s).reshape(N, 128, W).astype(np.float32).astype(BF),
            "pv": np.ascontiguousarray(pv).astype(np.int32), "sp": np.ascontiguousarray(sp).astype(np.int32)}
def setup_inputs(rng):
    ka, nm, xa, pv, sp = parts(rng)
    return pack(ka, nm, xa, states(rng), pv, sp)
def setup_inputs_spread(rng):
    ka, nm, xa, pv, sp = parts(rng)
    s = (0.125 + 0.875 * rng.random((N, 8, 16, W))) * np.exp2(rng.integers(-1, 2, (N, 8, 1, W)))
    s = np.where(rng.random((N, 8, 1, W)) > 0.0625, s, 0.0625)
    return pack(ka, nm, xa, s, pv, sp)
def setup_inputs_ends(rng):
    ka, nm, xa, pv, sp = parts(rng)
    def ends(x, hi, share):
        return np.where(rng.random(x.shape) < share, hi * rng.integers(0, 2, x.shape), x)
    kind = rng.integers(0, 4, (N, 8, 1, NN))
    ka = np.where(kind == 0, 0, np.where(kind == 1, NN - 1, ends(ka, NN - 1, 0.7)))
    nm = ends(nm, W - 1, 0.8); pv = ends(pv, NN - 1, 0.75); sp = ends(sp, NN - 1, 0.75)
    kind = rng.integers(0, 4, (N, 8, 1, NN))
    xa = np.where(kind == 0, 0, np.where(kind == 1, 3, 3 * rng.integers(0, 2, (N, 8, 16, NN))))
    u = P * (LN - 1); v = 0 if u == NN - 1 else NN - 1
    ka[:, :, :15, u] = 0; ka[:, :, 15, u] = NN - 1
    ka[:, :, 1:7, v] = 0; ka[:, :, 8:15, v] = rng.integers(0, NN - 3, (N, 8, 7)); ka[:, :, 15, v] = NN - 1
    ka[:, 0::2, 0, v] = 2; ka[:, 0::2, 7, v] = NN - 3; ka[:, 1::2, 0, v] = NN - 3; ka[:, 1::2, 7, v] = 2
    nm[:, :, 7, v] = W - 1; pv[:, :, u] = v
    for z in (2, NN - 3):
        xa[0::2, :, :, z] = xa[0::2, :, :, u]; xa[1::2, :, :, z] = 3 - xa[1::2, :, :, u]
    u2 = P * (LN - 2); v2 = 1
    ka[:, :, :, u2] = 5; ka[:, :, :7, v2] = 5; ka[:, :, 7, v2] = 0; ka[:, :, 8:, v2] = 5
    pv[:, :, u2] = v2; sp[:, :, LN - 2] = 7; xa[1::2, :, :, 0] = 3 - xa[1::2, :, :, u2]
    s = np.where(rng.random((N, 8, 16, W)) < 0.65, 2.0 - 1.9375 * rng.integers(0, 2, (N, 8, 16, W)), states(rng))
    s[..., W - 2] = 2.0625 - s[..., W - 1]
    return pack(ka, nm, xa, s, pv, sp)
def setup_inputs_corners(rng):
    ka, nm, xa, pv, sp = parts(rng); u = np.arange(NN); h = NN // 2
    for q in range(N):
        for g in range(8):
            c = (g + q) % 8
            if c == 0: pv[q, g] = u; sp[q, g] = ACT
            if c == 1: ka[q, g] = rng.integers(0, NN, NN)[None, :]
            if c == 2:
                ka[q, g] = 2 * rng.integers(0, h, (16, NN)) + (u >= h)[None, :]
                pv[q, g] = np.where(u < h, h + rng.integers(0, h, NN), rng.integers(0, h, NN))
            if c == 3:
                ka[q, g, :15] = rng.integers(0, h, (15, NN)); ka[q, g, 15] = NN - 1; nm[q, g, 7] = 8 * rng.permutation(NN) + 7
            if c == 4: xa[q, g] = 3
            if c == 5:
                ka[q, g, :7] = np.arange(7)[:, None]; ka[q, g, 8:15] = np.arange(7)[:, None]; ka[q, g, 15] = 0; ka[q, g, 7] = rng.integers(7, NN, NN)
            if c == 6: ka[q, g] = rng.permutation(NN)[:16][np.argsort(rng.random((16, NN)), axis=0)]
            if c == 7:
                pv[q, g] = NN - 1 if rng.random() < 0.5 else int(rng.integers(0, NN)); sp[q, g] = int(rng.integers(1, NN))
                k = rng.integers(0, 3, NN)[None, :]
                off = np.where(k == 0, 0, np.where(k == 1, (np.arange(16) == 15)[:, None].astype(np.int64), 1))
                xa[q, g] = (rng.integers(0, 4, (16, 1)) + off) & 3
    return pack(ka, nm, xa, states(rng), pv, sp)
def setup_inputs_ties(rng):
    ka, nm, xa, pv, sp = parts(rng, (4, 8, 16, 32))
    row = rng.integers(0, 16, (N, 8, 1, 1)); flip = rng.integers(0, 2, (N, 8, 1, NN))
    xa = (rng.integers(0, 4, (N, 8, 16, 1)) + (np.arange(16)[:, None] == row) * flip) & 3
    ka[:, :, 8:, ::2] = ka[:, :, :8, ::2]; ka[:, :, 5:8, 1::2] = ka[:, :, 3:4, 1::2]
    return pack(ka, nm, xa, states(rng), pv, sp)
def check_ranges(d):
    bad = []
    for k, lo, hi in (("ka", 0, NN - 1), ("nm", 0, W - 1), ("xa", 0, 3), ("pv", 0, NN - 1), ("sp", 0, NN - 1)):
        v = np.asarray(d[k]).astype(np.float64)
        if not (np.min(v) >= lo and np.max(v) <= hi and np.all(v == np.floor(v))): bad.append("range of " + k)
    v = np.asarray(d["s0"]).astype(np.float64)
    if not (np.min(v) >= 0.0625 and np.max(v) <= 2): bad.append("range of s0")
    return bad
def reference(ka, nm, xa, s0, pv, sp):
    a = ka.astype(np.int64).reshape(N, 8, 16, NN); x = xa.astype(np.float32).reshape(N, 8, 16, NN); S = s0.astype(np.float64).reshape(N, 8, 16, W)
    own = np.broadcast_to(8 * np.arange(NN)[None, :] + np.arange(8)[:, None], (N, 8, 8, NN))
    nam = np.concatenate([own, nm.astype(np.int64).reshape(N, 8, 8, NN)], axis=2)
    p = pv.astype(np.int64).reshape(N, 8, NN); spare = sp.astype(np.int64).reshape(N, 8, RO * LN); out = np.zeros((N, 8, 16, RO * LN))
    for t in range(RO):
        u = P * np.arange(LN) + t % P; v = p[:, :, u]
        au = a[:, :, :, u]; su = nam[:, :, :, u]
        av = np.take_along_axis(a, v[:, :, None], 3); nv = np.take_along_axis(nam, v[:, :, None], 3)
        eq = au[:, :, :, None, :] == av[:, :, None, :, :]
        m = np.where(np.any(eq, axis=3), np.take_along_axis(nv, np.argmax(eq, axis=3), 2), su)
        left = np.take_along_axis(S, su.reshape(N, 8, 1, 16 * LN), 3); right = np.take_along_axis(S, m.reshape(N, 8, 1, 16 * LN), 3)
        gate = 0.5 + 0.5 * np.tanh(0.5 * left)
        O = np.sum((gate * right).reshape(N, 8, 16, 16, LN), axis=3)
        out[:, :, :, t * LN:(t + 1) * LN] = O
        c = av[:, :, :8]; ok = (c != u) & ~np.any(eq, axis=2)[:, :, :8]
        xw = np.take_along_axis(x, c.reshape(N, 8, 1, 8 * LN), 3).reshape(N, 8, 16, 8, LN)
        cnt = np.sum(xw == x[:, :, :, u][:, :, :, None, :], axis=2)
        j = np.argmax(np.where(ok, cnt, -1), axis=2); some = np.any(ok, axis=2)
        w = np.where(some, np.take_along_axis(c, j[:, :, None], 2)[:, :, 0], spare[:, :, t * LN:(t + 1) * LN])
        p[:, :, u] = w
        if t == RO - 1: break
        row = v & 3; place = 8 * u + row
        same = np.take_along_axis(au, row[:, :, None], 2) == v[:, :, None]
        new = np.tanh(0.125 * O + np.where(same, np.take_along_axis(S, place[:, :, None], 3), 0.0))
        sh = 1 + t % (N - 1)
        gv = np.roll(np.roll(v, sh, axis=0), 1, axis=1); gnew = np.roll(np.roll(new, sh, axis=0), 1, axis=1); grow = 4 + (gv & 3)
        np.put_along_axis(S, place[:, :, None], new, 3); np.put_along_axis(S, (8 * u + grow)[:, :, None], gnew, 3)
        rr = 8 + (w & 7); an = np.array(au); nn = np.array(su)
        np.put_along_axis(an, row[:, :, None], v[:, :, None], 2); np.put_along_axis(an, grow[:, :, None], gv[:, :, None], 2)
        np.put_along_axis(an, rr[:, :, None], np.where(some[:, :, None], w[:, :, None], np.take_along_axis(au, rr[:, :, None], 2)), 2)
        np.put_along_axis(nn, rr[:, :, None], np.where(some[:, :, None], (8 * v + j)[:, :, None], np.take_along_axis(su, rr[:, :, None], 2)), 2)
        a[:, :, :, u] = an; nam[:, :, :, u] = nn
    return {"yo": out.reshape(N, 128, RO * LN).astype(np.float32), "yp": p.astype(np.float32)}

def check_inputs(d):
    bad = list(check_ranges(d))
    if not bad:
        for name, y in reference(**d).items():
            for q in range(N):
                v = np.abs(np.asarray(y[q], np.float64)); s = np.sqrt(np.mean(v * v))
                if v.max() > 4 * s or s < 2.0 ** 1: bad.append('%s of rank %d is uneven or too small' % (name, q))
    return bad

@@ -1,0 +1,593 @@
+from concourse.bass import DstId, RemoteDMATransfer
+from concourse.mybir import dt, AluOpType, AxisListType, ActivationFunctionType
+
+NN, LN, RO, W = 384, 192, 6, 3072
+F32, F16, BF, I32, U16 = "float32", "float16", "bfloat16", "int32", "uint16"
+SCAN_LAST = (4, 5)
+
+
+def _sb(n, d, p=128):
+    return ("sbuf", [p, n], d)
+
+
+SCRATCH = {
+    "KI": _sb(NN, I32), "KA": _sb(NN, F32), "NM": _sb(NN, F32), "NR": _sb(NN, I32), "X": _sb(NN, BF), "S": _sb(W, F32),
+    "PVI": _sb(NN, I32), "SPI": _sb(1152, I32), "PV16": _sb(NN, F16), "SP16": _sb(1152, F16), "ALT": _sb(72, F32),
+    "CI": _sb(4, I32), "CF": _sb(4, F32), "C2": _sb(16, F32), "IO": _sb(NN, F32), "IO8": _sb(NN, F32), "GB": _sb(128, F32),
+    "UBI": _sb(24, F32), "UB": _sb(48, F32), "JV": _sb(8, F32), "EQ": _sb(16, F32), "EQN": _sb(16, F32), "EQB": _sb(16, F32),
+    "PW": _sb(256, F32), "PH": _sb(256, F16), "MM": _sb(512, F32), "BLK": _sb(128, F16), "BLK8": _sb(128, BF),
+    "SEL": _sb(2048, F16), "RW": _sb(640, F16), "CE": _sb(144, BF), "CS": _sb(144, BF), "WU": _sb(128, BF), "DGC": _sb(128, BF),
+    "ONES": _sb(LN, BF), "C192": _sb(LN, BF), "B8": _sb(144, F16), "TA": _sb(NN, F32), "TA2": _sb(NN, F32), "TB": _sb(NN, F32),
+    "TC": _sb(896, F32), "TJ": _sb(128, F32), "RST": _sb(W, BF), "RSZ": _sb(LN, F32), "RS8": _sb(768, BF), "XU": _sb(W, BF), "UN": _sb(NN, BF),
+    "KV": _sb(LN, BF), "KU": _sb(LN, BF), "NV": _sb(LN, F16), "SU": _sb(LN, F16), "EA": _sb(LN, F32), "EU": _sb(LN, BF), "EM": _sb(LN, BF),
+    "A": _sb(W, F32), "RR": _sb(W, F32), "SG": _sb(1536, BF), "E": _sb(1536, BF), "KP": _sb(96, U16), "ML": _sb(288, U16),
+    "MI": _sb(LN, I32), "MJ": _sb(LN, I32), "M16": _sb(LN, F16), "ZT": _sb(LN, F32), "ZR": _sb(LN, F32), "BI": _sb(12, I32),
+    "QI": _sb(8 * 48, I32), "QU": _sb(8 * 36, U16), "VF": _sb(24, F32), "VS": _sb(5 * 12, F32), "GV": _sb(5 * 12, F32),
+    "LI": _sb(36, I32), "LJ": _sb(24, I32), "LU": _sb(5 * 36, U16), "T1": _sb(LN, F32), "T2": _sb(LN, F32), "T3": _sb(LN, F32),
+    "N1": _sb(LN, F32), "N2": _sb(LN, F32), "V8": _sb(LN, F32), "HG": _sb(LN, F32), "H8": _sb(LN, F32), "H8R": _sb(LN, F32),
+    "LLO": _sb(1536, F32), "LHI": _sb(1536, F32), "P": _sb(W, F32), "PS": _sb(768, F32), "TS": _sb(5 * LN, F32), "TL": _sb(5 * LN, F32),
+    "SL": _sb(LN, F32), "OB": _sb(RO * LN, F32), "YT": _sb(LN, F32), "YP": _sb(NN, F32),
+    "pD0": ("psum", [128, 512], F32), "pD1": ("psum", [128, 512], F32), "pD2": ("psum", [128, 512], F32), "pZ": ("psum", [128, 512], F32),
+    "pR": ("psum", [128, 512], F32), "pO": ("psum", [128, 512], F32), "pM": ("psum", [128, 512], F32), "pN": ("psum", [128, 512], F32),
+}
+DSEMS = ["dka", "dpv", "dsp", "dx", "ds0", "dn0", "dn1", "do0", "do1", "dyp"]
+SEMAPHORES = ["ev", "es", "et", "eg", "lsent"] + DSEMS + ["av%d" % t for t in range(5)] + ["at%d" % t for t in range(5)]
+
+OP = AluOpType
+AF = ActivationFunctionType
+
+
+def route(T, topo, r, t):
+    src, dst = T.cores[r], T.cores[(r + 1 + t % 7) % len(T.cores)]
+    if topo.may_write(src, dst):
+        return None, dst
+    c = [k for k in topo.cores_of(src) if k != src and T.rank_of(k) is None and topo.may_write(k, dst)]
+    c.sort(key=lambda k: topo.die(k) != topo.die(src))
+    return c[0], dst
+
+
+def messages():
+    return [("v", 0), ("v", 1), ("v", 2), ("t", 0), ("v", 3), ("t", 1), ("v", 4), ("t", 2), ("t", 3), ("t", 4)]
+
+
+def land(T, kind, t):
+    return T.GV[:, 12 * t:12 * t + 12] if kind == "v" else T.TL[:, LN * t:LN * t + LN]
+
+
+def relay_program(g, core, T, topo):
+    total = 0
+    for r in range(len(T.cores)):
+        for kind, t in messages():
+            via, dst = route(T, topo, r, t)
+            if via != core:
+                continue
+            sem = T.sem["a%s%d" % (kind, t)]
+            g.wait_ge(sem, len(topo.engines(T.cores[r], core)))
+            rid, pid = topo.addr(dst, core)
+            g.remote_dma(land(T, kind, t), land(T, kind, t), sem, T.sem.lsent, pid, rid, topo.mask(core, dst))
+            total += len(topo.engines(core, dst))
+    if total:
+        g.wait_ge(T.sem.lsent, total)
+
+
+def emit(g, T, ops):
+    queue = {"v": g.vector, "s": g.scalar, "t": g.tensor, "g": g, "y": g.sync}
+    lastw, readers, deps, need = {}, {}, [], set()
+    for i, o in enumerate(ops):
+        d = set()
+        for x in o["r"]:
+            if x in lastw:
+                d.add(lastw[x])
+            if x[0] == "p":
+                d.update(k for k in readers.get(x, []) if ops[k]["e"] != o["e"])
+        for x in o["w"]:
+            if x in lastw and not (x[0] == "p" and o["e"] == "t" and ops[lastw[x]]["e"] == "t"):
+                d.add(lastw[x])
+            d.update(readers.get(x, []))
+        d.discard(i)
+        for x in o["r"]:
+            readers.setdefault(x, []).append(i)
+        for x in o["w"]:
+            lastw[x] = i
+            readers[x] = []
+        last = {}
+        for k in d:
+            key = ops[k].get("dma") or ops[k]["e"]
+            last[key] = max(last.get(key, -1), k)
+        deps.append(sorted(last.values()))
+        need.update(last.values())
+    count, mark, seen = {}, {}, {}
+    for i, o in enumerate(ops):
+        e = o["e"]
+        waits = [mark[k] for k in deps[i]] + o.get("wait", [])
+        for s, n in waits:
+            if seen.get((e, s), 0) < n:
+                queue[e].wait_ge(T.sem[s], n)
+                seen[(e, s)] = n
+        res = o["f"](queue[e])
+        if o.get("dma"):
+            for ins in res:
+                ins.then_inc(T.sem[o["dma"]], 16)
+            count[o["dma"]] = 16 * len(res)
+            mark[i] = (o["dma"], 16 * len(res))
+        elif i in need:
+            s = "e" + e
+            res.then_inc(T.sem[s], 1)
+            count[s] = count.get(s, 0) + 1
+            mark[i] = (s, count[s])
+    return count
+
+
+def rank_program(g, core, T, topo):
+    rank = T.rank_of(core)
+    if rank is None:
+        relay_program(g, core, T, topo)
+        return
+    nr = len(T.cores)
+    ops = []
+    sent = [0]
+
+    def add(e, f, r, w, **k):
+        ops.append(dict(e=e, f=f, r=r.split(), w=w.split(), **k))
+
+    def ts(out, in0, s1, s2, o0, o1, r, w, **k):
+        if o1 is None:
+            add("v", lambda q: q.tensor_scalar(out, in0, s1, None, o0), r, w, **k)
+        else:
+            add("v", lambda q: q.tensor_scalar(out, in0, s1, s2, o0, o1), r, w, **k)
+
+    def tt(out, a, b, o, r, w):
+        add("v", lambda q: q.tensor_tensor(out, a, b, o), r, w)
+
+    def cp(out, a, r, w, **k):
+        add("v", lambda q: q.tensor_copy(out, a), r, w, **k)
+
+    def ms(out, c, w):
+        add("v", lambda q: q.memset(out, c), "", w)
+
+    def scan(out, d0, d1, o0, o1, r, w):
+        add("v", lambda q: q.tensor_tensor_scan(out, d0, d1, 0.0, o0, o1), r, w)
+
+    def act(out, a, f, r, w, bias=0.0, scale=1.0):
+        add("s", lambda q: q.activation(out, a, f, bias=bias, scale=scale), r, w)
+
+    def mm(out, terms, r, w, start=True, stop=True):
+        def f(q):
+            for i, (l, x) in enumerate(terms):
+                ins = q.matmul(out, l, x, start and i == 0, stop and i == len(terms) - 1)
+            return ins
+        add("t", f, r, w)
+
+    def iota(out, pat, base, cm, w, flt=True):
+        if flt:
+            add("g", lambda q: q.iota(out, pat, base, cm, allow_small_or_imprecise_dtypes=True), "", w)
+        else:
+            add("g", lambda q: q.iota(out, pat, base, cm), "", w)
+
+    def gcopy(out, a, n, r, w):
+        add("g", lambda q: q.affine_select(out, a, [[0, n]], OP.is_gt, 0.0, 1, 0), r, w)
+
+    def dma(e, sem, pairs, r, w):
+        add(e, lambda q: [q.dma_start(a, b) for a, b in pairs], r, w, dma=sem)
+
+    def send(kind, t, src, r):
+        via, dst = route(T, topo, rank, t)
+        to = dst if via is None else via
+        rid, pid = topo.addr(to, core)
+        sent[0] += len(topo.engines(core, to))
+        add("g", lambda q: q.remote_dma(land(T, kind, t), src, T.sem["a%s%d" % (kind, t)], T.sem.lsent, pid, rid, topo.mask(core, to)), r, "")
+
+    def arrival(kind, t):
+        s = (rank - 1 - t % 7) % nr
+        via, dst = route(T, topo, s, t)
+        return [("a%s%d" % (kind, t), len(topo.engines(T.cores[s] if via is None else via, core)))]
+
+    def names(p, n, a=0):
+        return " ".join("%s%d" % (p, i) for i in range(a, n))
+
+    def vl(t):
+        return T.QU[:, 36 * t:36 * t + 12]
+
+    def weave(*parts):
+        lists = []
+        for f in parts:
+            n = len(ops)
+            f()
+            lists.append(ops[n:])
+            del ops[n:]
+        while any(lists):
+            for l in lists:
+                while l:
+                    o = l.pop(0)
+                    ops.append(o)
+                    if o["e"] == "v":
+                        break
+
+    col = lambda i: T.C2[:, i:i + 1]
+    PC, KC, GC, HC = T.CF[:, 0:1], T.CF[:, 1:2], T.CF[:, 2:3], T.CF[:, 3:4]
+    LO, HI, H0, H1, CC, B8C, G15, DC, K16 = [col(i) for i in range(9)]
+    IDN, ROT, UNR = T.PW[:, 0:128], T.PW[:, 112:240], T.PW[:, 16:144]
+    IH = T.PH[:, 0:128]
+    rw = lambda i: T.RW[:, 128 * i:128 * i + 128]
+    Sw = T.S[:, 0:W]
+    KAw, NMw = T.KA[:, 0:NN], T.NM[:, 0:NN]
+
+    def ku(t):
+        act(T.KU[:], T.KA[:, t % 2::2], AF.Identity, "KA", "KU", bias=24704.0, scale=-128.0)
+
+    def su(t):
+        ts(T.SU[:], T.NM[:, t % 2::2], -67072.0, None, OP.add, None, "NM", "SU")
+
+    def kv(t):
+        act(T.KV[:], KAw.indirect(vl(t)), AF.Identity, "KA QU%d" % t, "KV", bias=-24704.0, scale=128.0)
+        mm(T.pR[:, 0:96], [(rw(0), T.KV[:, 0::2]), (rw(1), T.KV[:, 1::2])], "RW0 RW1 KV", "pR")
+
+    def eu(t):
+        par = t % 2
+        mm(T.pN[:, 288:480], [(IH, T.KV[:]), (IH, T.UN[:, LN * par:LN * par + LN])], "PH0 KV UN%d" % par, "pN")
+        act(T.EA[:], T.pN[:, 288:480], AF.Abs, "pN", "EA")
+
+    def eu2(t):
+        act(T.EU[:], T.EA[:], AF.Sign, "EA", "EU", bias=-64.0)
+
+    def nv(t):
+        ts(T.NV[:], NMw.indirect(vl(t)), -67072.0, 1.0 / 2048, OP.add, OP.mult, "NM QU%d" % t, "NV")
+
+    def dmm(j):
+        b = "pD%d" % ((j // 2) % 3)
+        sel = T.SEL[:, 128 * j:128 * j + 128]
+        mm(T[b][:, LN * (j % 2):LN * (j % 2) + LN], [(sel, T.KV[:]), (IH, T.KU[:]), (sel, T.NV[:])], "SEL%d PH0 KV KU NV" % j, b)
+
+    def dabs(j):
+        b = "pD%d" % ((j // 2) % 3)
+        act(T.A[:, j::16], T[b][:, LN * (j % 2):LN * (j % 2) + LN], AF.Abs, b, "A%d" % j, bias=1536.0 + 4096.0 * j, scale=2048.0)
+
+    def match_first():
+        for j in range(16):
+            dmm(j)
+            if j % 2 and j < 10:
+                dabs(j - 1)
+                dabs(j)
+
+    def match_rest(t):
+        for j in range(10, 16):
+            dabs(j)
+        for j in range(8):
+            act(T.SG[:, LN * j:LN * j + LN], T.A[:, j::16], AF.Sign, "A%d" % j, "SG%d" % j, bias=-65535.0)
+
+    def kp(t):
+        ts(T.KP[:], T.pR[:, 0:96], 1.0 / 128, 192.0, OP.mult, OP.add, "pR", "KP")
+
+    def counts(t):
+        par = t % 2
+        tt(T.E[:], T.X[:, 0:NN].indirect(T.KP[:]), T.XU[:, 1536 * par:1536 * par + 1536], OP.is_equal, "X KP " + names("XU%d_" % par, 8), "E")
+
+    def same(t):
+        tt(T.EM[:], T.TA2[:, 0:NN].indirect(vl(t)), T.KA[:, t % 2::2], OP.is_equal, "TA2 KA QU%d" % t, "EM")
+        mm(T.pM[:, 0:LN], [(T.BLK8[:], T.EM[:])], "BLK8 EM", "pM")
+
+    def h8(t):
+        tt(T.H8[:], T.HG[:], T.pM[:, 0:LN], OP.mult, "HG pM", "H8")
+
+    def lowest(t):
+        scan(T.RR[:], T.RST[:], T.A[:], OP.add, OP.min, "RST " + names("A", 16), "RR")
+
+    def mchain(t):
+        tt(T.MI[:], T.RR[:, 15::16], T.NM[:, t % 2::2], OP.min, "RR NM", "MI")
+        mm(T.pR[:, 320:416], [(rw(2), T.SU[:, 0::2]), (rw(3), T.SU[:, 1::2])], "RW2 RW3 SU", "pR")
+        ts(T.MJ[:], T.MI[:], 4095, None, OP.bitwise_and, None, "MI", "MJ")
+        ts(T.M16[:], T.MJ[:], -1536.0, None, OP.add, None, "MJ", "M16")
+        mm(T.pR[:, 128:224], [(rw(0), T.M16[:, 0::2]), (rw(1), T.M16[:, 1::2])], "RW0 RW1 M16", "pR")
+        mm(T.pR[:, 224:320], [(rw(2), T.M16[:, 0::2]), (rw(3), T.M16[:, 1::2])], "RW2 RW3 M16", "pR")
+
+    def ml(t):
+        ts(T.ML[:], T.pR[:, 128:416], 1536.0, None, OP.add, None, "pR", "ML")
+
+    def zmm(t):
+        terms = [(T.CE[:, 15 - j:143 - j], T.E[:, j::8]) for j in range(8)]
+        terms += [(rw(4), T.KV[:]), (rw(4), T.C192[:]), (T.WU[:], T.EU[:]), (T.DGC[:], T.ONES[:])]
+        mm(T.pZ[:, 0:LN], terms, "CE E RW4 KV C192 WU EU DGC ONES", "pZ", stop=False)
+
+    def zmm2(t):
+        mm(T.pZ[:, 0:LN], [(T.CS[:, 15 - j:143 - j], T.SG[:, LN * j:LN * j + LN]) for j in range(8)], "CS " + names("SG", 8), "pZ", start=False)
+
+    def zchain(t):
+        add("v", lambda q: q.transpose(T.ZT[:], T.pZ[:, 0:LN]), "pZ", "ZT")
+        scan(T.ZR[:], T.RSZ[:], T.ZT[:], OP.mult, OP.max, "RSZ ZT", "ZR")
+        for e in range(2):
+            mm(T.pZ[:, 256 + e:268:2], [(T.MM[:, 256 * e + 128 * h:256 * e + 128 * h + 128], T.ZR[:, 16 * h + 15::32]) for h in range(2)],
+               names("MM", 4) + " ZR", "pZ")
+
+    def best(t):
+        tt(T.BI[:], T.pZ[:, 256:268], T.ALT[:, 12 * t:12 * t + 12], OP.max, "pZ ALT", "BI")
+
+    def i4(t):
+        s = t + 2
+        a, q = 48 * s, "QI%d" % s
+        ts(T.QI[:, a + 24:a + 36], T.BI[:], 7, None, OP.bitwise_and, None, "BI", q + "b")
+        ts(T.QI[:, a + 36:a + 48], T.BI[:], 6, 120, OP.logical_shift_right, OP.bitwise_and, "BI", q + "c")
+        ts(T.QI[:, a:a + 12], T.BI[:], 511, None, OP.bitwise_and, None, "BI", q)
+        ts(T.QI[:, a + 12:a + 24], T.BI[:], 1023, None, OP.bitwise_and, None, "BI", q + "a")
+        tt(T.QI[:, a + 24:a + 36], T.QI[:, a + 24:a + 36], T.QI[:, a + 36:a + 48], OP.add, q + "b " + q + "c", q + "b")
+
+    def vf(s):
+        cp(T.VF[:, 0:12], T.QI[:, 48 * s:48 * s + 12], "QI%d" % s, "VF")
+        mm(T.pN[:, 256:268], [(ROT, T.VF[:, 0:12])], "PW0 PW1 VF", "pN")
+
+    def qu(s, n=36):
+        q = "QI%d" % s
+        cp(T.QU[:, 36 * s:36 * s + n], T.QI[:, 48 * s:48 * s + n], "%s %sa %sb" % (q, q, q), "QU%d" % s)
+
+    def vsend(s):
+        act(T.VS[:, 12 * s:12 * s + 12], T.pN[:, 256:268], AF.Copy, "pN", "VS%d" % s)
+        send("v", s, T.VS[:, 12 * s:12 * s + 12], "VS%d" % s)
+
+    def lists(t):
+        par = t % 2
+        cp(T.LI[:, 24:36], T.GV[:, 12 * t:12 * t + 12], "", "LIc", wait=arrival("v", t))
+        ts(T.LJ[:, 0:12], T.QI[:, 48 * t:48 * t + 12], 3, None, OP.bitwise_and, None, "QI%d" % t, "LJa")
+        ts(T.LJ[:, 12:24], T.LI[:, 24:36], 3, None, OP.bitwise_and, None, "LIc", "LJb")
+        tt(T.LI[:, 0:24], T.LJ[:], T.UB[:, 24 * par:24 * par + 24], OP.add, "LJa LJb UB%d" % par, "LIa")
+        cp(T.LU[:, 36 * t:36 * t + 36], T.LI[:], "LIa LIc", "LU%d" % t)
+
+    def v8(t):
+        act(T.V8[:], T.IO8[:, 0:NN].indirect(vl(t)), AF.Identity, "IO8 QU%d" % t, "V8")
+
+    def advance(t):
+        par, s = t % 2, t + 2
+        tt(T.T1[:], T.TA[:, 0:NN].indirect(vl(t)), T.KA[:, par::2], OP.min, names("TA", 4) + " KA QU%d" % t, "T1")
+        best(t)
+        ku(t + 1)
+        tt(T.T2[:], T.TB[:, 0:NN].indirect(T.LU[:, 36 * t + 24:36 * t + 36]), T.T1[:], OP.min, names("TB", 4) + " T1 LU%d" % t, "T2")
+        i4(t)
+        su(t + 1)
+        qu(s)
+        if s < 5:
+            vf(s)
+        tt(T.T3[:], T.TC[:, 0:896].indirect(T.QU[:, 36 * s + 12:36 * s + 24]), T.T2[:], OP.min, names("TC", 9) + " T2 QU%d" % s, "T3")
+        act(T.KA[:, par::2], T.T3[:], AF.Abs, "T3", "KA")
+        tt(T.N1[:], T.TJ[:, 0:128].indirect(T.QU[:, 36 * s + 24:36 * s + 36]), T.V8[:], OP.subtract, names("TJ", 8) + " V8 QU%d" % s, "N1")
+        kv(t + 1)
+        tt(T.N2[:], T.N1[:], T.NM[:, par::2], OP.min, "N1 NM", "N2")
+        act(T.NM[:, par::2], T.N2[:], AF.Abs, "N2", "NM")
+        eu(t + 1)
+        if t == 0:
+            h8(0)
+        if t + 1 < 5:
+            same(t + 1)
+        kp(t + 1)
+        nv(t + 1)
+        if s < 5:
+            vsend(s)
+        eu2(t + 1)
+        match_first()
+        if t > 0:
+            own(t - 1)
+        else:
+            spares(12, 72)
+            ms(T.RS8[:, 0::8], 0.0, "RS8")
+        counts(t + 1)
+        zmm(t + 1)
+
+    def spares(a, b):
+        cp(T.SP16[0:8, 16 * a:16 * b], T.SPI[0:8, 16 * a:16 * b], "SPI", "SP16")
+
+    def spares2(a, b):
+        mm(T.pM[:, 400 + a:400 + b], [(T.B8[0:8, 15 - p:143 - p], T.SP16[0:8, 16 * a + p:16 * b:16]) for p in range(16)], "B8 SP16", "pM")
+
+    def alt(a, b):
+        act(T.ALT[:, a:b], T.pM[:, 400 + a:400 + b], AF.Identity, "pM", "ALT", bias=2096640.0)
+
+    def llo(t):
+        for k in range(8):
+            act(T.LLO[:, k::8], T.S[:, 8 * (t % 2) + k::16], AF.Sigmoid, "S", "LL%d" % k)
+
+    def hg(t):
+        act(T.HG[:], Sw.indirect(T.LU[:, 36 * t:36 * t + 12]), AF.Identity, "S LU%d" % t, "HG")
+
+    def products(t):
+        turn = ROT if t < 5 else IDN
+        for h in range(2):
+            act(T.LHI[:, 768 * h:768 * h + 768], Sw.indirect(T.ML[:, 192 + 48 * h:240 + 48 * h]), AF.Sigmoid, "S ML", "LH%d" % h)
+        for h in range(2):
+            for u in range(2):
+                a = 1536 * u + 768 * h
+                left = T.LHI[:, 768 * h:768 * h + 768] if u else T.LLO[:, 768 * h:768 * h + 768]
+                r = "P%d%d" % (h, u)
+                tt(T.P[:, a:a + 768], Sw.indirect(T.ML[:, 96 * u + 48 * h:96 * u + 48 * h + 48]), left, OP.mult,
+                   "S ML " + ("LH%d" % h if u else names("LL", 8)), r)
+                if h == 1 and u == 1 and t in SCAN_LAST:
+                    scan(T.PS[:], T.RS8[:], T.P[:, a:a + 768], OP.mult, OP.add, "RS8 " + r, "PS")
+                    terms, r = [(turn, T.PS[:, 7::8])], "PS"
+                else:
+                    terms = [(turn, T.P[:, a + k:a + 768:8]) for k in range(8)]
+                if u == 0 and t < 5:
+                    terms = [(ROT, T.H8[:, 96 * h:96 * h + 96])] + terms
+                    r += " H8"
+                mm(T.pO[:, 96 * h:96 * h + 96], terms, "PW0 PW1 " + r, "pO", start=(u == 0), stop=(u == 1))
+
+    def post(t):
+        ap = T.TS[:, LN * t:LN * t + LN]
+        act(ap, T.pO[:, 0:LN], AF.Sigmoid, "pO", "TS%d" % t, scale=0.25)
+        send("t", t, ap, "TS%d" % t)
+        mm(T.pM[:, LN:2 * LN], [(ROT, T.H8[:])], "PW0 PW1 H8", "pM")
+        mm(T.pN[:, 0:LN], [(UNR, ap)], "PW0 PW1 TS%d" % t, "pN")
+        act(T.H8R[:], T.pM[:, LN:2 * LN], AF.Copy, "pM", "H8R")
+        act(T.SL[:], T.pN[:, 0:LN], AF.Copy, "pN", "SL")
+
+    def own(t):
+        ts(Sw.indirect(T.LU[:, 36 * t:36 * t + 12]), T.SL[:], 2.0, -1.0, OP.mult, OP.add, "SL LU%d" % t, "S")
+
+    def outp(t):
+        tt(T.OB[:, LN * t:LN * t + LN], T.pO[:, 0:LN], T.H8R[:], OP.subtract, "pO H8R", "OB%d" % t)
+
+    def guest(t):
+        ts(Sw.indirect(T.LU[:, 36 * t + 12:36 * t + 24]), T.TL[:, LN * t:LN * t + LN], 2.0, -1.0, OP.mult, OP.add, "LU%d" % t, "S",
+           wait=arrival("t", t))
+
+    def partners(par):
+        cp(T.YT[:], T.IO[:, 0:NN].indirect(vl(6 + par)), "IO QU%d" % (6 + par), "YT")
+        cp(T.YP[:, par::2], T.YT[:], "YT", "YP%d" % par)
+
+    ms(T.NR[:], 0, "NR0 NR1")
+    dma("y", "dpv", [(T.PVI[0:8, :], T.pv[:])], "", "PVI")
+    dma("s", "dka", [(T.KI[:], T.ka[:])], "", "KI")
+    dma("y", "dx", [(T.X[:], T.xa[:])], "", "X")
+    dma("y", "dn0", [(T.NR[16 * a + 8:16 * a + 16, :], T.nm[8 * a:8 * a + 8, :]) for a in range(4)], "", "NR0")
+    dma("s", "dn1", [(T.NR[16 * a + 8:16 * a + 16, :], T.nm[8 * a:8 * a + 8, :]) for a in range(4, 8)], "", "NR1")
+    dma("y", "dsp", [(T.SPI[0:8, :], T.sp[:])], "", "SPI")
+    iota(T.CI[:, 0:1], [[0, 1]], 0, 1, "CI0", False)
+    iota(T.IO[:], [[1, NN]], 0, 0, "IO")
+    iota(T.GB[:], [[16, 8], [0, 16]], 0, 0, "GB")
+    dma("g", "ds0", [(T.S[:], T.s0[:])], "", "S")
+    iota(T.UBI[:], [[4, 2], [256, 12]], 0, 0, "UBI")
+    iota(T.JV[:], [[1, 8]], -(7 + 65536 + 1048576), 0, "JV")
+    iota(T.RST[:, 0:1536], [[0, 1536]], 0, 0, "RSTa")
+    ts(T.CI[:, 1:2], T.CI[:, 0:1], 15, None, OP.bitwise_and, None, "CI0", "CI1")
+    ts(T.CI[:, 2:3], T.CI[:, 0:1], 112, None, OP.bitwise_and, None, "CI0", "CI2")
+    ts(T.CI[:, 3:4], T.CI[:, 0:1], 16, None, OP.bitwise_and, None, "CI0", "CI3")
+    ms(T.ONES[:], 1.0, "ONES")
+    cp(T.CF[:], T.CI[:], "CI0 CI1 CI2 CI3", "CF")
+    ms(T.C192[:], 24576.0, "C192")
+    ts(B8C, PC, 16.0, 15.0, OP.mult, OP.add, "CF", "B8C")
+    ts(LO, KC, 8.0, None, OP.is_lt, None, "CF", "LO")
+    ts(HI, KC, 8.0, None, OP.is_ge, None, "CF", "HI")
+    ts(T.EQ[:], T.IO[:, 0:16], KC, None, OP.is_equal, None, "IO CF", "EQ")
+    ts(T.B8[0:8, :], T.IO[0:8, 0:144], T.C2[0:8, 5:6], None, OP.is_equal, None, "IO B8C", "B8")
+    ts(CC, KC, LO, 65536.0, OP.mult, OP.add, "CF LO", "CC")
+    ts(T.BLK[:], T.GB[:], GC, None, OP.is_equal, None, "GB CF", "BLK")
+    ts(T.PH[:, 0:128], T.IO[:, 0:128], PC, None, OP.is_equal, None, "IO CF", "PH0")
+    ts(T.PH[:, 128:256], T.IO[:, 0:128], PC, None, OP.is_equal, None, "IO CF", "PH1")
+    act(T.IO8[:], T.IO[:], AF.Identity, "IO", "IO8", scale=8.0)
+    for par in range(2):
+        act(T.UN[:, LN * par:LN * par + LN], T.IO[:, par::2], AF.Identity, "IO", "UN%d" % par, bias=24576.0, scale=-128.0)
+    act(T.pD0[:, 0:NN], T.IO8[:], AF.Identity, "IO8 LO CC", "pD0", bias=CC, scale=LO)
+
+    def sel(a, b):
+        for j in range(a, b):
+            ts(T.SEL[:, 128 * j:128 * j + 128], T.BLK[:], T.EQ[:, j:j + 1], None, OP.mult, None, "BLK EQ", "SEL%d" % j)
+    sel(0, 4)
+    cp(T.PV16[0:8, :], T.PVI[0:8, :], "PVI", "PV16")
+    for par in range(2):
+        mm(T.pN[:, 12 * par:12 * par + 12], [(T.B8[0:8, 15 - p:143 - p], T.PV16[0:8, 2 * p + par::32]) for p in range(16)], "B8 PV16", "pN")
+    ts(T.KA[:], T.KI[:], 1.0, None, OP.add, None, "KI", "KA")
+    for k in range(8):
+        act(T.XU[:, k:1536:8], T.X[:, 0::2], AF.Copy, "X", "XU0_%d" % k)
+    ts(rw(0), T.PH[:, 0:128], LO, None, OP.mult, None, "PH0 LO", "RW0")
+    ts(rw(1), T.PH[:, 120:248], LO, None, OP.mult, None, "PH0 PH1 LO", "RW1")
+    ku(0)
+    tt(T.NM[:], T.pD0[:, 0:NN], T.NR[:], OP.add, "pD0 NR0 NR1", "NM")
+    for par in range(2):
+        cp(T.QU[:, 36 * par:36 * par + 12], T.pN[:, 12 * par:12 * par + 12], "pN", "QU%d" % par)
+    cp(T.VF[:], T.pN[:, 0:24], "pN", "VF")
+    kv(0)
+    nv(0)
+    sel(4, 16)
+    ts(T.PW[:, 0:128], T.IO[:, 0:128], PC, None, OP.is_equal, None, "IO CF", "PW0")
+    ts(T.PW[:, 128:256], T.IO[:, 0:128], PC, None, OP.is_equal, None, "IO CF", "PW1")
+    eu(0)
+    mm(T.pM[:, 480:504], [(ROT, T.VF[:])], "PW0 PW1 VF", "pM")
+    eu2(0)
+    match_first()
+    kp(0)
+    cp(T.VS[:, 0:24], T.pM[:, 480:504], "pM", "VS0 VS1")
+    send("v", 0, T.VS[:, 0:12], "VS0")
+    send("v", 1, T.VS[:, 12:24], "VS1")
+    iota(T.RST[:, 1536:W], [[0, 1536]], 0, 0, "RSTb")
+    iota(T.TJ[:], [[0, 128]], 1048576, 0, names("TJ", 8))
+    iota(T.TC[:, NN:896], [[0, 512]], 4096, 0, "TC8")
+    for k in range(8):
+        gcopy(T.XU[:, 1536 + k:W:8], T.X[:, 1::2], LN, "X", "XU1_%d" % k)
+    iota(T.RS8[:], [[0, 768]], 1, 0, "RS8")
+    for par in range(2):
+        cp(T.QI[:, 48 * par:48 * par + 12], T.VF[:, 12 * par:12 * par + 12], "VF", "QI%d" % par)
+    counts(0)
+    match_rest(0)
+    spares(0, 12)
+    spares2(0, 12)
+    ts(H0, HC, 0.0, None, OP.is_equal, None, "CF", "H0")
+    ts(H1, HC, 16.0, None, OP.is_equal, None, "CF", "H1")
+    ts(T.EQN[:], T.EQ[:], -1.0, None, OP.mult, None, "EQ", "EQN")
+    ts(T.EQB[:], T.EQ[:], -4097.0, 4096.0, OP.mult, OP.add, "EQ", "EQB")
+    ts(G15, GC, 15.0, None, OP.add, None, "CF", "G15")
+    ts(DC, KC, -1024.0, 7168.0 - 262144.0, OP.mult, OP.add, "CF", "DC")
+    ts(K16, KC, 16.0, None, OP.mult, None, "CF", "K16")
+    ts(rw(2), T.PH[:, 8:136], HI, None, OP.mult, None, "PH0 PH1 HI", "RW2")
+    ts(rw(3), IH, HI, None, OP.mult, None, "PH0 HI", "RW3")
+    ts(rw(4), IH, LO, 1.0 / 128, OP.mult, OP.mult, "PH0 LO", "RW4")
+    ts(T.WU[:], IH, LO, 262144.0, OP.mult, OP.mult, "PH0 LO", "WU")
+    ts(T.BLK8[:], T.BLK[:], 8.0, None, OP.mult, None, "BLK", "BLK8")
+    ms(T.RSZ[:], 1.0, "RSZ")
+    ts(T.CE[:], T.IO[:, 0:144], G15, 8192.0, OP.is_equal, OP.mult, "IO G15", "CE")
+    ts(T.CS[:], T.IO[:, 0:144], G15, 131072.0, OP.is_equal, OP.mult, "IO G15", "CS")
+    ms(T.RSZ[:, 0::16], 0.0, "RSZ")
+    ts(T.DGC[:], IH, DC, LO, OP.mult, OP.mult, "PH0 DC LO", "DGC")
+    su(0)
+    ms(T.RST[:, 0::16], 1.0e9, "RST RSTa RSTb")
+    act(T.MM[:, 0:128], IDN, AF.Identity, "PW0 H0", "MM0", scale=H0)
+    act(T.MM[:, 128:256], ROT, AF.Identity, "PW0 PW1 H0", "MM1", scale=H0)
+    act(T.MM[:, 256:384], UNR, AF.Identity, "PW0 PW1 H1", "MM2", scale=H1)
+    act(T.MM[:, 384:512], IDN, AF.Identity, "PW0 H1", "MM3", scale=H1)
+    zmm(0)
+    zmm2(0)
+    for r in range(4):
+        act(T.TA[:, r::4], T.IO[:, r::4], AF.Identity, "IO EQN EQB", "TA%d" % r, bias=T.EQB[:, r:r + 1], scale=T.EQN[:, r:r + 1])
+    alt(0, 12)
+    act(T.TA2[:], T.TA[:], AF.Identity, names("TA", 4), "TA2", scale=-1.0)
+    for r in range(4):
+        act(T.TB[:, r::4], T.IO[:, r::4], AF.Identity, "IO EQN EQB", "TB%d" % r, bias=T.EQB[:, 4 + r:5 + r], scale=T.EQN[:, 4 + r:5 + r])
+    for r in range(8):
+        act(T.TC[:, r:NN:8], T.IO[:, r::8], AF.Identity, "IO EQN EQB", "TC%d" % r, bias=T.EQB[:, 8 + r:9 + r], scale=T.EQN[:, 8 + r:9 + r])
+    v8(0)
+    llo(0)
+    lowest(0)
+    for par in range(2):
+        ts(T.UB[:, 24 * par:24 * par + 24], T.UBI[:], K16, 8.0 * par, OP.add, OP.add, "UBI K16", "UB%d" % par)
+    for r in range(8):
+        ts(T.TJ[:, r::16], T.JV[:], T.EQ[:, 8 + r:9 + r], 1048576.0, OP.mult, OP.add, "JV EQ", "TJ%d" % r)
+    weave(lambda: mchain(0), lambda: zchain(0), lambda: lists(0))
+    same(0)
+    hg(0)
+    ml(0)
+    advance(0)
+
+    for t in range(RO):
+        products(t)
+        if t == 5:
+            break
+        match_rest(t + 1)
+        zmm2(t + 1)
+        post(t)
+        if t == 0:
+            spares2(12, 72)
+            alt(12, 72)
+        lowest(t + 1)
+        n = t + 1
+        if n < 5:
+            weave(lambda: mchain(n), lambda: lists(n))
+            hg(n)
+            v8(n)
+            llo(n)
+            weave(lambda: zchain(n), lambda: [ml(n), outp(t)])
+            h8(n)
+            advance(n)
+        else:
+            n5 = 5 * LN
+            llo(n)
+            weave(lambda: mchain(n), lambda: partners(0))
+            weave(lambda: zchain(n), lambda: [ml(n), outp(t)])
+            dma("y", "do0", [(T.yo[0:112, 0:n5], T.OB[16:128, 0:n5]), (T.yo[112:128, 0:n5], T.OB[0:16, 0:n5])], names("OB", 5), "")
+            own(t)
+            best(n)
+            ts(T.QI[:, 336:348], T.BI[:], 511, None, OP.bitwise_and, None, "BI", "QI7")
+            qu(7, 12)
+            partners(1)
+            dma("y", "dyp", [(T.yp[:], T.YP[0::16, :])], "YP0 YP1", "")
+        guest(t)
+    act(T.OB[:, 5 * LN:6 * LN], T.pO[:, 0:LN], AF.Copy, "pO", "OB5")
+    dma("s", "do1", [(T.yo[:, 5 * LN:6 * LN], T.OB[:, 5 * LN:6 * LN])], "OB5", "")
+
+    count = emit(g, T, ops)
+    for s in sorted(count):
+        g.wait_ge(T.sem[s], count[s])
+    g.wait_ge(T.sem.lsent, sent[0])

@@ -1,9 +1,10 @@
+import numpy as np
 from concourse.bass import DstId, RemoteDMATransfer
 from concourse.mybir import dt, AluOpType, AxisListType, ActivationFunctionType
 
 NN, LN, RO, W = 384, 192, 6, 3072
 F32, F16, BF, I32, U16 = "float32", "float16", "bfloat16", "int32", "uint16"
-SCAN_LAST = (4, 5)
+SCAN_LAST = (0, 1, 2, 3, 4, 5)
 
 
 def _sb(n, d, p=128):
@@ -17,48 +18,54 @@ SCRATCH = {
     "UBI": _sb(24, F32), "UB": _sb(48, F32), "JV": _sb(8, F32), "EQ": _sb(16, F32), "EQN": _sb(16, F32), "EQB": _sb(16, F32),
     "PW": _sb(256, F32), "PH": _sb(256, F16), "MM": _sb(512, F32), "BLK": _sb(128, F16), "BLK8": _sb(128, BF),
     "SEL": _sb(2048, F16), "RW": _sb(640, F16), "CE": _sb(144, BF), "CS": _sb(144, BF), "WU": _sb(128, BF), "DGC": _sb(128, BF),
-    "ONES": _sb(LN, BF), "C192": _sb(LN, BF), "B8": _sb(144, F16), "TA": _sb(NN, F32), "TA2": _sb(NN, F32), "TB": _sb(NN, F32),
-    "TC": _sb(896, F32), "TJ": _sb(128, F32), "RST": _sb(W, BF), "RSZ": _sb(LN, F32), "RS8": _sb(768, BF), "XU": _sb(W, BF), "UN": _sb(NN, BF),
+    "ONES": _sb(LN, BF), "C192": _sb(LN, BF), "B8": _sb(144, F16), "TA": _sb(NN, F32), "TB": _sb(NN, F32),
+    "TC": _sb(896, F32), "TJ": _sb(128, F32), "RST": _sb(1536, BF), "RSZ": _sb(LN, F32), "RS8": _sb(768, BF), "XU": _sb(W, BF), "UN": _sb(NN, BF),
     "KV": _sb(LN, BF), "KU": _sb(LN, BF), "NV": _sb(LN, F16), "SU": _sb(LN, F16), "EA": _sb(LN, F32), "EU": _sb(LN, BF), "EM": _sb(LN, BF),
-    "A": _sb(W, F32), "RR": _sb(W, F32), "SG": _sb(1536, BF), "E": _sb(1536, BF), "KP": _sb(96, U16), "ML": _sb(288, U16),
+    "AL": _sb(1536, BF), "RL": _sb(1536, BF), "DG": _sb(768, BF), "EB": _sb(LN, F32),
+    "GA": _sb(LN, BF), "GT": _sb(LN, BF), "GU": _sb(LN, BF), "GJ": _sb(LN, BF),
+    "A": _sb(1536, F32), "RR": _sb(1536, F32), "SG": _sb(1536, BF), "E": _sb(1536, BF), "KP": _sb(96, U16), "ML": _sb(288, U16),
     "MI": _sb(LN, I32), "MJ": _sb(LN, I32), "M16": _sb(LN, F16), "ZT": _sb(LN, F32), "ZR": _sb(LN, F32), "BI": _sb(12, I32),
     "QI": _sb(8 * 48, I32), "QU": _sb(8 * 36, U16), "VF": _sb(24, F32), "VS": _sb(5 * 12, F32), "GV": _sb(5 * 12, F32),
-    "LI": _sb(36, I32), "LJ": _sb(24, I32), "LU": _sb(5 * 36, U16), "T1": _sb(LN, F32), "T2": _sb(LN, F32), "T3": _sb(LN, F32),
-    "N1": _sb(LN, F32), "N2": _sb(LN, F32), "V8": _sb(LN, F32), "HG": _sb(LN, F32), "H8": _sb(LN, F32), "H8R": _sb(LN, F32),
+    "LI": _sb(36, I32), "LJ": _sb(24, I32), "LU": _sb(5 * 36, U16), "T3": _sb(LN, F32),
+    "N2": _sb(LN, F32), "V8": _sb(LN, BF), "HG": _sb(LN, F32), "H8": _sb(LN, F32), "H8R": _sb(LN, F32),
     "LLO": _sb(1536, F32), "LHI": _sb(1536, F32), "P": _sb(W, F32), "PS": _sb(768, F32), "TS": _sb(5 * LN, F32), "TL": _sb(5 * LN, F32),
     "SL": _sb(LN, F32), "OB": _sb(RO * LN, F32), "YT": _sb(LN, F32), "YP": _sb(NN, F32),
     "pD0": ("psum", [128, 512], F32), "pD1": ("psum", [128, 512], F32), "pD2": ("psum", [128, 512], F32), "pZ": ("psum", [128, 512], F32),
     "pR": ("psum", [128, 512], F32), "pO": ("psum", [128, 512], F32), "pM": ("psum", [128, 512], F32), "pN": ("psum", [128, 512], F32),
 }
 DSEMS = ["dka", "dpv", "dsp", "dx", "ds0", "dn0", "dn1", "do0", "do1", "dyp"]
-SEMAPHORES = ["ev", "es", "et", "eg", "lsent"] + DSEMS + ["av%d" % t for t in range(5)] + ["at%d" % t for t in range(5)]
+SEMAPHORES = ["ev", "es", "et", "eg", "lsent"] + DSEMS + ["a%s%d" % (k, t) for k in "vab" for t in range(5)]
 
 OP = AluOpType
 AF = ActivationFunctionType
 
 
-def route(T, topo, r, t):
+def route(T, topo, r, t, kind):
     src, dst = T.cores[r], T.cores[(r + 1 + t % 7) % len(T.cores)]
     if topo.may_write(src, dst):
         return None, dst
     c = [k for k in topo.cores_of(src) if k != src and T.rank_of(k) is None and topo.may_write(k, dst)]
     c.sort(key=lambda k: topo.die(k) != topo.die(src))
-    return c[0], dst
+    return c[1 if kind == "b" or (kind == "v" and t % 2) else 0], dst
 
 
 def messages():
-    return [("v", 0), ("v", 1), ("v", 2), ("t", 0), ("v", 3), ("t", 1), ("v", 4), ("t", 2), ("t", 3), ("t", 4)]
+    m = [("v", 0), ("v", 1), ("a", 0), ("b", 0), ("v", 2), ("v", 3), ("a", 1), ("b", 1), ("v", 4)]
+    return m + [(k, t) for t in (2, 3, 4) for k in "ab"]
 
 
 def land(T, kind, t):
-    return T.GV[:, 12 * t:12 * t + 12] if kind == "v" else T.TL[:, LN * t:LN * t + LN]
+    if kind == "v":
+        return T.GV[:, 12 * t:12 * t + 12]
+    a = LN * t + (96 if kind == "b" else 0)
+    return T.TL[:, a:a + 96]
 
 
 def relay_program(g, core, T, topo):
     total = 0
     for r in range(len(T.cores)):
         for kind, t in messages():
-            via, dst = route(T, topo, r, t)
+            via, dst = route(T, topo, r, t, kind)
             if via != core:
                 continue
             sem = T.sem["a%s%d" % (kind, t)]
@@ -70,18 +77,17 @@ def relay_program(g, core, T, topo):
         g.wait_ge(T.sem.lsent, total)
 
 
-def emit(g, T, ops):
-    queue = {"v": g.vector, "s": g.scalar, "t": g.tensor, "g": g, "y": g.sync}
-    lastw, readers, deps, need = {}, {}, [], set()
+def hazards(ops, order_only):
+    lastw, readers, out = {}, {}, []
     for i, o in enumerate(ops):
         d = set()
-        for x in o["r"]:
+        for x in o["r"] + (o.get("after", []) if order_only else []):
             if x in lastw:
                 d.add(lastw[x])
-            if x[0] == "p":
+            if x[0] == "p" and not order_only:
                 d.update(k for k in readers.get(x, []) if ops[k]["e"] != o["e"])
         for x in o["w"]:
-            if x in lastw and not (x[0] == "p" and o["e"] == "t" and ops[lastw[x]]["e"] == "t"):
+            if x in lastw and (order_only or not (x[0] == "p" and o["e"] == "t" and ops[lastw[x]]["e"] == "t")):
                 d.add(lastw[x])
             d.update(readers.get(x, []))
         d.discard(i)
@@ -90,20 +96,144 @@ def emit(g, T, ops):
         for x in o["w"]:
             lastw[x] = i
             readers[x] = []
+        out.append(d)
+    return out
+
+
+GATHER = 1.3
+COST = {"v": {"P": 50 + 768 * GATHER, "E": 50 + 1536 * GATHER, "RL": 670, "RR": 1300, "PS": 670, "S": 655, "ML": 270, "NV": 50 + LN * GATHER,
+              "EM": 50 + LN * GATHER, "YT": 50 + LN * GATHER, "NR": 350, "PV": 350, "KA": 350, "NM": 350, "SP": 830, "KP": 110, "pR": 190,
+              "MI": 190, "MJ": 190, "M": 190, "ZT": 190, "ZR": 190, "OB": 110, "SU": 190, "T": 190, "N": 190, "H": 190, "YP": 190,
+              "RSZ": 140, "CE": 150, "CS": 150, "B": 150, "PH": 140, "PW": 140, "BLK": 140, "TA": 110, "": 85},
+        "s": {"LH": 80 + 768 * GATHER, "KV": 80 + LN * GATHER, "V": 80 + LN * GATHER, "GA": 80 + LN * GATHER, "GT": 80 + LN * GATHER,
+              "GU": 80 + LN * GATHER, "GJ": 80 + LN * GATHER, "HG": 80 + LN * GATHER, "IO": 380, "pD": 380, "MM": 170, "TA": 140, "TB": 140,
+              "TC": 140, "VS": 115, "ALT": 115, "SG": 700, "TS": 140, "": 220},
+        "g": {"IO": 770, "GB": 340, "RST": 2700, "RS": 1400, "XU": 490, "TJ": 340, "TC": 340, "": 150}}
+HOP, DMA, TRAVEL = 160, 2300, 8500
+CASES = ((1.0, 200, 0.8), (1.0, 100, 1.05), (0.7, 150, 0.9), (1.3, 150, 1.0))
+SEED, ROUNDS, NOISE, SHARE, EASE, KEPT = 7, 700, 3000.0, 0.05, 200, []
+
+
+def schedule(ops):
+    n = len(ops)
+    deps = [dict.fromkeys(d, HOP) for d in hazards(ops, True)]
+    cost, loose, sends, prev = [], [], {}, None
+    for i, o in enumerate(ops):
+        key = (o["w"][0] if o["w"] else "").rstrip("0123456789_abc")
+        key = key.split("0")[0].split("1")[0].split("8")[0].split("2")[0]
+        c = o.get("c") or (100 if o.get("dma") else COST[o["e"]].get(key, COST[o["e"]][""]))
+        cost.append(c)
+        loose.append(o["e"] + key in "vP vE vS vNV vEM vYT sLH sKV sV sGA sGT sGU sGJ sHG".split())
+        for k in deps[i]:
+            if ops[k].get("dma"):
+                deps[i][k] = DMA * (2.5 if ops[k]["dma"] == "ds0" else 1)
+            elif ops[k]["e"] == "t" and o["e"] == "t":
+                deps[i][k] = 0
+        if "msg" in o:
+            sends[o["msg"]] = i
+            if prev is not None:
+                deps[i][prev] = 0
+            prev = i
+        for s, _ in o.get("wait", []):
+            deps[i][sends[s]] = TRAVEL * (1.4 if s[1] == "v" else 1)
+    users = [[] for _ in ops]
+    for i in range(n):
+        for k, lat in deps[i].items():
+            users[k].append((i, lat))
+    way = [0] * n
+    for i in reversed(range(n)):
+        way[i] = cost[i] + max([lat + way[u] for u, lat in users[i]] + [DMA if ops[i].get("dma") else 0])
+    if not KEPT:
+        eng = [o["e"] for o in ops]
+        tail = [DMA if o.get("dma") else 0 for o in ops]
+        back = [list(d.items()) for d in deps]
+
+        def there_and_back(key):
+            st, end = place(eng, back, users, cost, key, tail)
+            rs, _ = place(eng, users, back, cost, [-(a + c + z) for a, c, z in zip(st, cost, tail)], [0] * n)
+            s2, e2 = place(eng, back, users, cost, [-(a + c) for a, c in zip(rs, cost)], tail)
+            return min(((s, replay(s)) for s in (st, s2)), key=lambda x: x[1])
+
+        def replay(st):
+            order, total = sorted(range(n), key=lambda i: (st[i], i)), 0.0
+            for fg, hop, way_ in CASES:
+                free, fin = dict.fromkeys("vstgy", 0.0), [0.0] * n
+                for i in order:
+                    t = free[eng[i]]
+                    for k, lat in back[i]:
+                        x = fin[k] + (hop if lat == HOP else lat * way_ if lat >= TRAVEL else lat)
+                        if x > t:
+                            t = x
+                    fin[i] = free[eng[i]] = t + cost[i] * (fg if loose[i] else 1)
+                total += max(a + z for a, z in zip(fin, tail))
+            return total / len(CASES)
+
+        best = cur = min((there_and_back(k) for k in ([-w for w in way], list(range(n)))), key=lambda x: x[1])
+        rng = np.random.default_rng(SEED)
+        for _ in range(ROUNDS):
+            c = there_and_back([a + float(x) for a, x in zip(cur[0], NOISE * rng.random() * (rng.random(n) - 0.5) * (rng.random(n) < SHARE))])
+            if c[1] <= cur[1] + EASE:
+                cur = c
+            if c[1] < best[1]:
+                best = c
+        KEPT.append((best[1], sorted(range(n), key=lambda i: (best[0][i], i))))
+    return [ops[i] for i in KEPT[0][1]]
+
+
+def place(eng, deps, users, cost, key, tail):
+    n = len(eng)
+    left = [len(d) for d in deps]
+    ready, st = [0.0] * n, [0.0] * n
+    begins, ends = {e: [] for e in "vstgy"}, {e: [] for e in "vstgy"}
+    pool = [i for i in range(n) if not left[i]]
+    end = 0
+    while pool:
+        i = min(pool, key=lambda k: key[k])
+        pool.remove(i)
+        s, f, c, t = begins[eng[i]], ends[eng[i]], cost[i], ready[i]
+        p = len(f)
+        while p and f[p - 1] > t:
+            p -= 1
+        while p < len(s) and s[p] < t + c:
+            t = max(t, f[p])
+            p += 1
+        s.insert(p, t)
+        f.insert(p, t + c)
+        st[i] = t
+        end = max(end, t + c + tail[i])
+        for u, lat in users[i]:
+            ready[u] = max(ready[u], t + c + lat)
+            left[u] -= 1
+            if not left[u]:
+                pool.append(u)
+    return st, end
+
+
+def emit(g, T, ops):
+    queue = {"v": g.vector, "s": g.scalar, "t": g.tensor, "g": g, "y": g.sync}
+    ops = schedule(ops)
+    deps, need = [], set()
+    for d in hazards(ops, False):
         last = {}
         for k in d:
             key = ops[k].get("dma") or ops[k]["e"]
             last[key] = max(last.get(key, -1), k)
         deps.append(sorted(last.values()))
         need.update(last.values())
-    count, mark, seen = {}, {}, {}
+    count, mark, clock = {}, {}, {}
+    seen = {e: {} for e in queue}
     for i, o in enumerate(ops):
         e = o["e"]
-        waits = [mark[k] for k in deps[i]] + o.get("wait", [])
-        for s, n in waits:
-            if seen.get((e, s), 0) < n:
+        for k in reversed(deps[i]):
+            s, n = mark[k]
+            if seen[e].get(s, 0) < n:
                 queue[e].wait_ge(T.sem[s], n)
-                seen[(e, s)] = n
+                seen[e][s] = n
+                for s2, n2 in clock[k].items():
+                    seen[e][s2] = max(seen[e].get(s2, 0), n2)
+        for s, n in o.get("wait", []):
+            queue[e].wait_ge(T.sem[s], n)
+        clock[i] = dict(seen[e])
         res = o["f"](queue[e])
         if o.get("dma"):
             for ins in res:
@@ -151,12 +281,14 @@ def rank_program(g, core, T, topo):
     def act(out, a, f, r, w, bias=0.0, scale=1.0):
         add("s", lambda q: q.activation(out, a, f, bias=bias, scale=scale), r, w)
 
-    def mm(out, terms, r, w, start=True, stop=True):
+    def mm(out, terms, r, w, start=True, stop=True, n=None):
         def f(q):
             for i, (l, x) in enumerate(terms):
                 ins = q.matmul(out, l, x, start and i == 0, stop and i == len(terms) - 1)
             return ins
-        add("t", f, r, w)
+        wide = r.startswith("PW") or r.startswith("MM")
+        n = n or (96 if r.startswith("RW") else 64 if r.startswith("B8") or r.startswith("MM") or "VF" in r else LN)
+        add("t", f, r, w, c=len(terms) * n * 0.42 * (4 if wide else 1))
 
     def iota(out, pat, base, cm, w, flt=True):
         if flt:
@@ -171,15 +303,16 @@ def rank_program(g, core, T, topo):
         add(e, lambda q: [q.dma_start(a, b) for a, b in pairs], r, w, dma=sem)
 
     def send(kind, t, src, r):
-        via, dst = route(T, topo, rank, t)
+        via, dst = route(T, topo, rank, t, kind)
         to = dst if via is None else via
         rid, pid = topo.addr(to, core)
         sent[0] += len(topo.engines(core, to))
-        add("g", lambda q: q.remote_dma(land(T, kind, t), src, T.sem["a%s%d" % (kind, t)], T.sem.lsent, pid, rid, topo.mask(core, to)), r, "")
+        add("g", lambda q: q.remote_dma(land(T, kind, t), src, T.sem["a%s%d" % (kind, t)], T.sem.lsent, pid, rid, topo.mask(core, to)), r, "",
+            msg="a%s%d" % (kind, t), c=700)
 
     def arrival(kind, t):
         s = (rank - 1 - t % 7) % nr
-        via, dst = route(T, topo, s, t)
+        via, dst = route(T, topo, s, t, kind)
         return [("a%s%d" % (kind, t), len(topo.engines(T.cores[s] if via is None else via, core)))]
 
     def names(p, n, a=0):
@@ -205,7 +338,7 @@ def rank_program(g, core, T, topo):
 
     col = lambda i: T.C2[:, i:i + 1]
     PC, KC, GC, HC = T.CF[:, 0:1], T.CF[:, 1:2], T.CF[:, 2:3], T.CF[:, 3:4]
-    LO, HI, H0, H1, CC, B8C, G15, DC, K16 = [col(i) for i in range(9)]
+    LO, HI, H0, H1, CC, B8C, G15, DC, K16, R0, R1, R2 = [col(i) for i in range(12)]
     IDN, ROT, UNR = T.PW[:, 0:128], T.PW[:, 112:240], T.PW[:, 16:144]
     IH = T.PH[:, 0:128]
     rw = lambda i: T.RW[:, 128 * i:128 * i + 128]
@@ -236,14 +369,19 @@ def rank_program(g, core, T, topo):
     def dmm(j):
         b = "pD%d" % ((j // 2) % 3)
         sel = T.SEL[:, 128 * j:128 * j + 128]
-        mm(T[b][:, LN * (j % 2):LN * (j % 2) + LN], [(sel, T.KV[:]), (IH, T.KU[:]), (sel, T.NV[:])], "SEL%d PH0 KV KU NV" % j, b)
+        terms = [(sel, T.KV[:]), (IH, T.KU[:])] + ([(sel, T.NV[:])] if j >= 8 else [])
+        mm(T[b][:, LN * (j % 2):LN * (j % 2) + LN], terms, "SEL%d PH0 KV KU" % j + (" NV" if j >= 8 else ""), b)
 
     def dabs(j):
         b = "pD%d" % ((j // 2) % 3)
-        act(T.A[:, j::16], T[b][:, LN * (j % 2):LN * (j % 2) + LN], AF.Abs, b, "A%d" % j, bias=1536.0 + 4096.0 * j, scale=2048.0)
+        src = T[b][:, LN * (j % 2):LN * (j % 2) + LN]
+        if j < 8:
+            act(T.AL[:, j::8], src, AF.Abs, b, "A%d" % j, bias=float(j), scale=2048.0)
+        else:
+            act(T.A[:, j - 8::8], src, AF.Abs, b, "A%d" % j, bias=1536.0 + 4096.0 * (j - 7), scale=2048.0)
 
-    def match_first():
-        for j in range(16):
+    def match(a, b):
+        for j in range(a, b):
             dmm(j)
             if j % 2 and j < 10:
                 dabs(j - 1)
@@ -252,8 +390,8 @@ def rank_program(g, core, T, topo):
     def match_rest(t):
         for j in range(10, 16):
             dabs(j)
-        for j in range(8):
-            act(T.SG[:, LN * j:LN * j + LN], T.A[:, j::16], AF.Sign, "A%d" % j, "SG%d" % j, bias=-65535.0)
+        for h in range(2):
+            act(T.SG[:, 768 * h:768 * h + 768], T.AL[:, 768 * h:768 * h + 768], AF.Sign, names("A", 8), "SG%d" % h, bias=-65535.0)
 
     def kp(t):
         ts(T.KP[:], T.pR[:, 0:96], 1.0 / 128, 192.0, OP.mult, OP.add, "pR", "KP")
@@ -263,18 +401,26 @@ def rank_program(g, core, T, topo):
         tt(T.E[:], T.X[:, 0:NN].indirect(T.KP[:]), T.XU[:, 1536 * par:1536 * par + 1536], OP.is_equal, "X KP " + names("XU%d_" % par, 8), "E")
 
     def same(t):
-        tt(T.EM[:], T.TA2[:, 0:NN].indirect(vl(t)), T.KA[:, t % 2::2], OP.is_equal, "TA2 KA QU%d" % t, "EM")
-        mm(T.pM[:, 0:LN], [(T.BLK8[:], T.EM[:])], "BLK8 EM", "pM")
+        act(T.GA[:], T.TA[:, 0:NN].indirect(vl(t)), AF.Identity, names("TA", 4) + " QU%d" % t, "GA")
+        mm(T.pM[:, 0:LN], [(T.DG[:, 640:768], T.GA[:]), (T.DG[:, 384:512], T.KU[:])], "DG5 DG3 GA KU", "pM")
+        act(T.EB[:], T.pM[:, 0:LN], AF.Abs, "pM", "EB")
+        act(T.EM[:], T.EB[:], AF.Sign, "EB", "EM", bias=-64.0)
+        mm(T.pM[:, 0:LN], [(T.BLK8[:], T.EM[:]), (T.DG[:, 512:640], T.ONES[:])], "BLK8 EM DG4 ONES", "pM")
 
     def h8(t):
         tt(T.H8[:], T.HG[:], T.pM[:, 0:LN], OP.mult, "HG pM", "H8")
 
     def lowest(t):
-        scan(T.RR[:], T.RST[:], T.A[:], OP.add, OP.min, "RST " + names("A", 16), "RR")
+        scan(T.RL[:], T.RST[:], T.AL[:], OP.add, OP.min, "RST " + names("A", 8), "RL")
+        mm(T.pR[:, 128:320], [(IH, T.RL[:, 7::8]), (IH, T.V8[:]), (T.DG[:, 0:128], T.ONES[:])], "PH0 RL V8 DG0 ONES", "pR")
+        mm(T.pR[:, 320:416], [(rw(2), T.SU[:, 0::2]), (rw(3), T.SU[:, 1::2])], "RW2 RW3 SU", "pR")
+
+    def lowest2(t):
+        tt(T.pR[:, 128:320], T.pR[:, 128:320], T.NM[:, t % 2::2], OP.min, "pR NM", "pR")
+        scan(T.RR[:], T.RST[:], T.A[:], OP.add, OP.min, "RST " + names("A", 16, 8), "RR")
 
     def mchain(t):
-        tt(T.MI[:], T.RR[:, 15::16], T.NM[:, t % 2::2], OP.min, "RR NM", "MI")
-        mm(T.pR[:, 320:416], [(rw(2), T.SU[:, 0::2]), (rw(3), T.SU[:, 1::2])], "RW2 RW3 SU", "pR")
+        tt(T.MI[:], T.pR[:, 128:320], T.RR[:, 7::8], OP.min, "RR pR", "MI")
         ts(T.MJ[:], T.MI[:], 4095, None, OP.bitwise_and, None, "MI", "MJ")
         ts(T.M16[:], T.MJ[:], -1536.0, None, OP.add, None, "MJ", "M16")
         mm(T.pR[:, 128:224], [(rw(0), T.M16[:, 0::2]), (rw(1), T.M16[:, 1::2])], "RW0 RW1 M16", "pR")
@@ -289,7 +435,7 @@ def rank_program(g, core, T, topo):
         mm(T.pZ[:, 0:LN], terms, "CE E RW4 KV C192 WU EU DGC ONES", "pZ", stop=False)
 
     def zmm2(t):
-        mm(T.pZ[:, 0:LN], [(T.CS[:, 15 - j:143 - j], T.SG[:, LN * j:LN * j + LN]) for j in range(8)], "CS " + names("SG", 8), "pZ", start=False)
+        mm(T.pZ[:, 0:LN], [(T.CS[:, 15 - j:143 - j], T.SG[:, j::8]) for j in range(8)], "CS " + names("SG", 2), "pZ", start=False)
 
     def zchain(t):
         add("v", lambda q: q.transpose(T.ZT[:], T.pZ[:, 0:LN]), "pZ", "ZT")
@@ -331,59 +477,74 @@ def rank_program(g, core, T, topo):
         cp(T.LU[:, 36 * t:36 * t + 36], T.LI[:], "LIa LIc", "LU%d" % t)
 
     def v8(t):
-        act(T.V8[:], T.IO8[:, 0:NN].indirect(vl(t)), AF.Identity, "IO8 QU%d" % t, "V8")
+        act(T.V8[:], T.IO[:, 0:NN].indirect(vl(t)), AF.Identity, "IO QU%d" % t, "V8", bias=-1536.0, scale=8.0)
+
+    def gab(t):
+        act(T.GT[:], T.TB[:, 0:NN].indirect(T.LU[:, 36 * t + 24:36 * t + 36]), AF.Identity, names("TB", 4) + " LU%d" % t, "GT")
 
     def advance(t):
         par, s = t % 2, t + 2
-        tt(T.T1[:], T.TA[:, 0:NN].indirect(vl(t)), T.KA[:, par::2], OP.min, names("TA", 4) + " KA QU%d" % t, "T1")
-        best(t)
         ku(t + 1)
-        tt(T.T2[:], T.TB[:, 0:NN].indirect(T.LU[:, 36 * t + 24:36 * t + 36]), T.T1[:], OP.min, names("TB", 4) + " T1 LU%d" % t, "T2")
-        i4(t)
         su(t + 1)
+        best(t)
+        if t > 0:
+            h8(t)
+            h8r(t)
+        i4(t)
         qu(s)
+        act(T.GU[:], T.TC[:, 0:896].indirect(T.QU[:, 36 * s + 12:36 * s + 24]), AF.Identity, names("TC", 10) + " QU%d" % s, "GU")
+        mm(T.pZ[:, 272:464], [(IH, T.GA[:]), (IH, T.GT[:]), (T.DG[:, 128:256], T.ONES[:]), (IH, T.GU[:])], "PH0 GA GT GU DG1 ONES", "pZ")
+        act(T.GJ[:], T.TJ[:, 0:128].indirect(T.QU[:, 36 * s + 24:36 * s + 36]), AF.Identity, names("TJ", 8) + " QU%d" % s, "GJ")
+        mm(T.pO[:, 256:448], [(T.DG[:, 384:512], T.V8[:]), (T.DG[:, 256:384], T.ONES[:]), (IH, T.GJ[:])], "PH0 GJ V8 DG2 DG3 ONES", "pO")
         if s < 5:
             vf(s)
-        tt(T.T3[:], T.TC[:, 0:896].indirect(T.QU[:, 36 * s + 12:36 * s + 24]), T.T2[:], OP.min, names("TC", 9) + " T2 QU%d" % s, "T3")
-        act(T.KA[:, par::2], T.T3[:], AF.Abs, "T3", "KA")
-        tt(T.N1[:], T.TJ[:, 0:128].indirect(T.QU[:, 36 * s + 24:36 * s + 36]), T.V8[:], OP.subtract, names("TJ", 8) + " V8 QU%d" % s, "N1")
-        kv(t + 1)
-        tt(T.N2[:], T.N1[:], T.NM[:, par::2], OP.min, "N1 NM", "N2")
-        act(T.NM[:, par::2], T.N2[:], AF.Abs, "N2", "NM")
-        eu(t + 1)
-        if t == 0:
-            h8(0)
-        if t + 1 < 5:
-            same(t + 1)
-        kp(t + 1)
-        nv(t + 1)
-        if s < 5:
-            vsend(s)
-        eu2(t + 1)
-        match_first()
         if t > 0:
             own(t - 1)
         else:
             spares(12, 72)
-            ms(T.RS8[:, 0::8], 0.0, "RS8")
+        tt(T.T3[:], T.pZ[:, 272:464], T.KA[:, par::2], OP.min, "pZ KA", "T3")
+        tt(T.N2[:], T.pO[:, 256:448], T.NM[:, par::2], OP.min, "pO NM", "N2")
+        act(T.KA[:, par::2], T.T3[:], AF.Abs, "T3", "KA")
+        kv(t + 1)
+        act(T.NM[:, par::2], T.N2[:], AF.Abs, "N2", "NM")
+        if t + 1 < 5:
+            same(t + 1)
+        eu(t + 1)
+        match(0, 6)
+        kp(t + 1)
+        nv(t + 1)
+        eu2(t + 1)
+        match(6, 8)
+        v8(t + 1)
+        match(8, 16)
+        if s < 5:
+            vsend(s)
         counts(t + 1)
         zmm(t + 1)
+        lowest(t + 1)
 
     def spares(a, b):
         cp(T.SP16[0:8, 16 * a:16 * b], T.SPI[0:8, 16 * a:16 * b], "SPI", "SP16")
 
     def spares2(a, b):
-        mm(T.pM[:, 400 + a:400 + b], [(T.B8[0:8, 15 - p:143 - p], T.SP16[0:8, 16 * a + p:16 * b:16]) for p in range(16)], "B8 SP16", "pM")
+        mm(T.pR[:, 424 + a:424 + b], [(T.B8[0:8, 15 - p:143 - p], T.SP16[0:8, 16 * a + p:16 * b:16]) for p in range(16)], "B8 SP16", "pR")
 
     def alt(a, b):
-        act(T.ALT[:, a:b], T.pM[:, 400 + a:400 + b], AF.Identity, "pM", "ALT", bias=2096640.0)
+        act(T.ALT[:, a:b], T.pR[:, 424 + a:424 + b], AF.Identity, "pR", "ALT", bias=2096640.0)
 
     def llo(t):
         for k in range(8):
             act(T.LLO[:, k::8], T.S[:, 8 * (t % 2) + k::16], AF.Sigmoid, "S", "LL%d" % k)
+            if t == 0:
+                ops[-1].update(dict(c=1520, w=["LL0", "SIG"]) if k == 0 else dict(after=["SIG"]))
 
     def hg(t):
         act(T.HG[:], Sw.indirect(T.LU[:, 36 * t:36 * t + 12]), AF.Identity, "S LU%d" % t, "HG")
+
+    bank = ("pO", "pM")
+
+    def half(h):
+        return T.pM[:, 384:480] if h else T.pO[:, 0:96]
 
     def products(t):
         turn = ROT if t < 5 else IDN
@@ -402,32 +563,39 @@ def rank_program(g, core, T, topo):
                 else:
                     terms = [(turn, T.P[:, a + k:a + 768:8]) for k in range(8)]
                 if u == 0 and t < 5:
-                    terms = [(ROT, T.H8[:, 96 * h:96 * h + 96])] + terms
-                    r += " H8"
-                mm(T.pO[:, 96 * h:96 * h + 96], terms, "PW0 PW1 " + r, "pO", start=(u == 0), stop=(u == 1))
+                    mm(half(h), [(ROT, T.H8[:, 96 * h:96 * h + 96])], "PW0 PW1 H8", bank[h], stop=False, n=96)
+                mm(half(h), terms, "PW0 PW1 " + r, bank[h], start=(u == 0 and t == 5), stop=(u == 1), n=96)
+            if t < 5:
+                ap = T.TS[:, LN * t + 96 * h:LN * t + 96 * h + 96]
+                act(ap, half(h), AF.Sigmoid, bank[h], "TS%d%s" % (t, "ab"[h]), scale=0.25)
+                send("ab"[h], t, ap, "TS%d%s" % (t, "ab"[h]))
+            else:
+                act(T.OB[:, 5 * LN + 96 * h:5 * LN + 96 * h + 96], half(h), AF.Copy, bank[h], "TS5" + "ab"[h])
+
+    def h8r(t):
+        mm(T.pM[:, LN:2 * LN], [(ROT, T.H8[:])], "PW0 PW1 H8", "pM")
+        act(T.H8R[:], T.pM[:, LN:2 * LN], AF.Copy, "pM", "H8R")
 
     def post(t):
-        ap = T.TS[:, LN * t:LN * t + LN]
-        act(ap, T.pO[:, 0:LN], AF.Sigmoid, "pO", "TS%d" % t, scale=0.25)
-        send("t", t, ap, "TS%d" % t)
-        mm(T.pM[:, LN:2 * LN], [(ROT, T.H8[:])], "PW0 PW1 H8", "pM")
-        mm(T.pN[:, 0:LN], [(UNR, ap)], "PW0 PW1 TS%d" % t, "pN")
-        act(T.H8R[:], T.pM[:, LN:2 * LN], AF.Copy, "pM", "H8R")
+        mm(T.pN[:, 0:LN], [(UNR, T.TS[:, LN * t:LN * t + LN])], "PW0 PW1 TS%da TS%db" % (t, t), "pN")
         act(T.SL[:], T.pN[:, 0:LN], AF.Copy, "pN", "SL")
 
     def own(t):
         ts(Sw.indirect(T.LU[:, 36 * t:36 * t + 12]), T.SL[:], 2.0, -1.0, OP.mult, OP.add, "SL LU%d" % t, "S")
 
     def outp(t):
-        tt(T.OB[:, LN * t:LN * t + LN], T.pO[:, 0:LN], T.H8R[:], OP.subtract, "pO H8R", "OB%d" % t)
+        for h in range(2):
+            a = LN * t + 96 * h
+            tt(T.OB[:, a:a + 96], half(h), T.H8R[:, 96 * h:96 * h + 96], OP.subtract, bank[h] + " H8R", "OB%d%s" % (t, "ab"[h]))
 
     def guest(t):
-        ts(Sw.indirect(T.LU[:, 36 * t + 12:36 * t + 24]), T.TL[:, LN * t:LN * t + LN], 2.0, -1.0, OP.mult, OP.add, "LU%d" % t, "S",
-           wait=arrival("t", t))
+        for h in range(2):
+            ts(Sw.indirect(T.LU[:, 36 * t + 12 + 6 * h:36 * t + 18 + 6 * h]), land(T, "ab"[h], t), 2.0, -1.0, OP.mult, OP.add, "LU%d" % t, "S",
+               wait=arrival("ab"[h], t), c=350)
 
     def partners(par):
         cp(T.YT[:], T.IO[:, 0:NN].indirect(vl(6 + par)), "IO QU%d" % (6 + par), "YT")
-        cp(T.YP[:, par::2], T.YT[:], "YT", "YP%d" % par)
+        act(T.YP[:, par::2], T.YT[:], AF.Copy, "YT", "YP%d" % par)
 
     ms(T.NR[:], 0, "NR0 NR1")
     dma("y", "dpv", [(T.PVI[0:8, :], T.pv[:])], "", "PVI")
@@ -441,8 +609,8 @@ def rank_program(g, core, T, topo):
     iota(T.GB[:], [[16, 8], [0, 16]], 0, 0, "GB")
     dma("g", "ds0", [(T.S[:], T.s0[:])], "", "S")
     iota(T.UBI[:], [[4, 2], [256, 12]], 0, 0, "UBI")
-    iota(T.JV[:], [[1, 8]], -(7 + 65536 + 1048576), 0, "JV")
-    iota(T.RST[:, 0:1536], [[0, 1536]], 0, 0, "RSTa")
+    iota(T.JV[:], [[1, 8]], -(7 + 1048576), 0, "JV")
+    iota(T.RST[:], [[0, 1536]], 0, 0, "RST")
     ts(T.CI[:, 1:2], T.CI[:, 0:1], 15, None, OP.bitwise_and, None, "CI0", "CI1")
     ts(T.CI[:, 2:3], T.CI[:, 0:1], 112, None, OP.bitwise_and, None, "CI0", "CI2")
     ts(T.CI[:, 3:4], T.CI[:, 0:1], 16, None, OP.bitwise_and, None, "CI0", "CI3")
@@ -488,14 +656,13 @@ def rank_program(g, core, T, topo):
     eu(0)
     mm(T.pM[:, 480:504], [(ROT, T.VF[:])], "PW0 PW1 VF", "pM")
     eu2(0)
-    match_first()
+    match(0, 16)
     kp(0)
     cp(T.VS[:, 0:24], T.pM[:, 480:504], "pM", "VS0 VS1")
     send("v", 0, T.VS[:, 0:12], "VS0")
     send("v", 1, T.VS[:, 12:24], "VS1")
-    iota(T.RST[:, 1536:W], [[0, 1536]], 0, 0, "RSTb")
     iota(T.TJ[:], [[0, 128]], 1048576, 0, names("TJ", 8))
-    iota(T.TC[:, NN:896], [[0, 512]], 4096, 0, "TC8")
+    iota(T.TC[:, NN:512], [[0, 128]], 0, 0, "TC8")
     for k in range(8):
         gcopy(T.XU[:, 1536 + k:W:8], T.X[:, 1::2], LN, "X", "XU1_%d" % k)
     iota(T.RS8[:], [[0, 768]], 1, 0, "RS8")
@@ -508,7 +675,14 @@ def rank_program(g, core, T, topo):
     ts(H0, HC, 0.0, None, OP.is_equal, None, "CF", "H0")
     ts(H1, HC, 16.0, None, OP.is_equal, None, "CF", "H1")
     ts(T.EQN[:], T.EQ[:], -1.0, None, OP.mult, None, "EQ", "EQN")
-    ts(T.EQB[:], T.EQ[:], -4097.0, 4096.0, OP.mult, OP.add, "EQ", "EQB")
+    ts(R0, KC, 4.0, 2048.0, OP.is_lt, OP.mult, "CF", "R0")
+    ts(R2, HI, 2048.0, None, OP.mult, None, "HI", "R2")
+    ts(R1, LO, 2048.0, R0, OP.mult, OP.subtract, "LO R0", "R1")
+    ts(T.EQB[:, 0:4], T.EQ[:, 0:4], -1856.0, R0, OP.mult, OP.add, "EQ R0", "EQBa")
+    ts(T.EQB[:, 8:16], T.EQ[:, 8:16], -1856.0, R2, OP.mult, OP.add, "EQ R2", "EQBc")
+    ts(T.EQB[:, 4:8], T.EQ[:, 4:8], -1856.0, R1, OP.mult, OP.add, "EQ R1", "EQBb")
+    for i, c in enumerate((1536.0, -193.0, -67072.0, -1.0, 16.0, 128.0)):
+        ts(T.DG[:, 128 * i:128 * i + 128], IH, c, None, OP.mult, None, "PH0", "DG%d" % i)
     ts(G15, GC, 15.0, None, OP.add, None, "CF", "G15")
     ts(DC, KC, -1024.0, 7168.0 - 262144.0, OP.mult, OP.add, "CF", "DC")
     ts(K16, KC, 16.0, None, OP.mult, None, "CF", "K16")
@@ -516,67 +690,73 @@ def rank_program(g, core, T, topo):
     ts(rw(3), IH, HI, None, OP.mult, None, "PH0 HI", "RW3")
     ts(rw(4), IH, LO, 1.0 / 128, OP.mult, OP.mult, "PH0 LO", "RW4")
     ts(T.WU[:], IH, LO, 262144.0, OP.mult, OP.mult, "PH0 LO", "WU")
-    ts(T.BLK8[:], T.BLK[:], 8.0, None, OP.mult, None, "BLK", "BLK8")
+    ts(T.BLK8[:], T.BLK[:], R0, -1.0 / 512, OP.mult, OP.mult, "BLK R0", "BLK8")
     ms(T.RSZ[:], 1.0, "RSZ")
     ts(T.CE[:], T.IO[:, 0:144], G15, 8192.0, OP.is_equal, OP.mult, "IO G15", "CE")
     ts(T.CS[:], T.IO[:, 0:144], G15, 131072.0, OP.is_equal, OP.mult, "IO G15", "CS")
     ms(T.RSZ[:, 0::16], 0.0, "RSZ")
     ts(T.DGC[:], IH, DC, LO, OP.mult, OP.mult, "PH0 DC LO", "DGC")
     su(0)
-    ms(T.RST[:, 0::16], 1.0e9, "RST RSTa RSTb")
+    ms(T.RST[:, 0::8], 1.0e9, "RST")
+    v8(0)
     act(T.MM[:, 0:128], IDN, AF.Identity, "PW0 H0", "MM0", scale=H0)
     act(T.MM[:, 128:256], ROT, AF.Identity, "PW0 PW1 H0", "MM1", scale=H0)
     act(T.MM[:, 256:384], UNR, AF.Identity, "PW0 PW1 H1", "MM2", scale=H1)
     act(T.MM[:, 384:512], IDN, AF.Identity, "PW0 H1", "MM3", scale=H1)
     zmm(0)
-    zmm2(0)
-    for r in range(4):
-        act(T.TA[:, r::4], T.IO[:, r::4], AF.Identity, "IO EQN EQB", "TA%d" % r, bias=T.EQB[:, r:r + 1], scale=T.EQN[:, r:r + 1])
-    alt(0, 12)
-    act(T.TA2[:], T.TA[:], AF.Identity, names("TA", 4), "TA2", scale=-1.0)
-    for r in range(4):
-        act(T.TB[:, r::4], T.IO[:, r::4], AF.Identity, "IO EQN EQB", "TB%d" % r, bias=T.EQB[:, 4 + r:5 + r], scale=T.EQN[:, 4 + r:5 + r])
-    for r in range(8):
-        act(T.TC[:, r:NN:8], T.IO[:, r::8], AF.Identity, "IO EQN EQB", "TC%d" % r, bias=T.EQB[:, 8 + r:9 + r], scale=T.EQN[:, 8 + r:9 + r])
-    v8(0)
-    llo(0)
     lowest(0)
+    zmm2(0)
+    alt(0, 12)
+    for r in range(4):
+        act(T.TA[:, r::4], T.IO[:, r::4], AF.Identity, "IO EQN EQBa", "TA%d" % r, bias=T.EQB[:, r:r + 1], scale=T.EQN[:, r:r + 1])
+    for r in range(4):
+        act(T.TB[:, r::4], T.IO[:, r::4], AF.Identity, "IO EQN EQBb", "TB%d" % r, bias=T.EQB[:, 4 + r:5 + r], scale=T.EQN[:, 4 + r:5 + r])
+    for r in range(8):
+        act(T.TC[:, r:NN:8], T.IO[:, r::8], AF.Identity, "IO EQN EQBc", "TC%d" % r, bias=T.EQB[:, 8 + r:9 + r], scale=T.EQN[:, 8 + r:9 + r])
+    act(T.TC[:, 512:896], T.IO[:], AF.Identity, "IO R2", "TC9", bias=R2, scale=0.0)
     for par in range(2):
         ts(T.UB[:, 24 * par:24 * par + 24], T.UBI[:], K16, 8.0 * par, OP.add, OP.add, "UBI K16", "UB%d" % par)
+    lowest2(0)
     for r in range(8):
         ts(T.TJ[:, r::16], T.JV[:], T.EQ[:, 8 + r:9 + r], 1048576.0, OP.mult, OP.add, "JV EQ", "TJ%d" % r)
-    weave(lambda: mchain(0), lambda: zchain(0), lambda: lists(0))
     same(0)
+    weave(lambda: mchain(0), lambda: zchain(0), lambda: lists(0))
     hg(0)
+    gab(0)
     ml(0)
-    advance(0)
+    h8(0)
+    h8r(0)
+    llo(0)
+    ms(T.RS8[:, 0::8], 0.0, "RS8")
 
     for t in range(RO):
         products(t)
         if t == 5:
             break
+        if t == 0:
+            advance(0)
         match_rest(t + 1)
         zmm2(t + 1)
         post(t)
         if t == 0:
             spares2(12, 72)
             alt(12, 72)
-        lowest(t + 1)
+        lowest2(t + 1)
         n = t + 1
         if n < 5:
             weave(lambda: mchain(n), lambda: lists(n))
             hg(n)
-            v8(n)
+            gab(n)
             llo(n)
             weave(lambda: zchain(n), lambda: [ml(n), outp(t)])
-            h8(n)
             advance(n)
         else:
             n5 = 5 * LN
             llo(n)
             weave(lambda: mchain(n), lambda: partners(0))
             weave(lambda: zchain(n), lambda: [ml(n), outp(t)])
-            dma("y", "do0", [(T.yo[0:112, 0:n5], T.OB[16:128, 0:n5]), (T.yo[112:128, 0:n5], T.OB[0:16, 0:n5])], names("OB", 5), "")
+            dma("y", "do0", [(T.yo[0:112, 0:n5], T.OB[16:128, 0:n5]), (T.yo[112:128, 0:n5], T.OB[0:16, 0:n5])],
+                " ".join("OB%d%s" % (i, x) for i in range(5) for x in "ab"), "")
             own(t)
             best(n)
             ts(T.QI[:, 336:348], T.BI[:], 511, None, OP.bitwise_and, None, "BI", "QI7")
@@ -584,8 +764,7 @@ def rank_program(g, core, T, topo):
             partners(1)
             dma("y", "dyp", [(T.yp[:], T.YP[0::16, :])], "YP0 YP1", "")
         guest(t)
-    act(T.OB[:, 5 * LN:6 * LN], T.pO[:, 0:LN], AF.Copy, "pO", "OB5")
-    dma("s", "do1", [(T.yo[:, 5 * LN:6 * LN], T.OB[:, 5 * LN:6 * LN])], "OB5", "")
+    dma("s", "do1", [(T.yo[:, 5 * LN:6 * LN], T.OB[:, 5 * LN:6 * LN])], "TS5a TS5b", "")
 
     count = emit(g, T, ops)
     for s in sorted(count):

@@ -4,7 +4,12 @@ from concourse.mybir import dt, AluOpType, AxisListType, ActivationFunctionType
 
 NN, LN, RO, W = 384, 192, 6, 3072
 F32, F16, BF, I32, U16 = "float32", "float16", "bfloat16", "int32", "uint16"
-SCAN_LAST = (0, 1, 2, 3, 4, 5)
+PARTS = ((0, 64, "a"), (64, 128, "a"), (128, 192, "b"))
+SPAN = {"a": (0, 128), "b": (128, 192)}
+SCAN_FROM = (2, 2, 2, 2, 2, 1)
+BIG = 262144.0
+MESSAGES = [(k, t) for k in "vab" for t in range(RO - 1)]
+DIRECT = "b"
 
 
 def _sb(n, d, p=128):
@@ -12,59 +17,61 @@ def _sb(n, d, p=128):
 
 
 SCRATCH = {
-    "KI": _sb(NN, I32), "KA": _sb(NN, F32), "NM": _sb(NN, F32), "NR": _sb(NN, I32), "X": _sb(NN, BF), "S": _sb(W, F32),
-    "PVI": _sb(NN, I32), "SPI": _sb(1152, I32), "PV16": _sb(NN, F16), "SP16": _sb(1152, F16), "ALT": _sb(72, F32),
-    "CI": _sb(4, I32), "CF": _sb(4, F32), "C2": _sb(16, F32), "IO": _sb(NN, F32), "IO8": _sb(NN, F32), "GB": _sb(128, F32),
-    "UBI": _sb(24, F32), "UB": _sb(48, F32), "JV": _sb(8, F32), "EQ": _sb(16, F32), "EQN": _sb(16, F32), "EQB": _sb(16, F32),
-    "PW": _sb(256, F32), "PH": _sb(256, F16), "MM": _sb(512, F32), "BLK": _sb(128, F16), "BLK8": _sb(128, BF),
-    "SEL": _sb(2048, F16), "RW": _sb(640, F16), "CE": _sb(144, BF), "CS": _sb(144, BF), "WU": _sb(128, BF), "DGC": _sb(128, BF),
-    "ONES": _sb(LN, BF), "C192": _sb(LN, BF), "B8": _sb(144, F16), "TA": _sb(NN, F32), "TB": _sb(NN, F32),
-    "TC": _sb(896, F32), "TJ": _sb(128, F32), "RST": _sb(1536, BF), "RSZ": _sb(LN, F32), "RS8": _sb(768, BF), "XU": _sb(W, BF), "UN": _sb(NN, BF),
-    "KV": _sb(LN, BF), "KU": _sb(LN, BF), "NV": _sb(LN, F16), "SU": _sb(LN, F16), "EA": _sb(LN, F32), "EU": _sb(LN, BF), "EM": _sb(LN, BF),
-    "AL": _sb(1536, BF), "RL": _sb(1536, BF), "DG": _sb(768, BF), "EB": _sb(LN, F32),
-    "GA": _sb(LN, BF), "GT": _sb(LN, BF), "GU": _sb(LN, BF), "GJ": _sb(LN, BF),
-    "A": _sb(1536, F32), "RR": _sb(1536, F32), "SG": _sb(1536, BF), "E": _sb(1536, BF), "KP": _sb(96, U16), "ML": _sb(288, U16),
+    "KI": _sb(NN, I32), "KN": _sb(2 * NN, F32), "NR": _sb(NN, I32), "X": _sb(NN, BF), "S": _sb(W, F32),
+    "PVI": _sb(NN, I32), "PV16": _sb(NN, F16), "SP16": _sb(NN, F16),
+    "CI": _sb(5, I32), "CF": _sb(5, F32), "C2": _sb(24, F32), "IO": _sb(392, F32), "GB": _sb(256, F32),
+    "UBI": _sb(12, F32), "UB": _sb(72, F32), "EQ": _sb(16, F32), "EQN": _sb(16, F32), "EQB": _sb(24, F32),
+    "PW": _sb(256, F32), "PH": _sb(256, BF), "MM": _sb(512, BF), "BLK": _sb(128, BF), "BR": _sb(128, BF), "RF": _sb(256, F32),
+    "SEL": _sb(2176, BF), "RW": _sb(512, BF), "CE": _sb(144, BF), "CS": _sb(144, BF), "DG": _sb(1152, BF),
+    "ONES": _sb(LN, BF), "B8": _sb(144, F16), "TB": _sb(392, F32), "TC": _sb(400, F32),
+    "RST": _sb(1536, BF), "RSZ": _sb(LN, BF), "RS8": _sb(512, BF), "XU": _sb(W, BF), "UN": _sb(NN, BF),
+    "KL": _sb(NN, F32), "KV": _sb(2 * LN, BF), "KH": _sb(LN, BF), "KU": _sb(2 * LN, BF), "NV": _sb(LN, F16), "AL": _sb(1920, BF),
+    "RL": _sb(2 * 1536, BF), "T2": _sb(LN, F32), "GT": _sb(2 * LN, BF), "GW": _sb(NN, BF),
+    "A": _sb(1536, F32), "RR": _sb(1536, F32), "SG": _sb(2 * 1920, BF), "E": _sb(1536, BF), "KP": _sb(96, U16), "ML": _sb(RO * 288, U16),
     "MI": _sb(LN, I32), "MJ": _sb(LN, I32), "M16": _sb(LN, F16), "ZT": _sb(LN, F32), "ZR": _sb(LN, F32), "BI": _sb(12, I32),
-    "QI": _sb(8 * 48, I32), "QU": _sb(8 * 36, U16), "VF": _sb(24, F32), "VS": _sb(5 * 12, F32), "GV": _sb(5 * 12, F32),
-    "LI": _sb(36, I32), "LJ": _sb(24, I32), "LU": _sb(5 * 36, U16), "T3": _sb(LN, F32),
-    "N2": _sb(LN, F32), "V8": _sb(LN, BF), "HG": _sb(LN, F32), "H8": _sb(LN, F32), "H8R": _sb(LN, F32),
-    "LLO": _sb(1536, F32), "LHI": _sb(1536, F32), "P": _sb(W, F32), "PS": _sb(768, F32), "TS": _sb(5 * LN, F32), "TL": _sb(5 * LN, F32),
-    "SL": _sb(LN, F32), "OB": _sb(RO * LN, F32), "YT": _sb(LN, F32), "YP": _sb(NN, F32),
-    "pD0": ("psum", [128, 512], F32), "pD1": ("psum", [128, 512], F32), "pD2": ("psum", [128, 512], F32), "pZ": ("psum", [128, 512], F32),
-    "pR": ("psum", [128, 512], F32), "pO": ("psum", [128, 512], F32), "pM": ("psum", [128, 512], F32), "pN": ("psum", [128, 512], F32),
+    "QI": _sb(36, I32), "QH": _sb(36, F16), "QA": _sb(48, I32),
+    "QF": _sb(8 * 36, F32), "QU": _sb(8 * 36, U16), "VS": _sb(5 * 24, F32), "GV": _sb(5 * 24, F32),
+    "LG": _sb(5 * 24, U16), "T3": _sb(NN, F32), "HG": _sb(LN, F32), "H8": _sb(2 * LN, F32),
+    "LLO": _sb(2 * 1536, F32), "LHI": _sb(1536, F32), "P": _sb(W, F32), "PS": _sb(1536, F32), "TS": _sb(5 * LN, F32), "TL": _sb(5 * LN, F32),
+    "SL": _sb(LN, F32), "OB": _sb(RO * LN, F32), "YP": _sb(NN, F32),
+    "pD0": ("psum", [128, 512], F32), "pD1": ("psum", [128, 512], F32), "pU": ("psum", [128, 512], F32), "pZ": ("psum", [128, 512], F32),
+    "pR": ("psum", [128, 512], F32), "pa": ("psum", [128, 512], F32), "pb": ("psum", [128, 512], F32), "pN": ("psum", [128, 512], F32),
 }
-DSEMS = ["dka", "dpv", "dsp", "dx", "ds0", "dn0", "dn1", "do0", "do1", "dyp"]
-SEMAPHORES = ["ev", "es", "et", "eg", "lsent"] + DSEMS + ["a%s%d" % (k, t) for k in "vab" for t in range(5)]
+DSEMS = ["dka", "dpv", "dsp", "dx", "ds0", "dn0", "dn1", "do0", "doa", "dob", "dyp"] + ["dt%d" % t for t in range(RO - 1)]
+SEMAPHORES = ["ev", "es", "et", "eg", "lsent"] + DSEMS + ["a%s%d" % m for m in MESSAGES]
 
 OP = AluOpType
 AF = ActivationFunctionType
 
 
+def line(kind, t):
+    return 2 if kind == "v" and t > 1 else 0 if kind in "vb" else 1
+
+
 def route(T, topo, r, t, kind):
     src, dst = T.cores[r], T.cores[(r + 1 + t % 7) % len(T.cores)]
-    if topo.may_write(src, dst):
+    if kind in DIRECT and topo.may_write(src, dst):
         return None, dst
-    c = [k for k in topo.cores_of(src) if k != src and T.rank_of(k) is None and topo.may_write(k, dst)]
+    c = [k for k in topo.cores_of(src) if T.rank_of(k) is None and all(topo.may_write(k, x) for x in T.cores)]
     c.sort(key=lambda k: topo.die(k) != topo.die(src))
-    return c[1 if kind == "b" or (kind == "v" and t % 2) else 0], dst
+    return c[line(kind, t)], dst
 
 
-def messages():
-    m = [("v", 0), ("v", 1), ("a", 0), ("b", 0), ("v", 2), ("v", 3), ("a", 1), ("b", 1), ("v", 4)]
-    return m + [(k, t) for t in (2, 3, 4) for k in "ab"]
+def spot(kind, t):
+    if kind in "ab":
+        return LN * t + SPAN[kind][0], LN * t + SPAN[kind][1]
+    return 24 * t, 24 * t + 24
 
 
 def land(T, kind, t):
-    if kind == "v":
-        return T.GV[:, 12 * t:12 * t + 12]
-    a = LN * t + (96 if kind == "b" else 0)
-    return T.TL[:, a:a + 96]
+    a, b = spot(kind, t)
+    return T.TL[:, a:b] if kind in "ab" else T.GV[:, a:b]
 
 
 def relay_program(g, core, T, topo):
     total = 0
     for r in range(len(T.cores)):
-        for kind, t in messages():
+        for kind, t in MESSAGES:
             via, dst = route(T, topo, r, t, kind)
             if via != core:
                 continue
@@ -84,8 +91,8 @@ def hazards(ops, order_only):
         for x in o["r"] + (o.get("after", []) if order_only else []):
             if x in lastw:
                 d.add(lastw[x])
-            if x[0] == "p" and not order_only:
-                d.update(k for k in readers.get(x, []) if ops[k]["e"] != o["e"])
+            if x[0] == "p":
+                d.update(k for k in readers.get(x, []) if order_only or ops[k]["e"] != o["e"])
         for x in o["w"]:
             if x in lastw and (order_only or not (x[0] == "p" and o["e"] == "t" and ops[lastw[x]]["e"] == "t")):
                 d.add(lastw[x])
@@ -100,113 +107,176 @@ def hazards(ops, order_only):
     return out
 
 
-GATHER = 1.3
-COST = {"v": {"P": 50 + 768 * GATHER, "E": 50 + 1536 * GATHER, "RL": 670, "RR": 1300, "PS": 670, "S": 655, "ML": 270, "NV": 50 + LN * GATHER,
-              "EM": 50 + LN * GATHER, "YT": 50 + LN * GATHER, "NR": 350, "PV": 350, "KA": 350, "NM": 350, "SP": 830, "KP": 110, "pR": 190,
-              "MI": 190, "MJ": 190, "M": 190, "ZT": 190, "ZR": 190, "OB": 110, "SU": 190, "T": 190, "N": 190, "H": 190, "YP": 190,
-              "RSZ": 140, "CE": 150, "CS": 150, "B": 150, "PH": 140, "PW": 140, "BLK": 140, "TA": 110, "": 85},
-        "s": {"LH": 80 + 768 * GATHER, "KV": 80 + LN * GATHER, "V": 80 + LN * GATHER, "GA": 80 + LN * GATHER, "GT": 80 + LN * GATHER,
-              "GU": 80 + LN * GATHER, "GJ": 80 + LN * GATHER, "HG": 80 + LN * GATHER, "IO": 380, "pD": 380, "MM": 170, "TA": 140, "TB": 140,
-              "TC": 140, "VS": 115, "ALT": 115, "SG": 700, "TS": 140, "": 220},
-        "g": {"IO": 770, "GB": 340, "RST": 2700, "RS": 1400, "XU": 490, "TJ": 340, "TC": 340, "": 150}}
-HOP, DMA, TRAVEL = 160, 2300, 8500
-CASES = ((1.0, 200, 0.8), (1.0, 100, 1.05), (0.7, 150, 0.9), (1.3, 150, 1.0))
-SEED, ROUNDS, NOISE, SHARE, EASE, KEPT = 7, 700, 3000.0, 0.05, 200, []
+CASES = ((1.56, 3.8, 1.0, 150, 6500, 600, 1), (1.8, 4.5, 1.3, 250, 10000, 800, 1), (1.56, 3.8, 1.0, 150, 6500, 600, 2))
+WEIGHTS, HOPE = (0.45, 0.15, 0.15), 200
+CYCLE, FIXED, DMA, OPEN, ROUND = 0.83, {"v": 50, "s": 65, "t": 0, "g": 150, "y": 0}, 2300, 2400, 13.5
+SEED, ROUNDS, REACH, PATIENCE, SWAP, KEPT = 11, 170000, 0.3, 0.8, 0.15, []
+WINDOWS = ((0, 0.5, 0.3, 120), (0.3, 0.7, 0.1, 80), (0.5, 0.85, 0.1, 80), (0.65, 1, 0.1, 80), (0, 0.55, 0.2, 50), (0.35, 1, 0.2, 40))
 
 
 def schedule(ops):
+    if KEPT:
+        _, order, eng = KEPT[0]
+        return [dict(ops[i], e=eng[i], f=ops[i]["ways"][eng[i]][0]) if "ways" in ops[i] else ops[i] for i in order]
     n = len(ops)
-    deps = [dict.fromkeys(d, HOP) for d in hazards(ops, True)]
-    cost, loose, sends, prev = [], [], {}, None
+    eng = [o["e"] for o in ops]
+    lane = ["vstgy".index(e) for e in eng]
+    kinds = [dict.fromkeys(d, "hop") for d in hazards(ops, True)]
+    sends, prev = {}, {}
     for i, o in enumerate(ops):
-        key = (o["w"][0] if o["w"] else "").rstrip("0123456789_abc")
-        key = key.split("0")[0].split("1")[0].split("8")[0].split("2")[0]
-        c = o.get("c") or (100 if o.get("dma") else COST[o["e"]].get(key, COST[o["e"]][""]))
-        cost.append(c)
-        loose.append(o["e"] + key in "vP vE vS vNV vEM vYT sLH sKV sV sGA sGT sGU sGJ sHG".split())
-        for k in deps[i]:
+        for k in kinds[i]:
             if ops[k].get("dma"):
-                deps[i][k] = DMA * (2.5 if ops[k]["dma"] == "ds0" else 1)
-            elif ops[k]["e"] == "t" and o["e"] == "t":
-                deps[i][k] = 0
+                kinds[i][k] = DMA * {"ds0": 2.5, "dsp": 1.6, "dn0": 1.3, "dn1": 1.3}.get(ops[k]["dma"], 1)
+            elif eng[k] == "t" and eng[i] == "t":
+                kinds[i][k] = 0
         if "msg" in o:
             sends[o["msg"]] = i
-            if prev is not None:
-                deps[i][prev] = 0
-            prev = i
+            if o["line"] in prev:
+                kinds[i][prev[o["line"]]] = 0
+            o["opens"] = o["line"] not in prev
+            prev[o["line"]] = i
+        if "behind" in o:
+            kinds[i][[k for k, x in enumerate(ops) if x["w"] == ["PS"]][o["behind"]]] = 0
         for s, _ in o.get("wait", []):
-            deps[i][sends[s]] = TRAVEL * (1.4 if s[1] == "v" else 1)
-    users = [[] for _ in ops]
-    for i in range(n):
-        for k, lat in deps[i].items():
-            users[k].append((i, lat))
-    way = [0] * n
+            kinds[i][sends[s]] = "open" if ops[sends[s]]["opens"] else "way"
+
+    def price(i, e, case):
+        o = ops[i]
+        k = o["ways"][e][1] if "ways" in o else o["k"]
+        if "c" in o:
+            return o["c"] + (case[5] if "msg" in o else 0)
+        return case[2] * (FIXED[e] + CYCLE * o["n"] * {"g": case[0], "s": case[1]}.get(k, k)) * (case[6] if e == "t" else 1)
+
+    def shift(i, e):
+        eng[i], lane[i] = e, "vstgy".index(e)
+        for co, case in zip(costs, CASES):
+            co[i] = price(i, e, case)
+
+    costs = [[price(i, eng[i], case) for i in range(n)] for case in CASES]
+    backs = [[[(k, {"hop": case[3], "way": case[4], "open": case[4] + OPEN}.get(x, x)) for k, x in d.items()] for d in kinds] for case in CASES]
+    ahead = [[[] for _ in ops] for _ in CASES]
+    for us, ba in zip(ahead, backs):
+        for i in range(n):
+            for k, lat in ba[i]:
+                us[k].append((i, lat))
+    tail = [DMA if o.get("dma") else 0 for o in ops]
+    key = [0.0] * n
     for i in reversed(range(n)):
-        way[i] = cost[i] + max([lat + way[u] for u, lat in users[i]] + [DMA if ops[i].get("dma") else 0])
-    if not KEPT:
-        eng = [o["e"] for o in ops]
-        tail = [DMA if o.get("dma") else 0 for o in ops]
-        back = [list(d.items()) for d in deps]
+        key[i] = ops[i]["at"] if ops[i]["at"] is not None else min(key[u] for u, _ in ahead[0][i]) - costs[0][i] / 1000 - 0.15
+    cur = dispatch(lane, ahead[0], [len(d) for d in kinds], costs[0], key)
 
-        def there_and_back(key):
-            st, end = place(eng, back, users, cost, key, tail)
-            rs, _ = place(eng, users, back, cost, [-(a + c + z) for a, c, z in zip(st, cost, tail)], [0] * n)
-            s2, e2 = place(eng, back, users, cost, [-(a + c) for a, c in zip(rs, cost)], tail)
-            return min(((s, replay(s)) for s in (st, s2)), key=lambda x: x[1])
+    def onward(order, z):
+        out = []
+        for co, us in zip(costs, ahead):
+            free, way = [0.0] * 5, {}
+            for i in reversed(order[z:]):
+                way[i] = free[lane[i]] = co[i] + max([free[lane[i]], tail[i]] + [lat + way[k] for k, lat in us[i]])
+            rest = [(i, max([tail[i]] + [lat + way[k] for k, lat in us[i] if k in way])) for i in order[:z]]
+            out.append(([x for x in rest if x[1]], free))
+        return out
 
-        def replay(st):
-            order, total = sorted(range(n), key=lambda i: (st[i], i)), 0.0
-            for fg, hop, way_ in CASES:
-                free, fin = dict.fromkeys("vstgy", 0.0), [0.0] * n
-                for i in order:
-                    t = free[eng[i]]
-                    for k, lat in back[i]:
-                        x = fin[k] + (hop if lat == HOP else lat * way_ if lat >= TRAVEL else lat)
-                        if x > t:
-                            t = x
-                    fin[i] = free[eng[i]] = t + cost[i] * (fg if loose[i] else 1)
-                total += max(a + z for a, z in zip(fin, tail))
-            return total / len(CASES)
+    def replay(order, a, z, on, old=None, bar=1e18):
+        total, held, part, before = 0.0, [], order[a:z], {lane[i]: i for i in order[max(0, a - 100):a]}
+        for c, w in enumerate(WEIGHTS):
+            co, ba = costs[c], backs[c]
+            fin, by = ([0.0] * n, [-1] * n) if old is None else (old[c][1][:], old[c][2][:])
+            last = [before.get(e, -1) for e in range(5)]
+            free = [fin[i] if i >= 0 else 0.0 for i in last]
+            for i in part:
+                e = lane[i]
+                t, b = free[e], last[e]
+                for k, lat in ba[i]:
+                    x = fin[k] + lat
+                    if x > t:
+                        t, b = x, k
+                fin[i] = free[e] = t + co[i]
+                by[i], last[e] = b, i
+            end, i = max([(fin[i] + x, i) for i, x in on[c][0]] + [(free[e] + x, last[e]) for e, x in enumerate(on[c][1]) if last[e] >= 0])
+            total += w * end
+            held.append((i, fin, by, end))
+            if old and total + sum(x * (y[3] - HOPE) for x, y in zip(WEIGHTS[c + 1:], old[c + 1:])) > bar:
+                return 1e18, None
+        return total, held
 
-        best = cur = min((there_and_back(k) for k in ([-w for w in way], list(range(n)))), key=lambda x: x[1])
-        rng = np.random.default_rng(SEED)
-        for _ in range(ROUNDS):
-            c = there_and_back([a + float(x) for a, x in zip(cur[0], NOISE * rng.random() * (rng.random(n) - 0.5) * (rng.random(n) < SHARE))])
-            if c[1] <= cur[1] + EASE:
-                cur = c
-            if c[1] < best[1]:
-                best = c
-        KEPT.append((best[1], sorted(range(n), key=lambda i: (best[0][i], i))))
-    return [ops[i] for i in KEPT[0][1]]
+    def moved(part, up):
+        if up:
+            need = {part[-1]}
+            for k in reversed(part):
+                if k in need:
+                    need.update(kinds[k])
+        else:
+            need = {part[0]}
+            for k in part:
+                if not need.isdisjoint(kinds[k]):
+                    need.add(k)
+        if part[0] in need and part[-1] in need:
+            return None
+        return [k for k in part if (k in need) == up] + [k for k in part if (k in need) != up]
+
+    rng = np.random.default_rng(SEED)
+    for y, z, share, ease in WINDOWS:
+        y, z, rounds = int(y * n), int(z * n), int(share * ROUNDS)
+        on, inside = onward(cur, z), set(cur[y:z])
+        val, held = replay(cur, 0, z, on)
+        best = (val, cur, eng[:])
+        for it, (r0, r1, r2, r3, r4) in enumerate(rng.random((rounds, 5)).tolist()):
+            i, _, by, _ = held[int(r0 * len(CASES))]
+            pairs = []
+            while i in inside:
+                j = by[i]
+                if j in inside and j not in kinds[i]:
+                    pairs.append((i, j))
+                i = j
+            if not pairs:
+                continue
+            i, j = pairs[int(r1 * len(pairs))]
+            a, b, was, new = cur.index(j), cur.index(i), eng[j], cur
+            if r2 > 1 - SWAP and "ways" in ops[j]:
+                others = [e for e in ops[j]["ways"] if e != was]
+                shift(j, others[int(r3 * len(others))])
+            else:
+                far, step = int(np.log(r2 + 1e-12) / np.log(1 - REACH)), -1 if r3 < 0.5 else 1
+                p = a if step < 0 else b
+                while far and y <= p + step < z:
+                    p += step
+                    if lane[cur[p]] == lane[i]:
+                        far -= 1
+                        a, b = min(a, p), max(b, p)
+                part = moved(cur[a:b + 1], step < 0)
+                if part is None:
+                    continue
+                new = cur[:a] + part + cur[b + 1:]
+            bar = val - ease * (1 - it / rounds) * float(np.log(r4 + 1e-12))
+            v, h = replay(new, a, z, on, held, bar)
+            if v <= bar:
+                cur, val, held = new, v, h
+                if v < best[0]:
+                    best = (v, new, eng[:])
+            elif eng[j] != was:
+                shift(j, was)
+        cur = best[1]
+        for i, e in enumerate(best[2]):
+            shift(i, e)
+    KEPT.append(best)
+    return schedule(ops)
 
 
-def place(eng, deps, users, cost, key, tail):
-    n = len(eng)
-    left = [len(d) for d in deps]
-    ready, st = [0.0] * n, [0.0] * n
-    begins, ends = {e: [] for e in "vstgy"}, {e: [] for e in "vstgy"}
-    pool = [i for i in range(n) if not left[i]]
-    end = 0
-    while pool:
-        i = min(pool, key=lambda k: key[k])
-        pool.remove(i)
-        s, f, c, t = begins[eng[i]], ends[eng[i]], cost[i], ready[i]
-        p = len(f)
-        while p and f[p - 1] > t:
-            p -= 1
-        while p < len(s) and s[p] < t + c:
-            t = max(t, f[p])
-            p += 1
-        s.insert(p, t)
-        f.insert(p, t + c)
-        st[i] = t
-        end = max(end, t + c + tail[i])
+def dispatch(lane, users, left, cost, key):
+    ready, free, begun = [0.0] * len(lane), [0.0] * 5, []
+    pool = [[i for i in range(len(lane)) if lane[i] == e and not left[i]] for e in range(5)]
+    for _ in lane:
+        soon, e = min((max(ready[i], free[e]) + cost[i], e) for e in range(5) for i in pool[e])
+        first = min(max(ready[i], free[e]) for i in pool[e])
+        i = min((i for i in pool[e] if max(ready[i], free[e]) <= first + PATIENCE * (soon - first)), key=lambda k: key[k])
+        pool[e].remove(i)
+        begun.append((max(ready[i], free[e]), len(begun), i))
+        free[e] = begun[-1][0] + cost[i]
         for u, lat in users[i]:
-            ready[u] = max(ready[u], t + c + lat)
+            ready[u] = max(ready[u], free[e] + lat)
             left[u] -= 1
             if not left[u]:
-                pool.append(u)
-    return st, end
+                pool[lane[u]].append(u)
+    return [i for _, _, i in sorted(begun)]
 
 
 def emit(g, T, ops):
@@ -256,59 +326,77 @@ def rank_program(g, core, T, topo):
     nr = len(T.cores)
     ops = []
     sent = [0]
+    base = [0.0]
 
-    def add(e, f, r, w, **k):
-        ops.append(dict(e=e, f=f, r=r.split(), w=w.split(), **k))
+    def add(e, f, r, w, n=12, k=1, at=None, **more):
+        ops.append(dict(e=e, f=f, r=r.split(), w=w.split(), n=n, k=k, at=None if at is None else at + base[0], **more))
 
-    def ts(out, in0, s1, s2, o0, o1, r, w, **k):
+    def during(round_):
+        base[0] = ROUND * round_
+
+    def ts(out, in0, s1, s2, o0, o1, r, w, n=12, k=1, **more):
         if o1 is None:
-            add("v", lambda q: q.tensor_scalar(out, in0, s1, None, o0), r, w, **k)
+            add("v", lambda q: q.tensor_scalar(out, in0, s1, None, o0), r, w, n, k, **more)
         else:
-            add("v", lambda q: q.tensor_scalar(out, in0, s1, s2, o0, o1), r, w, **k)
+            add("v", lambda q: q.tensor_scalar(out, in0, s1, s2, o0, o1), r, w, n, k, **more)
 
-    def tt(out, a, b, o, r, w):
-        add("v", lambda q: q.tensor_tensor(out, a, b, o), r, w)
+    def tt(out, a, b, o, r, w, n=LN, k=1, at=None):
+        add("v", lambda q: q.tensor_tensor(out, a, b, o), r, w, n, k, at)
 
-    def cp(out, a, r, w, **k):
-        add("v", lambda q: q.tensor_copy(out, a), r, w, **k)
+    def cp(out, a, r, w, n=12, at=None):
+        add("v", lambda q: q.tensor_copy(out, a), r, w, n, 1, at)
 
-    def ms(out, c, w):
-        add("v", lambda q: q.memset(out, c), "", w)
+    def ms(out, c, w, n, k=1):
+        add("v", lambda q: q.memset(out, c), "", w, n, k)
 
-    def scan(out, d0, d1, o0, o1, r, w):
-        add("v", lambda q: q.tensor_tensor_scan(out, d0, d1, 0.0, o0, o1), r, w)
+    def scan(out, d0, d1, o0, o1, r, w, n, k, at):
+        add("v", lambda q: q.tensor_tensor_scan(out, d0, d1, 0.0, o0, o1), r, w, n, k, at)
 
-    def act(out, a, f, r, w, bias=0.0, scale=1.0):
-        add("s", lambda q: q.activation(out, a, f, bias=bias, scale=scale), r, w)
+    def act(out, a, f, r, w, n=LN, k=1, at=None, bias=0.0, scale=1.0, **more):
+        add("s", lambda q: q.activation(out, a, f, bias=bias, scale=scale), r, w, n, k, at, **more)
 
-    def mm(out, terms, r, w, start=True, stop=True, n=None):
+    def lin(out, a, scale, bias, r, w, n=1, k=1, on="s", at=None, pool=False):
+        ways = {"v": (lambda q: q.tensor_scalar(out, a, scale, bias, OP.mult, OP.add), k),
+                "s": (lambda q: q.activation(out, a, AF.Identity, bias=bias, scale=scale), k if k == "g" else 1)}
+        if pool:
+            ways["g"] = (lambda q: q.affine_select(out, a, [[0, n]], OP.is_gt, 0.0, 1, 0), 2)
+        add(on, ways[on][0], r, w, n, ways[on][1], at, ways=ways)
+
+    def sign(out, a, r, w, n, at):
+        ways = {"v": (lambda q: q.tensor_scalar(out, a, -1.0, 1.0, OP.add, OP.min), 0.5),
+                "s": (lambda q: q.activation(out, a, AF.Sign, bias=-1.0, scale=1.0), 1)}
+        add("s", ways["s"][0], r, w, n, 1, at, ways=ways)
+
+    def fill(out, c, w, n):
+        ways = {"v": (lambda q: q.memset(out, float(c)), 0.5),
+                "g": (lambda q: q.iota(out, [[0, n]], c, 0, allow_small_or_imprecise_dtypes=True), 2)}
+        add("g", ways["g"][0], "", w, n, 2, ways=ways)
+
+    def mm(groups, r, w, n=LN, at=None, start=True, stop=True):
         def f(q):
-            for i, (l, x) in enumerate(terms):
-                ins = q.matmul(out, l, x, start and i == 0, stop and i == len(terms) - 1)
+            for out, terms in groups:
+                for i, x in enumerate(terms):
+                    ins = q.matmul(out, x[0], x[1], start and i == 0, stop and i == len(terms) - 1)
             return ins
-        wide = r.startswith("PW") or r.startswith("MM")
-        n = n or (96 if r.startswith("RW") else 64 if r.startswith("B8") or r.startswith("MM") or "VF" in r else LN)
-        add("t", f, r, w, c=len(terms) * n * 0.42 * (4 if wide else 1))
+        add("t", f, r, w, max(n, 64) * sum(x[-1] if len(x) > 2 else 1 for _, terms in groups for x in terms), 0.5, at)
 
-    def iota(out, pat, base, cm, w, flt=True):
+    def iota(out, pat, base_, cm, w, n, flt=True):
         if flt:
-            add("g", lambda q: q.iota(out, pat, base, cm, allow_small_or_imprecise_dtypes=True), "", w)
+            add("g", lambda q: q.iota(out, pat, base_, cm, allow_small_or_imprecise_dtypes=True), "", w, n, 2)
         else:
-            add("g", lambda q: q.iota(out, pat, base, cm), "", w)
+            add("g", lambda q: q.iota(out, pat, base_, cm), "", w, n, 2)
 
-    def gcopy(out, a, n, r, w):
-        add("g", lambda q: q.affine_select(out, a, [[0, n]], OP.is_gt, 0.0, 1, 0), r, w)
+    def dma(e, sem, pairs, r, w, at, c=100):
+        add(e, lambda q: [q.dma_start(a, b) for a, b in pairs], r, w, at=at, dma=sem, c=c * len(pairs))
 
-    def dma(e, sem, pairs, r, w):
-        add(e, lambda q: [q.dma_start(a, b) for a, b in pairs], r, w, dma=sem)
-
-    def send(kind, t, src, r):
+    def send(kind, t, buf, r, at):
         via, dst = route(T, topo, rank, t, kind)
         to = dst if via is None else via
         rid, pid = topo.addr(to, core)
+        a, b = spot(kind, t)
         sent[0] += len(topo.engines(core, to))
-        add("g", lambda q: q.remote_dma(land(T, kind, t), src, T.sem["a%s%d" % (kind, t)], T.sem.lsent, pid, rid, topo.mask(core, to)), r, "",
-            msg="a%s%d" % (kind, t), c=700)
+        add("g", lambda q: q.remote_dma(land(T, kind, t), buf[:, a:b], T.sem["a%s%d" % (kind, t)], T.sem.lsent, pid, rid, topo.mask(core, to)),
+            r, "", at=at, msg="a%s%d" % (kind, t), line=line(kind, t), c=OPEN if (kind, t) == MESSAGES[0] else 0)
 
     def arrival(kind, t):
         s = (rank - 1 - t % 7) % nr
@@ -318,453 +406,318 @@ def rank_program(g, core, T, topo):
     def names(p, n, a=0):
         return " ".join("%s%d" % (p, i) for i in range(a, n))
 
-    def vl(t):
-        return T.QU[:, 36 * t:36 * t + 12]
-
-    def weave(*parts):
-        lists = []
-        for f in parts:
-            n = len(ops)
-            f()
-            lists.append(ops[n:])
-            del ops[n:]
-        while any(lists):
-            for l in lists:
-                while l:
-                    o = l.pop(0)
-                    ops.append(o)
-                    if o["e"] == "v":
-                        break
+    def two(buf, t, a=0, b=LN, c=1, n=LN):
+        return buf[:, n * (t % 2) + a:n * (t % 2) + b:c]
 
     col = lambda i: T.C2[:, i:i + 1]
     PC, KC, GC, HC = T.CF[:, 0:1], T.CF[:, 1:2], T.CF[:, 2:3], T.CF[:, 3:4]
-    LO, HI, H0, H1, CC, B8C, G15, DC, K16, R0, R1, R2 = [col(i) for i in range(12)]
-    IDN, ROT, UNR = T.PW[:, 0:128], T.PW[:, 112:240], T.PW[:, 16:144]
+    LO, HI, H0, H1, CC, B8C, G15, DC, K16, R0, R1, R2, DN, L4, M4, DL, VS_, VB, D0, D1, LS, LB = [col(i) for i in range(22)]
+    IDN, ROT = T.PW[:, 0:128], T.PW[:, 112:240]
     IH = T.PH[:, 0:128]
     rw = lambda i: T.RW[:, 128 * i:128 * i + 128]
-    Sw = T.S[:, 0:W]
-    KAw, NMw = T.KA[:, 0:NN], T.NM[:, 0:NN]
+    dg = lambda i: T.DG[:, 128 * i:128 * i + 128]
+    sel = lambda j: T.SEL[:, 128 * j:128 * j + 128]
+    Sw, KAw, NMw = T.S[:, 0:W], T.KN[:, 0:NN], T.KN[:, NN:2 * NN]
+    vl = lambda s: T.QU[:, 36 * s + 12:36 * s + 24]
+    ol = lambda s: T.QU[:, 36 * s + 24:36 * s + 36]
+    sg = lambda t, a, b, c=1: two(T.SG, t, a, b, c, 1920)
+    GJ, GU = T.GW[:, 0:LN], T.GW[:, LN:NN]
 
-    def ku(t):
-        act(T.KU[:], T.KA[:, t % 2::2], AF.Identity, "KA", "KU", bias=24704.0, scale=-128.0)
-
-    def su(t):
-        ts(T.SU[:], T.NM[:, t % 2::2], -67072.0, None, OP.add, None, "NM", "SU")
-
-    def kv(t):
-        act(T.KV[:], KAw.indirect(vl(t)), AF.Identity, "KA QU%d" % t, "KV", bias=-24704.0, scale=128.0)
-        mm(T.pR[:, 0:96], [(rw(0), T.KV[:, 0::2]), (rw(1), T.KV[:, 1::2])], "RW0 RW1 KV", "pR")
-
-    def eu(t):
-        par = t % 2
-        mm(T.pN[:, 288:480], [(IH, T.KV[:]), (IH, T.UN[:, LN * par:LN * par + LN])], "PH0 KV UN%d" % par, "pN")
-        act(T.EA[:], T.pN[:, 288:480], AF.Abs, "pN", "EA")
-
-    def eu2(t):
-        act(T.EU[:], T.EA[:], AF.Sign, "EA", "EU", bias=-64.0)
-
-    def nv(t):
-        ts(T.NV[:], NMw.indirect(vl(t)), -67072.0, 1.0 / 2048, OP.add, OP.mult, "NM QU%d" % t, "NV")
-
-    def dmm(j):
-        b = "pD%d" % ((j // 2) % 3)
-        sel = T.SEL[:, 128 * j:128 * j + 128]
-        terms = [(sel, T.KV[:]), (IH, T.KU[:])] + ([(sel, T.NV[:])] if j >= 8 else [])
-        mm(T[b][:, LN * (j % 2):LN * (j % 2) + LN], terms, "SEL%d PH0 KV KU" % j + (" NV" if j >= 8 else ""), b)
-
-    def dabs(j):
-        b = "pD%d" % ((j // 2) % 3)
-        src = T[b][:, LN * (j % 2):LN * (j % 2) + LN]
-        if j < 8:
-            act(T.AL[:, j::8], src, AF.Abs, b, "A%d" % j, bias=float(j), scale=2048.0)
+    def differ(t, b, hi, at):
+        bank, a, par = "pD%d" % ((b + hi + t) % 2), 64 * b, t % 2
+        groups = []
+        for pos in range(8):
+            j = 8 * hi + 7 - pos
+            terms = [(sel(j), T.KH[:, a:a + 64] if hi else two(T.KV, t, a, a + 64)), (IH, two(T.KU, t, a, a + 64))]
+            groups.append((T[bank][:, pos::8], terms + ([(sel(j), T.NV[:, a:a + 64])] if hi else [])))
+        mm(groups, names("SEL", 8 * hi + 8, 8 * hi) + " PH0 KU%d " % par + ("KH NV" if hi else "KV%d" % par), bank, 64, at)
+        if hi:
+            act(T.A[:, 8 * a:8 * a + 512], T[bank][:], AF.Abs, bank, "A%d" % b, 512, 1, at + 0.8, bias=1536.0 + 4096.0)
         else:
-            act(T.A[:, j - 8::8], src, AF.Abs, b, "A%d" % j, bias=1536.0 + 4096.0 * (j - 7), scale=2048.0)
+            act(T.AL[:, 8 * a:8 * a + 512], T[bank][:], AF.Abs, bank, "AL%d" % b, 512, 1, at + 0.6, scale=4096.0)
 
-    def match(a, b):
-        for j in range(a, b):
-            dmm(j)
-            if j % 2 and j < 10:
-                dabs(j - 1)
-                dabs(j)
+    def low(t):
+        par, n, bank = t % 2, NN if t < 5 else LN, "pD%d" % ((t + 1) % 2)
+        during(t - 2)
+        lin(two(T.KV, t), T.KL[:, 0:NN].indirect(vl(t)), VS_, VB, "KL VS_ VB QU%d" % t, "KV%d" % par, LN, "g", "s", 9.3)
+        lin(two(T.KU, t), T.KN[:, par:NN:2], -BIG, 193 * BIG, "KA", "KU%d" % par, LN, 1, "s", 3.3)
+        mm([(T.pU[:, 400:496], [(rw(0), two(T.KV, t, 0, LN, 2)), (rw(1), two(T.KV, t, 1, LN, 2))])], "RW0 RW1 KV%d" % par, "pU", 96, 9.8)
+        ts(T.KP[:], T.pU[:, 400:496], 1 / BIG, 192.0, OP.mult, OP.add, "pU", "KP", 96, at=13.0)
+        for b in range(3):
+            differ(t, b, 0, 10.0 + 0.6 * b)
+        groups = [(T[bank][:, 0:LN], [(IH, two(T.KV, t)), (dg(6), two(T.UN, t))])]
+        if t < 5:
+            groups.append((T[bank][:, LN:NN], [(rw(2), two(T.KV, t)), (IH, two(T.KU, t))]))
+        mm(groups, "PH0 RW2 DG6 KV%d KU%d UN" % (par, par), bank, LN, 11.8)
+        act(T.AL[:, 1536:1536 + n], T[bank][:, 0:n], AF.Abs, bank, "AL3", n, 1, 12.3)
+        during(t - 1)
+        tt(T.E[:], T.X[:, 0:NN].indirect(T.KP[:]), two(T.XU, t, 0, 1536, 1, 1536), OP.is_equal, "X KP " + names("XU%d_" % par, 8), "E", 1536, "g", 5.4)
+        sign(sg(t, 0, 1024), T.AL[:, 0:1024], "AL0 AL1", "SG%da" % par, 1024, 3.5)
+        sign(sg(t, 1024, 1536 + n), T.AL[:, 1024:1536 + n], "AL2 AL3", "SG%db" % par, 512 + n, 4.9)
+        scan(two(T.RL, t, 0, 1536, 1, 1536), T.RST[:], T.AL[:, 0:1536], OP.add, OP.min, "RST " + names("AL", 3), "RL%d" % par, 1536, 0.5, 7.5)
 
-    def match_rest(t):
-        for j in range(10, 16):
-            dabs(j)
-        for h in range(2):
-            act(T.SG[:, 768 * h:768 * h + 768], T.AL[:, 768 * h:768 * h + 768], AF.Sign, names("A", 8), "SG%d" % h, bias=-65535.0)
+    def high(t):
+        during(t - 1 if t else -1.6)
+        lin(T.KH[:], KAw.indirect(vl(t)), BIG, -193 * BIG, "KA QU%d" % t, "KH", LN, "g", "s", 3.0)
+        ts(T.NV[:], NMw.indirect(vl(t)), -67072.0, None, OP.add, None, "NM QU%d" % t, "NV", LN, "g", at=5.1)
+        for b in range(3):
+            differ(t, b, 1, 5.7 + 0.65 * b)
 
-    def kp(t):
-        ts(T.KP[:], T.pR[:, 0:96], 1.0 / 128, 192.0, OP.mult, OP.add, "pR", "KP")
+    def choose(t):
+        par, s, row = t % 2, t + 2, 32 * (t // 2)
+        during(t - 1)
+        terms = [(T.CS[:, 8 + pos:136 + pos], sg(t, pos, 1536, 8)) for pos in range(8)] + [(dg(6), sg(t, 1536, 1728))]
+        terms += [(dg(4), two(T.KV, t)), (dg(5), T.ONES[:]), (T.B8[row:row + 8, 7:135], T.SP16[row:row + 8, LN * par:LN * par + LN])]
+        mm([(T.pZ[:, 0:LN], terms)], "CS DG6 SG%da SG%db DG4 KV%d DG5 ONES B8 SP16" % (par, par, par), "pZ", LN, 7.6, stop=False)
+        mm([(T.pZ[:, 0:LN], [(T.CE[:, 15 - j:143 - j], T.E[:, j::8]) for j in range(8)])], "CE E", "pZ", LN, 8.5, start=False)
+        add("v", lambda q: q.transpose(T.ZT[:], T.pZ[:, 0:LN]), "pZ", "ZT", LN, 1, 9.9)
+        scan(T.ZR[:], T.RSZ[:], T.ZT[:], OP.mult, OP.max, "RSZ ZT", "ZR", LN, 1, 10.3)
+        cp(T.BI[:], T.ZR[:, 15::16], "ZR", "BI", 12, 10.6)
+        b, c = 0 if s < 7 else 12, 36 if s < 5 else 24
+        ts(T.QI[:, 12:24], T.BI[:], 511, None, OP.bitwise_and, None, "BI", "QIv", at=10.9)
+        if s < 7:
+            ts(T.QI[:, 0:12], T.BI[:], 9, 15, OP.logical_shift_right, OP.bitwise_and, "BI", "QIj", at=10.95)
+        if s < 5:
+            ts(T.QI[:, 24:36], T.BI[:], 3, None, OP.bitwise_and, None, "BI", "QIo", at=11.0)
+        cp(T.QH[:, b:c], T.QI[:, b:c], "QIv QIj QIo", "QH", c - b, 11.3)
+        mm([(T.pZ[:, 256 + b + e:256 + c:2], [(T.MM[:, 256 * e + 128 * h:256 * e + 128 * h + 128], T.QH[:, b + h:c:2]) for h in range(2)])
+            for e in range(2)], names("MM", 4) + " QH", "pZ", 18, 11.6)
+        lists(s, b, c, T.pZ[:, 256 + b:256 + c], "pZ", 12.0)
 
-    def counts(t):
-        par = t % 2
-        tt(T.E[:], T.X[:, 0:NN].indirect(T.KP[:]), T.XU[:, 1536 * par:1536 * par + 1536], OP.is_equal, "X KP " + names("XU%d_" % par, 8), "E")
-
-    def same(t):
-        act(T.GA[:], T.TA[:, 0:NN].indirect(vl(t)), AF.Identity, names("TA", 4) + " QU%d" % t, "GA")
-        mm(T.pM[:, 0:LN], [(T.DG[:, 640:768], T.GA[:]), (T.DG[:, 384:512], T.KU[:])], "DG5 DG3 GA KU", "pM")
-        act(T.EB[:], T.pM[:, 0:LN], AF.Abs, "pM", "EB")
-        act(T.EM[:], T.EB[:], AF.Sign, "EB", "EM", bias=-64.0)
-        mm(T.pM[:, 0:LN], [(T.BLK8[:], T.EM[:]), (T.DG[:, 512:640], T.ONES[:])], "BLK8 EM DG4 ONES", "pM")
-
-    def h8(t):
-        tt(T.H8[:], T.HG[:], T.pM[:, 0:LN], OP.mult, "HG pM", "H8")
+    def lists(s, b, c, src, r, at):
+        a, u = 36 * s, 36 * (s % 2)
+        tt(T.QF[:, a + b:a + c], src, T.UB[:, u + b:u + c], OP.add, r + " UB", "QF%d" % s, c - b, 1, at)
+        cp(T.QU[:, a + b:a + c], T.QF[:, a + b:a + c], "QF%d" % s, "QU%d" % s, c - b, at + 0.3)
+        if s < 5:
+            mm([(T.pZ[:, 304:328], [(ROT, T.QF[:, a + 12:a + 36], 4)])], "PW QF%d" % s, "pZ", 24, at + 0.4)
+            lin(T.VS[:, 24 * s:24 * s + 24], T.pZ[:, 304:328], 1.0, 0.0, "pZ", "VS%d" % s, 24, 1, "s", at + 0.9)
+            send("v", s, T.VS, "VS%d" % s, at + 1.2)
 
     def lowest(t):
-        scan(T.RL[:], T.RST[:], T.AL[:], OP.add, OP.min, "RST " + names("A", 8), "RL")
-        mm(T.pR[:, 128:320], [(IH, T.RL[:, 7::8]), (IH, T.V8[:]), (T.DG[:, 0:128], T.ONES[:])], "PH0 RL V8 DG0 ONES", "pR")
-        mm(T.pR[:, 320:416], [(rw(2), T.SU[:, 0::2]), (rw(3), T.SU[:, 1::2])], "RW2 RW3 SU", "pR")
+        a, m = NN + t % 2, 288 * t
+        during(t - 1 if t else -1.6)
+        mm([(T.pR[:, 320:416], [(T.RF[:, 0:128], T.KN[:, a::4], 4), (T.RF[:, 128:256], T.KN[:, a + 2::4], 4)])], "RF0 RF1 NM", "pR", 96, 5.9)
+        ts(T.ML[:, m + LN:m + 288], T.pR[:, 320:416], -65536.0, None, OP.add, None, "pR", "MS%d" % t, 96, at=8.2)
+        mm([(T.pR[:, 128:320], [(dg(3), two(T.RL, t, 7, 1536, 8, 1536)), (sel(0), T.NV[:]), (dg(0), T.ONES[:])])],
+           "DG3 RL%d SEL0 NV DG0 ONES" % (t % 2), "pR", LN, 8.6)
+        tt(T.pR[:, 128:320], T.pR[:, 128:320], T.KN[:, a::2], OP.min, "pR NM", "pR", LN, 1, 10.1)
+        scan(T.RR[:], T.RST[:], T.A[:], OP.add, OP.min, "RST " + names("A", 3), "RR", 1536, 1, 8.6)
+        tt(T.MI[:], T.pR[:, 128:320], T.RR[:, 7::8], OP.min, "RR pR", "MI", LN, 1, 10.5)
+        ts(T.MJ[:], T.MI[:], 4095, None, OP.bitwise_and, None, "MI", "MJ", LN, at=11.4)
+        ts(T.M16[:], T.MJ[:], -1536.0, None, OP.add, None, "MJ", "M16", LN, at=11.9)
+        mm([(T.pR[:, 128 + 96 * h:224 + 96 * h], [(rw(2 * h), T.M16[:, 0::2]), (rw(2 * h + 1), T.M16[:, 1::2])]) for h in range(2)],
+           names("RW", 4) + " M16", "pR", 96, 12.2)
+        ts(T.ML[:, m:m + LN], T.pR[:, 128:320], 1536.0, None, OP.add, None, "pR", "ML%d" % t, LN, at=12.6)
 
-    def lowest2(t):
-        tt(T.pR[:, 128:320], T.pR[:, 128:320], T.NM[:, t % 2::2], OP.min, "pR NM", "pR")
-        scan(T.RR[:], T.RST[:], T.A[:], OP.add, OP.min, "RST " + names("A", 16, 8), "RR")
-
-    def mchain(t):
-        tt(T.MI[:], T.pR[:, 128:320], T.RR[:, 7::8], OP.min, "RR pR", "MI")
-        ts(T.MJ[:], T.MI[:], 4095, None, OP.bitwise_and, None, "MI", "MJ")
-        ts(T.M16[:], T.MJ[:], -1536.0, None, OP.add, None, "MJ", "M16")
-        mm(T.pR[:, 128:224], [(rw(0), T.M16[:, 0::2]), (rw(1), T.M16[:, 1::2])], "RW0 RW1 M16", "pR")
-        mm(T.pR[:, 224:320], [(rw(2), T.M16[:, 0::2]), (rw(3), T.M16[:, 1::2])], "RW2 RW3 M16", "pR")
-
-    def ml(t):
-        ts(T.ML[:], T.pR[:, 128:416], 1536.0, None, OP.add, None, "pR", "ML")
-
-    def zmm(t):
-        terms = [(T.CE[:, 15 - j:143 - j], T.E[:, j::8]) for j in range(8)]
-        terms += [(rw(4), T.KV[:]), (rw(4), T.C192[:]), (T.WU[:], T.EU[:]), (T.DGC[:], T.ONES[:])]
-        mm(T.pZ[:, 0:LN], terms, "CE E RW4 KV C192 WU EU DGC ONES", "pZ", stop=False)
-
-    def zmm2(t):
-        mm(T.pZ[:, 0:LN], [(T.CS[:, 15 - j:143 - j], T.SG[:, j::8]) for j in range(8)], "CS " + names("SG", 2), "pZ", start=False)
-
-    def zchain(t):
-        add("v", lambda q: q.transpose(T.ZT[:], T.pZ[:, 0:LN]), "pZ", "ZT")
-        scan(T.ZR[:], T.RSZ[:], T.ZT[:], OP.mult, OP.max, "RSZ ZT", "ZR")
-        for e in range(2):
-            mm(T.pZ[:, 256 + e:268:2], [(T.MM[:, 256 * e + 128 * h:256 * e + 128 * h + 128], T.ZR[:, 16 * h + 15::32]) for h in range(2)],
-               names("MM", 4) + " ZR", "pZ")
-
-    def best(t):
-        tt(T.BI[:], T.pZ[:, 256:268], T.ALT[:, 12 * t:12 * t + 12], OP.max, "pZ ALT", "BI")
-
-    def i4(t):
-        s = t + 2
-        a, q = 48 * s, "QI%d" % s
-        ts(T.QI[:, a + 24:a + 36], T.BI[:], 7, None, OP.bitwise_and, None, "BI", q + "b")
-        ts(T.QI[:, a + 36:a + 48], T.BI[:], 6, 120, OP.logical_shift_right, OP.bitwise_and, "BI", q + "c")
-        ts(T.QI[:, a:a + 12], T.BI[:], 511, None, OP.bitwise_and, None, "BI", q)
-        ts(T.QI[:, a + 12:a + 24], T.BI[:], 1023, None, OP.bitwise_and, None, "BI", q + "a")
-        tt(T.QI[:, a + 24:a + 36], T.QI[:, a + 24:a + 36], T.QI[:, a + 36:a + 48], OP.add, q + "b " + q + "c", q + "b")
-
-    def vf(s):
-        cp(T.VF[:, 0:12], T.QI[:, 48 * s:48 * s + 12], "QI%d" % s, "VF")
-        mm(T.pN[:, 256:268], [(ROT, T.VF[:, 0:12])], "PW0 PW1 VF", "pN")
-
-    def qu(s, n=36):
-        q = "QI%d" % s
-        cp(T.QU[:, 36 * s:36 * s + n], T.QI[:, 48 * s:48 * s + n], "%s %sa %sb" % (q, q, q), "QU%d" % s)
-
-    def vsend(s):
-        act(T.VS[:, 12 * s:12 * s + 12], T.pN[:, 256:268], AF.Copy, "pN", "VS%d" % s)
-        send("v", s, T.VS[:, 12 * s:12 * s + 12], "VS%d" % s)
-
-    def lists(t):
+    def rewrite_low(t):
         par = t % 2
-        cp(T.LI[:, 24:36], T.GV[:, 12 * t:12 * t + 12], "", "LIc", wait=arrival("v", t))
-        ts(T.LJ[:, 0:12], T.QI[:, 48 * t:48 * t + 12], 3, None, OP.bitwise_and, None, "QI%d" % t, "LJa")
-        ts(T.LJ[:, 12:24], T.LI[:, 24:36], 3, None, OP.bitwise_and, None, "LIc", "LJb")
-        tt(T.LI[:, 0:24], T.LJ[:], T.UB[:, 24 * par:24 * par + 24], OP.add, "LJa LJb UB%d" % par, "LIa")
-        cp(T.LU[:, 36 * t:36 * t + 36], T.LI[:], "LIa LIc", "LU%d" % t)
+        during(t - 1 if t else -0.3)
+        ts(T.LG[:, 24 * t:24 * t + 24], land(T, "v", t), 4.0, None, OP.add, None, "", "Lv%d" % t, 24, at=4.9, wait=arrival("v", t),
+           **(dict(behind=t - 1) if t else {}))
+        lin(two(T.GT, t), T.TB[:, 0:392].indirect(T.LG[:, 24 * t:24 * t + 12]), 1.0, 0.0, names("TB", 4) + " Lv%d" % t, "GT%d" % par, LN, "g", "s", 5.6)
+        mm([(T.pU[:, 0:LN], [(dg(7), two(T.KV, t)), (dg(8), T.ONES[:]), (IH, two(T.GT, t))])], "PH0 KV%d GT%d DG7 DG8 ONES" % (par, par), "pU",
+           LN, 7.0)
+        tt(T.T2[:], T.pU[:, 0:LN], T.KL[:, par::2], OP.min, "pU KL", "T2", LN, 1, 8.4)
+        act(T.KL[:, par::2], T.T2[:], AF.Abs, "T2", "KL", LN, 1, 8.8)
 
-    def v8(t):
-        act(T.V8[:], T.IO[:, 0:NN].indirect(vl(t)), AF.Identity, "IO QU%d" % t, "V8", bias=-1536.0, scale=8.0)
-
-    def gab(t):
-        act(T.GT[:], T.TB[:, 0:NN].indirect(T.LU[:, 36 * t + 24:36 * t + 36]), AF.Identity, names("TB", 4) + " LU%d" % t, "GT")
-
-    def advance(t):
+    def rewrite(t):
         par, s = t % 2, t + 2
-        ku(t + 1)
-        su(t + 1)
-        best(t)
-        if t > 0:
-            h8(t)
-            h8r(t)
-        i4(t)
-        qu(s)
-        act(T.GU[:], T.TC[:, 0:896].indirect(T.QU[:, 36 * s + 12:36 * s + 24]), AF.Identity, names("TC", 10) + " QU%d" % s, "GU")
-        mm(T.pZ[:, 272:464], [(IH, T.GA[:]), (IH, T.GT[:]), (T.DG[:, 128:256], T.ONES[:]), (IH, T.GU[:])], "PH0 GA GT GU DG1 ONES", "pZ")
-        act(T.GJ[:], T.TJ[:, 0:128].indirect(T.QU[:, 36 * s + 24:36 * s + 36]), AF.Identity, names("TJ", 8) + " QU%d" % s, "GJ")
-        mm(T.pO[:, 256:448], [(T.DG[:, 384:512], T.V8[:]), (T.DG[:, 256:384], T.ONES[:]), (IH, T.GJ[:])], "PH0 GJ V8 DG2 DG3 ONES", "pO")
-        if s < 5:
-            vf(s)
-        if t > 0:
-            own(t - 1)
-        else:
-            spares(12, 72)
-        tt(T.T3[:], T.pZ[:, 272:464], T.KA[:, par::2], OP.min, "pZ KA", "T3")
-        tt(T.N2[:], T.pO[:, 256:448], T.NM[:, par::2], OP.min, "pO NM", "N2")
-        act(T.KA[:, par::2], T.T3[:], AF.Abs, "T3", "KA")
-        kv(t + 1)
-        act(T.NM[:, par::2], T.N2[:], AF.Abs, "N2", "NM")
-        if t + 1 < 5:
-            same(t + 1)
-        eu(t + 1)
-        match(0, 6)
-        kp(t + 1)
-        nv(t + 1)
-        eu2(t + 1)
-        match(6, 8)
-        v8(t + 1)
-        match(8, 16)
-        if s < 5:
-            vsend(s)
-        counts(t + 1)
-        zmm(t + 1)
-        lowest(t + 1)
+        during(t)
+        lin(T.GW[:], T.TC[:, 0:400].indirect(T.QU[:, 36 * s:36 * s + 24]), 1.0, 0.0, names("TC", 10) + " QU%d" % s, "GW", NN, "g", "s", -0.8)
+        mm([(T.pU[:, 0:LN], [(dg(7), two(T.KV, t)), (IH, two(T.GT, t)), (dg(1), T.ONES[:]), (rw(3), GU), (rw(1), GJ)]),
+            (T.pU[:, LN:NN], [(sel(16), T.NV[:]), (dg(2), T.ONES[:]), (rw(1), GU), (rw(3), GJ)])],
+           "PH0 KV%d GT%d GW NV DG1 DG2 DG7 SEL16 RW1 RW3 ONES" % (par, par), "pU", LN, -0.1)
+        tt(T.T3[:], T.pU[:, 0:NN], T.KN[:, par::2], OP.min, "pU KA NM", "T3", NN, 1, 1.65)
+        act(T.KN[:, par::2], T.T3[:], AF.Abs, "T3", "KA NM", NN, 1, 2.6)
 
-    def spares(a, b):
-        cp(T.SP16[0:8, 16 * a:16 * b], T.SPI[0:8, 16 * a:16 * b], "SPI", "SP16")
-
-    def spares2(a, b):
-        mm(T.pR[:, 424 + a:424 + b], [(T.B8[0:8, 15 - p:143 - p], T.SP16[0:8, 16 * a + p:16 * b:16]) for p in range(16)], "B8 SP16", "pR")
-
-    def alt(a, b):
-        act(T.ALT[:, a:b], T.pR[:, 424 + a:424 + b], AF.Identity, "pR", "ALT", bias=2096640.0)
-
-    def llo(t):
+    def ahead(t):
+        during(t - 1)
         for k in range(8):
-            act(T.LLO[:, k::8], T.S[:, 8 * (t % 2) + k::16], AF.Sigmoid, "S", "LL%d" % k)
-            if t == 0:
-                ops[-1].update(dict(c=1520, w=["LL0", "SIG"]) if k == 0 else dict(after=["SIG"]))
+            act(two(T.LLO, t, k, 1536, 8, 1536), T.S[:, 8 * (t % 2) + k::16], AF.Sigmoid, "S", "LL%d_%d" % (t % 2, k), at=8.5, after=["ONES"])
+        if t < 5:
+            lin(T.HG[:], Sw.indirect(ol(t)), 1.0, 0.0, "S QU%d" % t, "HG", LN, "g", "s", 7.0)
 
-    def hg(t):
-        act(T.HG[:], Sw.indirect(T.LU[:, 36 * t:36 * t + 12]), AF.Identity, "S LU%d" % t, "HG")
-
-    bank = ("pO", "pM")
-
-    def half(h):
-        return T.pM[:, 384:480] if h else T.pO[:, 0:96]
+    def h8(t):
+        par = t % 2
+        during(t - 1)
+        mm([(T.pN[:, 0:LN], [(ROT, T.HG[:], 4), (T.BR[:], sg(t, 1728, 1920))])], "PW HG BR SG%db" % par, "pN", LN, 9.0)
+        act(two(T.H8, t), T.pN[:, 0:LN], AF.Relu, "pN", "H8%d" % par, LN, 1, 9.6, bias=32.0, scale=8.0)
 
     def products(t):
+        par, m = t % 2, 288 * t
         turn = ROT if t < 5 else IDN
-        for h in range(2):
-            act(T.LHI[:, 768 * h:768 * h + 768], Sw.indirect(T.ML[:, 192 + 48 * h:240 + 48 * h]), AF.Sigmoid, "S ML", "LH%d" % h)
-        for h in range(2):
+        during(t)
+        for i, (a, b, kind) in enumerate(PARTS):
+            act(T.LHI[:, 8 * a:8 * b], Sw.indirect(T.ML[:, m + LN + a // 2:m + LN + b // 2]), AF.Sigmoid, "S MS%d" % t, "LH%d" % i, 8 * (b - a), "g",
+                0.3 + a / 85, after=["ONES"])
+        for i, (a, b, kind) in enumerate(PARTS):
+            bank, n = "p" + kind, b - a
             for u in range(2):
-                a = 1536 * u + 768 * h
-                left = T.LHI[:, 768 * h:768 * h + 768] if u else T.LLO[:, 768 * h:768 * h + 768]
-                r = "P%d%d" % (h, u)
-                tt(T.P[:, a:a + 768], Sw.indirect(T.ML[:, 96 * u + 48 * h:96 * u + 48 * h + 48]), left, OP.mult,
-                   "S ML " + ("LH%d" % h if u else names("LL", 8)), r)
-                if h == 1 and u == 1 and t in SCAN_LAST:
-                    scan(T.PS[:], T.RS8[:], T.P[:, a:a + 768], OP.mult, OP.add, "RS8 " + r, "PS")
-                    terms, r = [(turn, T.PS[:, 7::8])], "PS"
+                p, at = 1536 * u + 8 * a, 0.3 + (2 * a + u * n) / 90
+                left = T.LHI[:, 8 * a:8 * b] if u else two(T.LLO, t, 8 * a, 8 * b, 1, 1536)
+                r = "P%d%d" % (i, u)
+                tt(T.P[:, p:p + 8 * n], Sw.indirect(T.ML[:, m + 96 * u + a // 2:m + 96 * u + b // 2]), left, OP.mult,
+                   "S ML%d " % t + ("LH%d" % i if u else names("LL%d_" % par, 8)), r, 8 * n, "g", at)
+                if u == 1 and i >= SCAN_FROM[t]:
+                    w = "PS" if i == len(PARTS) - 1 else "PS%d" % i
+                    scan(T.PS[:, 8 * a:8 * b], T.RS8[:, 0:8 * n], T.P[:, p:p + 8 * n], OP.mult, OP.add, "RS8 " + r, w, 8 * n, 1, at + 0.7)
+                    terms, r = [(turn, T.PS[:, 8 * a + 7:8 * b:8], 4)], w
                 else:
-                    terms = [(turn, T.P[:, a + k:a + 768:8]) for k in range(8)]
-                if u == 0 and t < 5:
-                    mm(half(h), [(ROT, T.H8[:, 96 * h:96 * h + 96])], "PW0 PW1 H8", bank[h], stop=False, n=96)
-                mm(half(h), terms, "PW0 PW1 " + r, bank[h], start=(u == 0 and t == 5), stop=(u == 1), n=96)
-            if t < 5:
-                ap = T.TS[:, LN * t + 96 * h:LN * t + 96 * h + 96]
-                act(ap, half(h), AF.Sigmoid, bank[h], "TS%d%s" % (t, "ab"[h]), scale=0.25)
-                send("ab"[h], t, ap, "TS%d%s" % (t, "ab"[h]))
-            else:
-                act(T.OB[:, 5 * LN + 96 * h:5 * LN + 96 * h + 96], half(h), AF.Copy, bank[h], "TS5" + "ab"[h])
+                    terms = [(turn, T.P[:, p + k:p + 8 * n:8], 4) for k in range(8)]
+                c, d = SPAN[kind]
+                if u == 0 and t < 5 and a == c:
+                    mm([(T[bank][:, c:d], [(IDN, two(T.H8, t, c, d), 4)])], "PW H8%d" % par, bank, d - c, at - 0.8, stop=False)
+                mm([(T[bank][:, a:b], terms)], "PW " + r, bank, n, 1.2 * at + 0.8, start=(u == 0 and t == 5), stop=(u == 1 and (b == d or t == 5)))
+            if b == SPAN[kind][1]:
+                a, at = SPAN[kind][0], 1.2 * at + 1.2
+                if t < 5:
+                    act(T.TS[:, LN * t + a:LN * t + b], T[bank][:, a:b], AF.Sigmoid, bank, "TS%d%s" % (t, kind), b - a, 1, at, scale=0.25)
+                    send(kind, t, T.TS, "TS%d%s" % (t, kind), at + 0.2)
+                else:
+                    lin(T.OB[:, 5 * LN + a:5 * LN + b], T[bank][:, a:b], 1.0, 0.0, bank, "OB5" + kind, b - a, 1, "s", at)
+                    dma("y", "do" + kind, [(T.yo[:, 5 * LN + a:5 * LN + b], T.OB[:, 5 * LN + a:5 * LN + b])], "OB5" + kind, "", at + 0.2)
 
-    def h8r(t):
-        mm(T.pM[:, LN:2 * LN], [(ROT, T.H8[:])], "PW0 PW1 H8", "pM")
-        act(T.H8R[:], T.pM[:, LN:2 * LN], AF.Copy, "pM", "H8R")
+    def settle(t):
+        during(t)
+        a = LN * t
+        dma("y", "dt%d" % t, [(T.SL[0:112, :], T.TS[16:128, a:a + LN]), (T.SL[112:128, :], T.TS[0:16, a:a + LN])], "TS%da TS%db A0" % (t, t),
+            "SL", 6.8)
+        ts(Sw.indirect(ol(t)), T.SL[:], 2.0, -1.0, OP.mult, OP.add, "SL QU%d" % t, "S", LN, "s", at=10.8)
+        for kind, (a, b) in SPAN.items():
+            tt(T.OB[:, LN * t + a:LN * t + b], T["p" + kind][:, a:b], two(T.H8, t, a, b), OP.subtract, "p%s H8%d" % (kind, t % 2),
+               "OB%d%s" % (t, kind), b - a, 1, 8.5 + a / 35)
+        for kind, (a, b) in SPAN.items():
+            ts(Sw.indirect(T.LG[:, 24 * t + 12 + a // 16:24 * t + 12 + b // 16]), land(T, kind, t), 2.0, -1.0, OP.mult, OP.add,
+               "Lv%d" % t, "S", b - a, "s", at=12.8 + a / 256, wait=arrival(kind, t))
 
-    def post(t):
-        mm(T.pN[:, 0:LN], [(UNR, T.TS[:, LN * t:LN * t + LN])], "PW0 PW1 TS%da TS%db" % (t, t), "pN")
-        act(T.SL[:], T.pN[:, 0:LN], AF.Copy, "pN", "SL")
-
-    def own(t):
-        ts(Sw.indirect(T.LU[:, 36 * t:36 * t + 12]), T.SL[:], 2.0, -1.0, OP.mult, OP.add, "SL LU%d" % t, "S")
-
-    def outp(t):
-        for h in range(2):
-            a = LN * t + 96 * h
-            tt(T.OB[:, a:a + 96], half(h), T.H8R[:, 96 * h:96 * h + 96], OP.subtract, bank[h] + " H8R", "OB%d%s" % (t, "ab"[h]))
-
-    def guest(t):
-        for h in range(2):
-            ts(Sw.indirect(T.LU[:, 36 * t + 12 + 6 * h:36 * t + 18 + 6 * h]), land(T, "ab"[h], t), 2.0, -1.0, OP.mult, OP.add, "LU%d" % t, "S",
-               wait=arrival("ab"[h], t), c=350)
-
-    def partners(par):
-        cp(T.YT[:], T.IO[:, 0:NN].indirect(vl(6 + par)), "IO QU%d" % (6 + par), "YT")
-        act(T.YP[:, par::2], T.YT[:], AF.Copy, "YT", "YP%d" % par)
-
-    ms(T.NR[:], 0, "NR0 NR1")
-    dma("y", "dpv", [(T.PVI[0:8, :], T.pv[:])], "", "PVI")
-    dma("s", "dka", [(T.KI[:], T.ka[:])], "", "KI")
-    dma("y", "dx", [(T.X[:], T.xa[:])], "", "X")
-    dma("y", "dn0", [(T.NR[16 * a + 8:16 * a + 16, :], T.nm[8 * a:8 * a + 8, :]) for a in range(4)], "", "NR0")
-    dma("s", "dn1", [(T.NR[16 * a + 8:16 * a + 16, :], T.nm[8 * a:8 * a + 8, :]) for a in range(4, 8)], "", "NR1")
-    dma("y", "dsp", [(T.SPI[0:8, :], T.sp[:])], "", "SPI")
-    iota(T.CI[:, 0:1], [[0, 1]], 0, 1, "CI0", False)
-    iota(T.IO[:], [[1, NN]], 0, 0, "IO")
-    iota(T.GB[:], [[16, 8], [0, 16]], 0, 0, "GB")
-    dma("g", "ds0", [(T.S[:], T.s0[:])], "", "S")
-    iota(T.UBI[:], [[4, 2], [256, 12]], 0, 0, "UBI")
-    iota(T.JV[:], [[1, 8]], -(7 + 1048576), 0, "JV")
-    iota(T.RST[:], [[0, 1536]], 0, 0, "RST")
-    ts(T.CI[:, 1:2], T.CI[:, 0:1], 15, None, OP.bitwise_and, None, "CI0", "CI1")
-    ts(T.CI[:, 2:3], T.CI[:, 0:1], 112, None, OP.bitwise_and, None, "CI0", "CI2")
-    ts(T.CI[:, 3:4], T.CI[:, 0:1], 16, None, OP.bitwise_and, None, "CI0", "CI3")
-    ms(T.ONES[:], 1.0, "ONES")
-    cp(T.CF[:], T.CI[:], "CI0 CI1 CI2 CI3", "CF")
-    ms(T.C192[:], 24576.0, "C192")
-    ts(B8C, PC, 16.0, 15.0, OP.mult, OP.add, "CF", "B8C")
-    ts(LO, KC, 8.0, None, OP.is_lt, None, "CF", "LO")
-    ts(HI, KC, 8.0, None, OP.is_ge, None, "CF", "HI")
-    ts(T.EQ[:], T.IO[:, 0:16], KC, None, OP.is_equal, None, "IO CF", "EQ")
-    ts(T.B8[0:8, :], T.IO[0:8, 0:144], T.C2[0:8, 5:6], None, OP.is_equal, None, "IO B8C", "B8")
-    ts(CC, KC, LO, 65536.0, OP.mult, OP.add, "CF LO", "CC")
-    ts(T.BLK[:], T.GB[:], GC, None, OP.is_equal, None, "GB CF", "BLK")
-    ts(T.PH[:, 0:128], T.IO[:, 0:128], PC, None, OP.is_equal, None, "IO CF", "PH0")
-    ts(T.PH[:, 128:256], T.IO[:, 0:128], PC, None, OP.is_equal, None, "IO CF", "PH1")
-    act(T.IO8[:], T.IO[:], AF.Identity, "IO", "IO8", scale=8.0)
+    during(-3)
+    iota(T.NR[:], [[8, NN]], 0, 1, "NR0 NR1", NN, False)
+    dma("y", "dpv", [(T.PVI[0:8, :], T.pv[:])], "", "PVI", 0.0)
+    dma("s", "dka", [(T.KI[:], T.ka[:])], "", "KI", 0.0)
+    dma("y", "dx", [(T.X[:], T.xa[:])], "", "X", 0.1)
+    dma("y", "dn0", [(T.NR[16 * a + 8:16 * a + 16, :], T.nm[8 * a:8 * a + 8, :]) for a in range(4)], "", "NR0", 3.0)
+    dma("y", "dn1", [(T.NR[16 * a + 8:16 * a + 16, :], T.nm[8 * a:8 * a + 8, :]) for a in range(4, 8)], "", "NR1", 3.0)
+    iota(T.CI[:, 0:1], [[0, 1]], 0, 1, "CI0", 1, False)
+    iota(T.IO[:], [[1, 392]], 0, 0, "IO", 392)
+    iota(T.GB[:], [[0, 2], [16, 8], [0, 16]], 0, 0, "GB", 256)
+    dma("g", "ds0", [(T.S[:], T.s0[:])], "", "S", 12.0, 1400)
+    iota(T.UBI[:], [[256, 12]], 0, 0, "UBI", 12)
+    iota(T.UN[:], [[-1, 2], [-2, LN]], 192, 0, "UN", NN)
+    fill(T.RST[:], 4096, "RST", 1536)
+    fill(T.RS8[:], 1, "RS8", 512)
+    fill(T.RSZ[:], 1, "RSZ", LN)
+    for i, mask in enumerate((15, 112, 16, 31)):
+        ts(T.CI[:, i + 1:i + 2], T.CI[:, 0:1], mask, None, OP.bitwise_and, None, "CI0", "CI%d" % (i + 1), 1)
+    cp(T.CF[:], T.CI[:], names("CI", 5), "CF", 5)
+    act(T.ONES[:], T.IO[:, 0:LN], AF.Sigmoid, "IO", "ONES", at=1.0, bias=30.0, scale=0.0, c=1520)
+    for c, src, x, o, w in ((LO, KC, 8.0, OP.is_lt, "LO"), (HI, KC, 8.0, OP.is_ge, "HI"), (L4, KC, 4.0, OP.is_lt, "L4"),
+                            (H0, HC, 0.0, OP.is_equal, "H0"), (H1, HC, 16.0, OP.is_equal, "H1")):
+        ts(c, src, x, None, o, None, "CF", w, 1)
+    ts(T.EQ[:], T.IO[:, 0:16], KC, None, OP.is_equal, None, "IO CF", "EQ", 16)
+    ts(CC, GC, LO, -1.0, OP.mult, OP.mult, "CF LO", "CC", 1)
+    ts(M4, KC, 12.0, HI, OP.is_lt, OP.mult, "CF HI", "M4", 1)
+    ts(R1, LO, L4, 2048.0, OP.subtract, OP.mult, "LO L4", "R1", 1)
+    for c, src, x, y, r, w in ((B8C, T.CF[:, 4:5], 16.0, 15.0, "CF", "B8C"),
+                               (VS_, HI, -2 * BIG, BIG, "HI", "VS_"), (VB, HI, 897 * BIG, -193 * BIG, "HI", "VB"),
+                               (R0, HI, 2752.0, 0.0, "HI", "R0"), (K16, KC, 16.0, 0.0, "CF", "K16"), (G15, GC, 1.0, 15.0, "CF", "G15"),
+                               (R2, LO, BIG - 2048, 2048.0, "LO", "R2"), (DL, HI, 4289.0, -193.0, "HI", "DL"),
+                               (DN, HI, -198144.0, 131072.0, "HI", "DN"), (D0, KC, -1024.0, 7168.0 + 192.0, "CF", "D0"),
+                               (D1, T.EQ[:, 8:9], 2293760.0, 0.0, "EQ", "D1"), (DC, D0, LO, D1, "D0 D1 LO", "DC"),
+                               (LS, LO, 1 / BIG, 0.0, "LO", "LS"), (LB, LO, BIG, 0.0, "LO", "LB"), (M4, M4, -1 / BIG, 0.0, "M4", "M4"),
+                               (L4, L4, -2.0, 0.0, "L4", "L4")):
+        lin(c, src, x, y, r, w)
+    ts(T.B8[:], T.IO[:, 0:144], B8C, None, OP.is_equal, None, "IO B8C", "B8", 144)
+    ts(T.BLK[:], T.GB[:, 0:128], GC, None, OP.is_equal, None, "GB CF", "BLK", 128)
+    for h in range(2):
+        ts(T.PH[:, 128 * h:128 * h + 128], T.IO[:, 0:128], PC, None, OP.is_equal, None, "IO CF", "PH%d" % h, 128)
+    lin(T.PW[:], T.PH[:], 1.0, 0.0, "PH0 PH1", "PW", 256, 1, "s")
+    for j in range(16):
+        lin(sel(j), T.BLK[:], T.EQ[:, j:j + 1], 0.0, "BLK EQ", "SEL%d" % j, 128, 0.5, "vs"[j // 8])
+    lin(sel(16), sel(0), -1.0, 0.0, "SEL0", "SEL16", 128, 0.5)
+    cp(T.PV16[0:8, :], T.PVI[0:8, :], "PVI", "PV16", NN)
     for par in range(2):
-        act(T.UN[:, LN * par:LN * par + LN], T.IO[:, par::2], AF.Identity, "IO", "UN%d" % par, bias=24576.0, scale=-128.0)
-    act(T.pD0[:, 0:NN], T.IO8[:], AF.Identity, "IO8 LO CC", "pD0", bias=CC, scale=LO)
-
-    def sel(a, b):
-        for j in range(a, b):
-            ts(T.SEL[:, 128 * j:128 * j + 128], T.BLK[:], T.EQ[:, j:j + 1], None, OP.mult, None, "BLK EQ", "SEL%d" % j)
-    sel(0, 4)
-    cp(T.PV16[0:8, :], T.PVI[0:8, :], "PVI", "PV16")
+        mm([(T.pa[:, 12 * par:12 * par + 12], [(T.B8[0:8, 15 - p:143 - p], T.PV16[0:8, 2 * p + par::32]) for p in range(16)])], "B8 PV16", "pa", 12)
+        cp(T.QA[:, 24 * par:24 * par + 12], T.pa[:, 12 * par:12 * par + 12], "pa", "QA%d" % par)
+    ts(KAw, T.KI[:], 1.0, None, OP.add, None, "KI", "KA", NN)
+    dma("y", "dsp", [(T.KI[32 * i:32 * i + 8, :], T.sp[:, NN * i:NN * i + NN]) for i in range(3)], "", "KI", None)
+    ts(T.SP16[0:72, :], T.KI[0:72, :], 512.0, None, OP.add, None, "KI", "SP16", NN)
+    ts(NMw, T.NR[:], CC, 65536.0, OP.add, OP.add, "CC NR0 NR1", "NM", NN)
     for par in range(2):
-        mm(T.pN[:, 12 * par:12 * par + 12], [(T.B8[0:8, 15 - p:143 - p], T.PV16[0:8, 2 * p + par::32]) for p in range(16)], "B8 PV16", "pN")
-    ts(T.KA[:], T.KI[:], 1.0, None, OP.add, None, "KI", "KA")
-    for k in range(8):
-        act(T.XU[:, k:1536:8], T.X[:, 0::2], AF.Copy, "X", "XU0_%d" % k)
-    ts(rw(0), T.PH[:, 0:128], LO, None, OP.mult, None, "PH0 LO", "RW0")
-    ts(rw(1), T.PH[:, 120:248], LO, None, OP.mult, None, "PH0 PH1 LO", "RW1")
-    ku(0)
-    tt(T.NM[:], T.pD0[:, 0:NN], T.NR[:], OP.add, "pD0 NR0 NR1", "NM")
+        for k in range(8):
+            lin(two(T.XU, par, k, 1536, 8, 1536), T.X[:, par::2], 1.0, 0.0, "X", "XU%d_%d" % (par, k), LN, 0.5, "vg"[par], pool=True)
+    lin(rw(0), IH, LO, 0.0, "PH0 LO", "RW0", 128, 0.5)
+    lin(rw(1), T.PH[:, 120:248], LO, 0.0, "PH0 PH1 LO", "RW1", 128, 0.5)
+    for i, a in enumerate((8, 0)):
+        lin(rw(2 + i), T.PH[:, a:a + 128], HI, 0.0, "PH0 PH1 HI", "RW%d" % (2 + i), 128, 0.5)
+        lin(T.RF[:, 128 * i:128 * i + 128], T.PH[:, a:a + 128], HI, 0.0, "PH0 PH1 HI", "RF%d" % i, 128, 1, "s")
+    ms(T.UB[:], 0.0, "UB", 72)
     for par in range(2):
-        cp(T.QU[:, 36 * par:36 * par + 12], T.pN[:, 12 * par:12 * par + 12], "pN", "QU%d" % par)
-    cp(T.VF[:], T.pN[:, 0:24], "pN", "VF")
-    kv(0)
-    nv(0)
-    sel(4, 16)
-    ts(T.PW[:, 0:128], T.IO[:, 0:128], PC, None, OP.is_equal, None, "IO CF", "PW0")
-    ts(T.PW[:, 128:256], T.IO[:, 0:128], PC, None, OP.is_equal, None, "IO CF", "PW1")
-    eu(0)
-    mm(T.pM[:, 480:504], [(ROT, T.VF[:])], "PW0 PW1 VF", "pM")
-    eu2(0)
-    match(0, 16)
-    kp(0)
-    cp(T.VS[:, 0:24], T.pM[:, 480:504], "pM", "VS0 VS1")
-    send("v", 0, T.VS[:, 0:12], "VS0")
-    send("v", 1, T.VS[:, 12:24], "VS1")
-    iota(T.TJ[:], [[0, 128]], 1048576, 0, names("TJ", 8))
-    iota(T.TC[:, NN:512], [[0, 128]], 0, 0, "TC8")
-    for k in range(8):
-        gcopy(T.XU[:, 1536 + k:W:8], T.X[:, 1::2], LN, "X", "XU1_%d" % k)
-    iota(T.RS8[:], [[0, 768]], 1, 0, "RS8")
-    for par in range(2):
-        cp(T.QI[:, 48 * par:48 * par + 12], T.VF[:, 12 * par:12 * par + 12], "VF", "QI%d" % par)
-    counts(0)
-    match_rest(0)
-    spares(0, 12)
-    spares2(0, 12)
-    ts(H0, HC, 0.0, None, OP.is_equal, None, "CF", "H0")
-    ts(H1, HC, 16.0, None, OP.is_equal, None, "CF", "H1")
-    ts(T.EQN[:], T.EQ[:], -1.0, None, OP.mult, None, "EQ", "EQN")
-    ts(R0, KC, 4.0, 2048.0, OP.is_lt, OP.mult, "CF", "R0")
-    ts(R2, HI, 2048.0, None, OP.mult, None, "HI", "R2")
-    ts(R1, LO, 2048.0, R0, OP.mult, OP.subtract, "LO R0", "R1")
-    ts(T.EQB[:, 0:4], T.EQ[:, 0:4], -1856.0, R0, OP.mult, OP.add, "EQ R0", "EQBa")
-    ts(T.EQB[:, 8:16], T.EQ[:, 8:16], -1856.0, R2, OP.mult, OP.add, "EQ R2", "EQBc")
-    ts(T.EQB[:, 4:8], T.EQ[:, 4:8], -1856.0, R1, OP.mult, OP.add, "EQ R1", "EQBb")
-    for i, c in enumerate((1536.0, -193.0, -67072.0, -1.0, 16.0, 128.0)):
-        ts(T.DG[:, 128 * i:128 * i + 128], IH, c, None, OP.mult, None, "PH0", "DG%d" % i)
-    ts(G15, GC, 15.0, None, OP.add, None, "CF", "G15")
-    ts(DC, KC, -1024.0, 7168.0 - 262144.0, OP.mult, OP.add, "CF", "DC")
-    ts(K16, KC, 16.0, None, OP.mult, None, "CF", "K16")
-    ts(rw(2), T.PH[:, 8:136], HI, None, OP.mult, None, "PH0 PH1 HI", "RW2")
-    ts(rw(3), IH, HI, None, OP.mult, None, "PH0 HI", "RW3")
-    ts(rw(4), IH, LO, 1.0 / 128, OP.mult, OP.mult, "PH0 LO", "RW4")
-    ts(T.WU[:], IH, LO, 262144.0, OP.mult, OP.mult, "PH0 LO", "WU")
-    ts(T.BLK8[:], T.BLK[:], R0, -1.0 / 512, OP.mult, OP.mult, "BLK R0", "BLK8")
-    ms(T.RSZ[:], 1.0, "RSZ")
-    ts(T.CE[:], T.IO[:, 0:144], G15, 8192.0, OP.is_equal, OP.mult, "IO G15", "CE")
-    ts(T.CS[:], T.IO[:, 0:144], G15, 131072.0, OP.is_equal, OP.mult, "IO G15", "CS")
-    ms(T.RSZ[:, 0::16], 0.0, "RSZ")
-    ts(T.DGC[:], IH, DC, LO, OP.mult, OP.mult, "PH0 DC LO", "DGC")
-    su(0)
-    ms(T.RST[:, 0::8], 1.0e9, "RST")
-    v8(0)
-    act(T.MM[:, 0:128], IDN, AF.Identity, "PW0 H0", "MM0", scale=H0)
-    act(T.MM[:, 128:256], ROT, AF.Identity, "PW0 PW1 H0", "MM1", scale=H0)
-    act(T.MM[:, 256:384], UNR, AF.Identity, "PW0 PW1 H1", "MM2", scale=H1)
-    act(T.MM[:, 384:512], IDN, AF.Identity, "PW0 H1", "MM3", scale=H1)
-    zmm(0)
-    lowest(0)
-    zmm2(0)
-    alt(0, 12)
+        ms(T.UB[:, 36 * par:36 * par + 12], float(NN), "UB", 12)
+        ts(T.UB[:, 36 * par + 24:36 * par + 36], T.UBI[:], K16, 8.0 * par, OP.add, OP.add, "UBI K16", "UB")
+    for s in range(2):
+        ts(T.QA[:, 24 * s + 12:24 * s + 24], T.QA[:, 24 * s:24 * s + 12], 3, None, OP.bitwise_and, None, "QA%d" % s, "QB%d" % s)
+        lists(s, 12, 36, T.QA[:, 24 * s:24 * s + 24], "QA%d QB%d" % (s, s), 10.0 + 18 * s)
+    lin(T.EQN[:], T.EQ[:], -1.0, 0.0, "EQ", "EQN", 16)
+    lin(T.EQB[:, 0:4], T.EQ[:, 8:12], -1856.0, R0, "EQ R0", "EQBa", 4)
+    lin(T.EQB[:, 4:8], T.EQ[:, 4:8], -1852.0, R1, "EQ R1", "EQBb", 4)
+    lin(T.EQB[:, 16:24], T.EQ[:, 0:8], -BIG, R2, "EQ R2", "EQBd", 8)
+    lin(T.EQB[:, 8:16], T.EQ[:, 8:16], -1856.0, 0.0, "EQ", "EQBc", 8)
+    tt(T.EQB[:, 8:16], T.EQB[:, 8:16], T.EQB[:, 16:24], OP.add, "EQBc EQBd", "EQBc", 8, 2)
+    for i, (c, r) in enumerate(((1536.0, ""), (-193.0, ""), (DN, "DN"), (1 / 4096, ""), (LS, "LS"), (DC, "DC"), (LB, "LB"), (M4, "M4 PH1"), (DL, "DL"))):
+        lin(dg(i), T.PH[:, 8:136] if i == 7 else IH, c, 0.0, "PH0 " + r, "DG%d" % i, 128, 0.5)
+    ts(T.BR[:], T.GB[:, 112:240], GC, L4, OP.is_equal, OP.mult, "GB CF L4", "BR", 128)
+    ms(T.RSZ[:, 0::16], 0.0, "RSZ", 12)
+    ts(T.CE[:], T.IO[:, 0:144], G15, 8192.0, OP.is_equal, OP.mult, "IO G15", "CE", 144)
+    lin(T.CS[:], T.CE[:], 16.0, 0.0, "CE", "CS", 144, 0.5)
+    ms(T.RST[:, 0::8], 1.0e12, "RST", LN, 0.5)
+    ms(T.RS8[:, 0::8], 0.0, "RS8", 64, 0.5)
+    for i, (a, c, r) in enumerate(((0, H0, "H0"), (112, H0, "H0"), (16, H1, "H1"), (0, H1, "H1"))):
+        lin(T.MM[:, 128 * i:128 * i + 128], T.PH[:, a:a + 128], c, 0.0, "PH0 PH1 " + r, "MM%d" % i, 128, 0.5)
     for r in range(4):
-        act(T.TA[:, r::4], T.IO[:, r::4], AF.Identity, "IO EQN EQBa", "TA%d" % r, bias=T.EQB[:, r:r + 1], scale=T.EQN[:, r:r + 1])
+        lin(T.pU[:, r:NN:4], T.IO[:, r:NN:4], T.EQN[:, 8 + r:9 + r], T.EQB[:, r:r + 1], "IO EQN EQBa", "pU", 96, 1, "s")
+    tt(T.KL[:], T.pU[:, 0:NN], KAw, OP.max, "pU KA", "KL", NN)
     for r in range(4):
-        act(T.TB[:, r::4], T.IO[:, r::4], AF.Identity, "IO EQN EQBb", "TB%d" % r, bias=T.EQB[:, 4 + r:5 + r], scale=T.EQN[:, 4 + r:5 + r])
+        lin(T.TB[:, r::4], T.IO[:, r::4], T.EQN[:, 4 + r:5 + r], T.EQB[:, 4 + r:5 + r], "IO EQN EQBb", "TB%d" % r, 98, 1, "s")
     for r in range(8):
-        act(T.TC[:, r:NN:8], T.IO[:, r::8], AF.Identity, "IO EQN EQBc", "TC%d" % r, bias=T.EQB[:, 8 + r:9 + r], scale=T.EQN[:, 8 + r:9 + r])
-    act(T.TC[:, 512:896], T.IO[:], AF.Identity, "IO R2", "TC9", bias=R2, scale=0.0)
-    for par in range(2):
-        ts(T.UB[:, 24 * par:24 * par + 24], T.UBI[:], K16, 8.0 * par, OP.add, OP.add, "UBI K16", "UB%d" % par)
-    lowest2(0)
-    for r in range(8):
-        ts(T.TJ[:, r::16], T.JV[:], T.EQ[:, 8 + r:9 + r], 1048576.0, OP.mult, OP.add, "JV EQ", "TJ%d" % r)
-    same(0)
-    weave(lambda: mchain(0), lambda: zchain(0), lambda: lists(0))
-    hg(0)
-    gab(0)
-    ml(0)
+        lin(T.TC[:, r:NN:8], T.IO[:, r:NN:8], T.EQN[:, 8 + r:9 + r], T.EQB[:, 8 + r:9 + r], "IO EQN EQBc", "TC%d" % r, 48, 1, "s")
+    ts(T.TC[:, NN::2], T.IO[:, 0:8], -7.0, HI, OP.add, OP.mult, "IO HI", "TC8", 8)
+    ms(T.TC[:, NN + 1::2], BIG, "TC9", 8)
+
+    def early(t):
+        low(t)
+        if t > 0:
+            rewrite(t - 1)
+        choose(t)
+        if t < 5:
+            rewrite_low(t)
+
+    def late(t):
+        high(t)
+        lowest(t)
+
+    early(0)
+    late(0)
+    ahead(0)
     h8(0)
-    h8r(0)
-    llo(0)
-    ms(T.RS8[:, 0::8], 0.0, "RS8")
-
+    early(1)
     for t in range(RO):
+        if t < 5:
+            late(t + 1)
+        if t < 4:
+            early(t + 2)
         products(t)
-        if t == 5:
-            break
-        if t == 0:
-            advance(0)
-        match_rest(t + 1)
-        zmm2(t + 1)
-        post(t)
-        if t == 0:
-            spares2(12, 72)
-            alt(12, 72)
-        lowest2(t + 1)
-        n = t + 1
-        if n < 5:
-            weave(lambda: mchain(n), lambda: lists(n))
-            hg(n)
-            gab(n)
-            llo(n)
-            weave(lambda: zchain(n), lambda: [ml(n), outp(t)])
-            advance(n)
-        else:
-            n5 = 5 * LN
-            llo(n)
-            weave(lambda: mchain(n), lambda: partners(0))
-            weave(lambda: zchain(n), lambda: [ml(n), outp(t)])
-            dma("y", "do0", [(T.yo[0:112, 0:n5], T.OB[16:128, 0:n5]), (T.yo[112:128, 0:n5], T.OB[0:16, 0:n5])],
-                " ".join("OB%d%s" % (i, x) for i in range(5) for x in "ab"), "")
-            own(t)
-            best(n)
-            ts(T.QI[:, 336:348], T.BI[:], 511, None, OP.bitwise_and, None, "BI", "QI7")
-            qu(7, 12)
-            partners(1)
-            dma("y", "dyp", [(T.yp[:], T.YP[0::16, :])], "YP0 YP1", "")
-        guest(t)
-    dma("s", "do1", [(T.yo[:, 5 * LN:6 * LN], T.OB[:, 5 * LN:6 * LN])], "TS5a TS5b", "")
+        if t < 5:
+            ahead(t + 1)
+            settle(t)
+        if t < 4:
+            h8(t + 1)
+    during(5)
+    n5 = 5 * LN
+    dma("y", "do0", [(T.yo[0:112, 0:n5], T.OB[16:128, 0:n5]), (T.yo[112:128, 0:n5], T.OB[0:16, 0:n5])],
+        " ".join("OB%d%s" % (i, x) for i in range(5) for x in "ab"), "", 0.0)
+    for par in range(2):
+        lin(T.YP[:, par::2], T.IO[:, 0:NN].indirect(vl(6 + par)), 1.0, 0.0, "IO QU%d" % (6 + par), "YP%d" % par, LN, "g", "s", 2.0)
+    dma("y", "dyp", [(T.yp[:], T.YP[0::16, :])], "YP0 YP1", "", 3.0)
 
     count = emit(g, T, ops)
     for s in sorted(count):

import numpy as np
from concourse.bass import DstId, RemoteDMATransfer
from concourse.mybir import dt, AluOpType, AxisListType, ActivationFunctionType

NN, LN, RO, W = 384, 192, 6, 3072
F32, F16, BF, I32, U16 = "float32", "float16", "bfloat16", "int32", "uint16"
PARTS = ((0, 64, "a"), (64, 128, "a"), (128, 192, "b"))
SPAN = {"a": (0, 128), "b": (128, 192)}
SCAN_FROM = (2, 2, 2, 2, 2, 1)
BIG = 262144.0
MESSAGES = [(k, t) for k in "vab" for t in range(RO - 1)]
DIRECT = "b"


def _sb(n, d, p=128):
    return ("sbuf", [p, n], d)


SCRATCH = {
    "KI": _sb(NN, I32), "KN": _sb(2 * NN, F32), "NR": _sb(NN, I32), "X": _sb(NN, BF), "S": _sb(W, F32),
    "PVI": _sb(NN, I32), "PV16": _sb(NN, F16), "SP16": _sb(NN, F16),
    "CI": _sb(5, I32), "CF": _sb(5, F32), "C2": _sb(24, F32), "IO": _sb(392, F32), "GB": _sb(256, F32),
    "UBI": _sb(12, F32), "UB": _sb(72, F32), "EQ": _sb(16, F32), "EQN": _sb(16, F32), "EQB": _sb(24, F32),
    "PW": _sb(256, F32), "PH": _sb(256, BF), "MM": _sb(512, BF), "BLK": _sb(128, BF), "BR": _sb(128, BF), "RF": _sb(256, F32),
    "SEL": _sb(2176, BF), "RW": _sb(512, BF), "CE": _sb(144, BF), "CS": _sb(144, BF), "DG": _sb(1152, BF),
    "ONES": _sb(LN, BF), "B8": _sb(144, F16), "TB": _sb(392, F32), "TC": _sb(400, F32),
    "RST": _sb(1536, BF), "RSZ": _sb(LN, BF), "RS8": _sb(512, BF), "XU": _sb(W, BF), "UN": _sb(NN, BF),
    "KL": _sb(NN, F32), "KV": _sb(2 * LN, BF), "KH": _sb(LN, BF), "KU": _sb(2 * LN, BF), "NV": _sb(LN, F16), "AL": _sb(1920, BF),
    "RL": _sb(2 * 1536, BF), "T2": _sb(LN, F32), "GT": _sb(2 * LN, BF), "GW": _sb(NN, BF),
    "A": _sb(1536, F32), "RR": _sb(1536, F32), "SG": _sb(2 * 1920, BF), "E": _sb(1536, BF), "KP": _sb(96, U16), "ML": _sb(RO * 288, U16),
    "MI": _sb(LN, I32), "MJ": _sb(LN, I32), "M16": _sb(LN, F16), "ZT": _sb(LN, F32), "ZR": _sb(LN, F32), "BI": _sb(12, I32),
    "QI": _sb(36, I32), "QH": _sb(36, F16), "QA": _sb(48, I32),
    "QF": _sb(8 * 36, F32), "QU": _sb(8 * 36, U16), "VS": _sb(5 * 24, F32), "GV": _sb(5 * 24, F32),
    "LG": _sb(5 * 24, U16), "T3": _sb(NN, F32), "HG": _sb(LN, F32), "H8": _sb(2 * LN, F32),
    "LLO": _sb(2 * 1536, F32), "LHI": _sb(1536, F32), "P": _sb(W, F32), "PS": _sb(1536, F32), "TS": _sb(5 * LN, F32), "TL": _sb(5 * LN, F32),
    "SL": _sb(LN, F32), "OB": _sb(RO * LN, F32), "YP": _sb(NN, F32),
    "pD0": ("psum", [128, 512], F32), "pD1": ("psum", [128, 512], F32), "pU": ("psum", [128, 512], F32), "pZ": ("psum", [128, 512], F32),
    "pR": ("psum", [128, 512], F32), "pa": ("psum", [128, 512], F32), "pb": ("psum", [128, 512], F32), "pN": ("psum", [128, 512], F32),
}
DSEMS = ["dka", "dpv", "dsp", "dx", "ds0", "dn0", "dn1", "do0", "doa", "dob", "dyp"] + ["dt%d" % t for t in range(RO - 1)]
SEMAPHORES = ["ev", "es", "et", "eg", "lsent"] + DSEMS + ["a%s%d" % m for m in MESSAGES]

OP = AluOpType
AF = ActivationFunctionType


def line(kind, t):
    return 2 if kind == "v" and t > 1 else 0 if kind in "vb" else 1


def route(T, topo, r, t, kind):
    src, dst = T.cores[r], T.cores[(r + 1 + t % 7) % len(T.cores)]
    if kind in DIRECT and topo.may_write(src, dst):
        return None, dst
    c = [k for k in topo.cores_of(src) if T.rank_of(k) is None and all(topo.may_write(k, x) for x in T.cores)]
    c.sort(key=lambda k: topo.die(k) != topo.die(src))
    return c[line(kind, t)], dst


def spot(kind, t):
    if kind in "ab":
        return LN * t + SPAN[kind][0], LN * t + SPAN[kind][1]
    return 24 * t, 24 * t + 24


def land(T, kind, t):
    a, b = spot(kind, t)
    return T.TL[:, a:b] if kind in "ab" else T.GV[:, a:b]


def relay_program(g, core, T, topo):
    total = 0
    for r in range(len(T.cores)):
        for kind, t in MESSAGES:
            via, dst = route(T, topo, r, t, kind)
            if via != core:
                continue
            sem = T.sem["a%s%d" % (kind, t)]
            g.wait_ge(sem, len(topo.engines(T.cores[r], core)))
            rid, pid = topo.addr(dst, core)
            g.remote_dma(land(T, kind, t), land(T, kind, t), sem, T.sem.lsent, pid, rid, topo.mask(core, dst))
            total += len(topo.engines(core, dst))
    if total:
        g.wait_ge(T.sem.lsent, total)


def hazards(ops, order_only):
    lastw, readers, out = {}, {}, []
    for i, o in enumerate(ops):
        d = set()
        for x in o["r"] + (o.get("after", []) if order_only else []):
            if x in lastw:
                d.add(lastw[x])
            if x[0] == "p":
                d.update(k for k in readers.get(x, []) if order_only or ops[k]["e"] != o["e"])
        for x in o["w"]:
            if x in lastw and (order_only or not (x[0] == "p" and o["e"] == "t" and ops[lastw[x]]["e"] == "t")):
                d.add(lastw[x])
            d.update(readers.get(x, []))
        d.discard(i)
        for x in o["r"]:
            readers.setdefault(x, []).append(i)
        for x in o["w"]:
            lastw[x] = i
            readers[x] = []
        out.append(d)
    return out


CASES = ((1.56, 3.8, 1.0, 150, 6500, 600, 1), (1.8, 4.5, 1.3, 250, 10000, 800, 1), (1.56, 3.8, 1.0, 150, 6500, 600, 2))
WEIGHTS, HOPE = (0.45, 0.15, 0.15), 200
CYCLE, FIXED, DMA, OPEN, ROUND = 0.83, {"v": 50, "s": 65, "t": 0, "g": 150, "y": 0}, 2300, 2400, 13.5
SEED, ROUNDS, REACH, PATIENCE, SWAP, KEPT = 11, 170000, 0.3, 0.8, 0.15, []
WINDOWS = ((0, 0.5, 0.3, 120), (0.3, 0.7, 0.1, 80), (0.5, 0.85, 0.1, 80), (0.65, 1, 0.1, 80), (0, 0.55, 0.2, 50), (0.35, 1, 0.2, 40))


def schedule(ops):
    if KEPT:
        _, order, eng = KEPT[0]
        return [dict(ops[i], e=eng[i], f=ops[i]["ways"][eng[i]][0]) if "ways" in ops[i] else ops[i] for i in order]
    n = len(ops)
    eng = [o["e"] for o in ops]
    lane = ["vstgy".index(e) for e in eng]
    kinds = [dict.fromkeys(d, "hop") for d in hazards(ops, True)]
    sends, prev = {}, {}
    for i, o in enumerate(ops):
        for k in kinds[i]:
            if ops[k].get("dma"):
                kinds[i][k] = DMA * {"ds0": 2.5, "dsp": 1.6, "dn0": 1.3, "dn1": 1.3}.get(ops[k]["dma"], 1)
            elif eng[k] == "t" and eng[i] == "t":
                kinds[i][k] = 0
        if "msg" in o:
            sends[o["msg"]] = i
            if o["line"] in prev:
                kinds[i][prev[o["line"]]] = 0
            o["opens"] = o["line"] not in prev
            prev[o["line"]] = i
        if "behind" in o:
            kinds[i][[k for k, x in enumerate(ops) if x["w"] == ["PS"]][o["behind"]]] = 0
        for s, _ in o.get("wait", []):
            kinds[i][sends[s]] = "open" if ops[sends[s]]["opens"] else "way"

    def price(i, e, case):
        o = ops[i]
        k = o["ways"][e][1] if "ways" in o else o["k"]
        if "c" in o:
            return o["c"] + (case[5] if "msg" in o else 0)
        return case[2] * (FIXED[e] + CYCLE * o["n"] * {"g": case[0], "s": case[1]}.get(k, k)) * (case[6] if e == "t" else 1)

    def shift(i, e):
        eng[i], lane[i] = e, "vstgy".index(e)
        for co, case in zip(costs, CASES):
            co[i] = price(i, e, case)

    costs = [[price(i, eng[i], case) for i in range(n)] for case in CASES]
    backs = [[[(k, {"hop": case[3], "way": case[4], "open": case[4] + OPEN}.get(x, x)) for k, x in d.items()] for d in kinds] for case in CASES]
    ahead = [[[] for _ in ops] for _ in CASES]
    for us, ba in zip(ahead, backs):
        for i in range(n):
            for k, lat in ba[i]:
                us[k].append((i, lat))
    tail = [DMA if o.get("dma") else 0 for o in ops]
    key = [0.0] * n
    for i in reversed(range(n)):
        key[i] = ops[i]["at"] if ops[i]["at"] is not None else min(key[u] for u, _ in ahead[0][i]) - costs[0][i] / 1000 - 0.15
    cur = dispatch(lane, ahead[0], [len(d) for d in kinds], costs[0], key)

    def onward(order, z):
        out = []
        for co, us in zip(costs, ahead):
            free, way = [0.0] * 5, {}
            for i in reversed(order[z:]):
                way[i] = free[lane[i]] = co[i] + max([free[lane[i]], tail[i]] + [lat + way[k] for k, lat in us[i]])
            rest = [(i, max([tail[i]] + [lat + way[k] for k, lat in us[i] if k in way])) for i in order[:z]]
            out.append(([x for x in rest if x[1]], free))
        return out

    def replay(order, a, z, on, old=None, bar=1e18):
        total, held, part, before = 0.0, [], order[a:z], {lane[i]: i for i in order[max(0, a - 100):a]}
        for c, w in enumerate(WEIGHTS):
            co, ba = costs[c], backs[c]
            fin, by = ([0.0] * n, [-1] * n) if old is None else (old[c][1][:], old[c][2][:])
            last = [before.get(e, -1) for e in range(5)]
            free = [fin[i] if i >= 0 else 0.0 for i in last]
            for i in part:
                e = lane[i]
                t, b = free[e], last[e]
                for k, lat in ba[i]:
                    x = fin[k] + lat
                    if x > t:
                        t, b = x, k
                fin[i] = free[e] = t + co[i]
                by[i], last[e] = b, i
            end, i = max([(fin[i] + x, i) for i, x in on[c][0]] + [(free[e] + x, last[e]) for e, x in enumerate(on[c][1]) if last[e] >= 0])
            total += w * end
            held.append((i, fin, by, end))
            if old and total + sum(x * (y[3] - HOPE) for x, y in zip(WEIGHTS[c + 1:], old[c + 1:])) > bar:
                return 1e18, None
        return total, held

    def moved(part, up):
        if up:
            need = {part[-1]}
            for k in reversed(part):
                if k in need:
                    need.update(kinds[k])
        else:
            need = {part[0]}
            for k in part:
                if not need.isdisjoint(kinds[k]):
                    need.add(k)
        if part[0] in need and part[-1] in need:
            return None
        return [k for k in part if (k in need) == up] + [k for k in part if (k in need) != up]

    rng = np.random.default_rng(SEED)
    for y, z, share, ease in WINDOWS:
        y, z, rounds = int(y * n), int(z * n), int(share * ROUNDS)
        on, inside = onward(cur, z), set(cur[y:z])
        val, held = replay(cur, 0, z, on)
        best = (val, cur, eng[:])
        for it, (r0, r1, r2, r3, r4) in enumerate(rng.random((rounds, 5)).tolist()):
            i, _, by, _ = held[int(r0 * len(CASES))]
            pairs = []
            while i in inside:
                j = by[i]
                if j in inside and j not in kinds[i]:
                    pairs.append((i, j))
                i = j
            if not pairs:
                continue
            i, j = pairs[int(r1 * len(pairs))]
            a, b, was, new = cur.index(j), cur.index(i), eng[j], cur
            if r2 > 1 - SWAP and "ways" in ops[j]:
                others = [e for e in ops[j]["ways"] if e != was]
                shift(j, others[int(r3 * len(others))])
            else:
                far, step = int(np.log(r2 + 1e-12) / np.log(1 - REACH)), -1 if r3 < 0.5 else 1
                p = a if step < 0 else b
                while far and y <= p + step < z:
                    p += step
                    if lane[cur[p]] == lane[i]:
                        far -= 1
                        a, b = min(a, p), max(b, p)
                part = moved(cur[a:b + 1], step < 0)
                if part is None:
                    continue
                new = cur[:a] + part + cur[b + 1:]
            bar = val - ease * (1 - it / rounds) * float(np.log(r4 + 1e-12))
            v, h = replay(new, a, z, on, held, bar)
            if v <= bar:
                cur, val, held = new, v, h
                if v < best[0]:
                    best = (v, new, eng[:])
            elif eng[j] != was:
                shift(j, was)
        cur = best[1]
        for i, e in enumerate(best[2]):
            shift(i, e)
    KEPT.append(best)
    return schedule(ops)


def dispatch(lane, users, left, cost, key):
    ready, free, begun = [0.0] * len(lane), [0.0] * 5, []
    pool = [[i for i in range(len(lane)) if lane[i] == e and not left[i]] for e in range(5)]
    for _ in lane:
        soon, e = min((max(ready[i], free[e]) + cost[i], e) for e in range(5) for i in pool[e])
        first = min(max(ready[i], free[e]) for i in pool[e])
        i = min((i for i in pool[e] if max(ready[i], free[e]) <= first + PATIENCE * (soon - first)), key=lambda k: key[k])
        pool[e].remove(i)
        begun.append((max(ready[i], free[e]), len(begun), i))
        free[e] = begun[-1][0] + cost[i]
        for u, lat in users[i]:
            ready[u] = max(ready[u], free[e] + lat)
            left[u] -= 1
            if not left[u]:
                pool[lane[u]].append(u)
    return [i for _, _, i in sorted(begun)]


def emit(g, T, ops):
    queue = {"v": g.vector, "s": g.scalar, "t": g.tensor, "g": g, "y": g.sync}
    ops = schedule(ops)
    deps, need = [], set()
    for d in hazards(ops, False):
        last = {}
        for k in d:
            key = ops[k].get("dma") or ops[k]["e"]
            last[key] = max(last.get(key, -1), k)
        deps.append(sorted(last.values()))
        need.update(last.values())
    count, mark, clock = {}, {}, {}
    seen = {e: {} for e in queue}
    for i, o in enumerate(ops):
        e = o["e"]
        for k in reversed(deps[i]):
            s, n = mark[k]
            if seen[e].get(s, 0) < n:
                queue[e].wait_ge(T.sem[s], n)
                seen[e][s] = n
                for s2, n2 in clock[k].items():
                    seen[e][s2] = max(seen[e].get(s2, 0), n2)
        for s, n in o.get("wait", []):
            queue[e].wait_ge(T.sem[s], n)
        clock[i] = dict(seen[e])
        res = o["f"](queue[e])
        if o.get("dma"):
            for ins in res:
                ins.then_inc(T.sem[o["dma"]], 16)
            count[o["dma"]] = 16 * len(res)
            mark[i] = (o["dma"], 16 * len(res))
        elif i in need:
            s = "e" + e
            res.then_inc(T.sem[s], 1)
            count[s] = count.get(s, 0) + 1
            mark[i] = (s, count[s])
    return count


def rank_program(g, core, T, topo):
    rank = T.rank_of(core)
    if rank is None:
        relay_program(g, core, T, topo)
        return
    nr = len(T.cores)
    ops = []
    sent = [0]
    base = [0.0]

    def add(e, f, r, w, n=12, k=1, at=None, **more):
        ops.append(dict(e=e, f=f, r=r.split(), w=w.split(), n=n, k=k, at=None if at is None else at + base[0], **more))

    def during(round_):
        base[0] = ROUND * round_

    def ts(out, in0, s1, s2, o0, o1, r, w, n=12, k=1, **more):
        if o1 is None:
            add("v", lambda q: q.tensor_scalar(out, in0, s1, None, o0), r, w, n, k, **more)
        else:
            add("v", lambda q: q.tensor_scalar(out, in0, s1, s2, o0, o1), r, w, n, k, **more)

    def tt(out, a, b, o, r, w, n=LN, k=1, at=None):
        add("v", lambda q: q.tensor_tensor(out, a, b, o), r, w, n, k, at)

    def cp(out, a, r, w, n=12, at=None):
        add("v", lambda q: q.tensor_copy(out, a), r, w, n, 1, at)

    def ms(out, c, w, n, k=1):
        add("v", lambda q: q.memset(out, c), "", w, n, k)

    def scan(out, d0, d1, o0, o1, r, w, n, k, at):
        add("v", lambda q: q.tensor_tensor_scan(out, d0, d1, 0.0, o0, o1), r, w, n, k, at)

    def act(out, a, f, r, w, n=LN, k=1, at=None, bias=0.0, scale=1.0, **more):
        add("s", lambda q: q.activation(out, a, f, bias=bias, scale=scale), r, w, n, k, at, **more)

    def lin(out, a, scale, bias, r, w, n=1, k=1, on="s", at=None, pool=False):
        ways = {"v": (lambda q: q.tensor_scalar(out, a, scale, bias, OP.mult, OP.add), k),
                "s": (lambda q: q.activation(out, a, AF.Identity, bias=bias, scale=scale), k if k == "g" else 1)}
        if pool:
            ways["g"] = (lambda q: q.affine_select(out, a, [[0, n]], OP.is_gt, 0.0, 1, 0), 2)
        add(on, ways[on][0], r, w, n, ways[on][1], at, ways=ways)

    def sign(out, a, r, w, n, at):
        ways = {"v": (lambda q: q.tensor_scalar(out, a, -1.0, 1.0, OP.add, OP.min), 0.5),
                "s": (lambda q: q.activation(out, a, AF.Sign, bias=-1.0, scale=1.0), 1)}
        add("s", ways["s"][0], r, w, n, 1, at, ways=ways)

    def fill(out, c, w, n):
        ways = {"v": (lambda q: q.memset(out, float(c)), 0.5),
                "g": (lambda q: q.iota(out, [[0, n]], c, 0, allow_small_or_imprecise_dtypes=True), 2)}
        add("g", ways["g"][0], "", w, n, 2, ways=ways)

    def mm(groups, r, w, n=LN, at=None, start=True, stop=True):
        def f(q):
            for out, terms in groups:
                for i, x in enumerate(terms):
                    ins = q.matmul(out, x[0], x[1], start and i == 0, stop and i == len(terms) - 1)
            return ins
        add("t", f, r, w, max(n, 64) * sum(x[-1] if len(x) > 2 else 1 for _, terms in groups for x in terms), 0.5, at)

    def iota(out, pat, base_, cm, w, n, flt=True):
        if flt:
            add("g", lambda q: q.iota(out, pat, base_, cm, allow_small_or_imprecise_dtypes=True), "", w, n, 2)
        else:
            add("g", lambda q: q.iota(out, pat, base_, cm), "", w, n, 2)

    def dma(e, sem, pairs, r, w, at, c=100):
        add(e, lambda q: [q.dma_start(a, b) for a, b in pairs], r, w, at=at, dma=sem, c=c * len(pairs))

    def send(kind, t, buf, r, at):
        via, dst = route(T, topo, rank, t, kind)
        to = dst if via is None else via
        rid, pid = topo.addr(to, core)
        a, b = spot(kind, t)
        sent[0] += len(topo.engines(core, to))
        add("g", lambda q: q.remote_dma(land(T, kind, t), buf[:, a:b], T.sem["a%s%d" % (kind, t)], T.sem.lsent, pid, rid, topo.mask(core, to)),
            r, "", at=at, msg="a%s%d" % (kind, t), line=line(kind, t), c=OPEN if (kind, t) == MESSAGES[0] else 0)

    def arrival(kind, t):
        s = (rank - 1 - t % 7) % nr
        via, dst = route(T, topo, s, t, kind)
        return [("a%s%d" % (kind, t), len(topo.engines(T.cores[s] if via is None else via, core)))]

    def names(p, n, a=0):
        return " ".join("%s%d" % (p, i) for i in range(a, n))

    def two(buf, t, a=0, b=LN, c=1, n=LN):
        return buf[:, n * (t % 2) + a:n * (t % 2) + b:c]

    col = lambda i: T.C2[:, i:i + 1]
    PC, KC, GC, HC = T.CF[:, 0:1], T.CF[:, 1:2], T.CF[:, 2:3], T.CF[:, 3:4]
    LO, HI, H0, H1, CC, B8C, G15, DC, K16, R0, R1, R2, DN, L4, M4, DL, VS_, VB, D0, D1, LS, LB = [col(i) for i in range(22)]
    IDN, ROT = T.PW[:, 0:128], T.PW[:, 112:240]
    IH = T.PH[:, 0:128]
    rw = lambda i: T.RW[:, 128 * i:128 * i + 128]
    dg = lambda i: T.DG[:, 128 * i:128 * i + 128]
    sel = lambda j: T.SEL[:, 128 * j:128 * j + 128]
    Sw, KAw, NMw = T.S[:, 0:W], T.KN[:, 0:NN], T.KN[:, NN:2 * NN]
    vl = lambda s: T.QU[:, 36 * s + 12:36 * s + 24]
    ol = lambda s: T.QU[:, 36 * s + 24:36 * s + 36]
    sg = lambda t, a, b, c=1: two(T.SG, t, a, b, c, 1920)
    GJ, GU = T.GW[:, 0:LN], T.GW[:, LN:NN]

    def differ(t, b, hi, at):
        bank, a, par = "pD%d" % ((b + hi + t) % 2), 64 * b, t % 2
        groups = []
        for pos in range(8):
            j = 8 * hi + 7 - pos
            terms = [(sel(j), T.KH[:, a:a + 64] if hi else two(T.KV, t, a, a + 64)), (IH, two(T.KU, t, a, a + 64))]
            groups.append((T[bank][:, pos::8], terms + ([(sel(j), T.NV[:, a:a + 64])] if hi else [])))
        mm(groups, names("SEL", 8 * hi + 8, 8 * hi) + " PH0 KU%d " % par + ("KH NV" if hi else "KV%d" % par), bank, 64, at)
        if hi:
            act(T.A[:, 8 * a:8 * a + 512], T[bank][:], AF.Abs, bank, "A%d" % b, 512, 1, at + 0.8, bias=1536.0 + 4096.0)
        else:
            act(T.AL[:, 8 * a:8 * a + 512], T[bank][:], AF.Abs, bank, "AL%d" % b, 512, 1, at + 0.6, scale=4096.0)

    def low(t):
        par, n, bank = t % 2, NN if t < 5 else LN, "pD%d" % ((t + 1) % 2)
        during(t - 2)
        lin(two(T.KV, t), T.KL[:, 0:NN].indirect(vl(t)), VS_, VB, "KL VS_ VB QU%d" % t, "KV%d" % par, LN, "g", "s", 9.3)
        lin(two(T.KU, t), T.KN[:, par:NN:2], -BIG, 193 * BIG, "KA", "KU%d" % par, LN, 1, "s", 3.3)
        mm([(T.pU[:, 400:496], [(rw(0), two(T.KV, t, 0, LN, 2)), (rw(1), two(T.KV, t, 1, LN, 2))])], "RW0 RW1 KV%d" % par, "pU", 96, 9.8)
        ts(T.KP[:], T.pU[:, 400:496], 1 / BIG, 192.0, OP.mult, OP.add, "pU", "KP", 96, at=13.0)
        for b in range(3):
            differ(t, b, 0, 10.0 + 0.6 * b)
        groups = [(T[bank][:, 0:LN], [(IH, two(T.KV, t)), (dg(6), two(T.UN, t))])]
        if t < 5:
            groups.append((T[bank][:, LN:NN], [(rw(2), two(T.KV, t)), (IH, two(T.KU, t))]))
        mm(groups, "PH0 RW2 DG6 KV%d KU%d UN" % (par, par), bank, LN, 11.8)
        act(T.AL[:, 1536:1536 + n], T[bank][:, 0:n], AF.Abs, bank, "AL3", n, 1, 12.3)
        during(t - 1)
        tt(T.E[:], T.X[:, 0:NN].indirect(T.KP[:]), two(T.XU, t, 0, 1536, 1, 1536), OP.is_equal, "X KP " + names("XU%d_" % par, 8), "E", 1536, "g", 5.4)
        sign(sg(t, 0, 1024), T.AL[:, 0:1024], "AL0 AL1", "SG%da" % par, 1024, 3.5)
        sign(sg(t, 1024, 1536 + n), T.AL[:, 1024:1536 + n], "AL2 AL3", "SG%db" % par, 512 + n, 4.9)
        scan(two(T.RL, t, 0, 1536, 1, 1536), T.RST[:], T.AL[:, 0:1536], OP.add, OP.min, "RST " + names("AL", 3), "RL%d" % par, 1536, 0.5, 7.5)

    def high(t):
        during(t - 1 if t else -1.6)
        lin(T.KH[:], KAw.indirect(vl(t)), BIG, -193 * BIG, "KA QU%d" % t, "KH", LN, "g", "s", 3.0)
        ts(T.NV[:], NMw.indirect(vl(t)), -67072.0, None, OP.add, None, "NM QU%d" % t, "NV", LN, "g", at=5.1)
        for b in range(3):
            differ(t, b, 1, 5.7 + 0.65 * b)

    def choose(t):
        par, s, row = t % 2, t + 2, 32 * (t // 2)
        during(t - 1)
        terms = [(T.CS[:, 8 + pos:136 + pos], sg(t, pos, 1536, 8)) for pos in range(8)] + [(dg(6), sg(t, 1536, 1728))]
        terms += [(dg(4), two(T.KV, t)), (dg(5), T.ONES[:]), (T.B8[row:row + 8, 7:135], T.SP16[row:row + 8, LN * par:LN * par + LN])]
        mm([(T.pZ[:, 0:LN], terms)], "CS DG6 SG%da SG%db DG4 KV%d DG5 ONES B8 SP16" % (par, par, par), "pZ", LN, 7.6, stop=False)
        mm([(T.pZ[:, 0:LN], [(T.CE[:, 15 - j:143 - j], T.E[:, j::8]) for j in range(8)])], "CE E", "pZ", LN, 8.5, start=False)
        add("v", lambda q: q.transpose(T.ZT[:], T.pZ[:, 0:LN]), "pZ", "ZT", LN, 1, 9.9)
        scan(T.ZR[:], T.RSZ[:], T.ZT[:], OP.mult, OP.max, "RSZ ZT", "ZR", LN, 1, 10.3)
        cp(T.BI[:], T.ZR[:, 15::16], "ZR", "BI", 12, 10.6)
        b, c = 0 if s < 7 else 12, 36 if s < 5 else 24
        ts(T.QI[:, 12:24], T.BI[:], 511, None, OP.bitwise_and, None, "BI", "QIv", at=10.9)
        if s < 7:
            ts(T.QI[:, 0:12], T.BI[:], 9, 15, OP.logical_shift_right, OP.bitwise_and, "BI", "QIj", at=10.95)
        if s < 5:
            ts(T.QI[:, 24:36], T.BI[:], 3, None, OP.bitwise_and, None, "BI", "QIo", at=11.0)
        cp(T.QH[:, b:c], T.QI[:, b:c], "QIv QIj QIo", "QH", c - b, 11.3)
        mm([(T.pZ[:, 256 + b + e:256 + c:2], [(T.MM[:, 256 * e + 128 * h:256 * e + 128 * h + 128], T.QH[:, b + h:c:2]) for h in range(2)])
            for e in range(2)], names("MM", 4) + " QH", "pZ", 18, 11.6)
        lists(s, b, c, T.pZ[:, 256 + b:256 + c], "pZ", 12.0)

    def lists(s, b, c, src, r, at):
        a, u = 36 * s, 36 * (s % 2)
        tt(T.QF[:, a + b:a + c], src, T.UB[:, u + b:u + c], OP.add, r + " UB", "QF%d" % s, c - b, 1, at)
        cp(T.QU[:, a + b:a + c], T.QF[:, a + b:a + c], "QF%d" % s, "QU%d" % s, c - b, at + 0.3)
        if s < 5:
            mm([(T.pZ[:, 304:328], [(ROT, T.QF[:, a + 12:a + 36], 4)])], "PW QF%d" % s, "pZ", 24, at + 0.4)
            lin(T.VS[:, 24 * s:24 * s + 24], T.pZ[:, 304:328], 1.0, 0.0, "pZ", "VS%d" % s, 24, 1, "s", at + 0.9)
            send("v", s, T.VS, "VS%d" % s, at + 1.2)

    def lowest(t):
        a, m = NN + t % 2, 288 * t
        during(t - 1 if t else -1.6)
        mm([(T.pR[:, 320:416], [(T.RF[:, 0:128], T.KN[:, a::4], 4), (T.RF[:, 128:256], T.KN[:, a + 2::4], 4)])], "RF0 RF1 NM", "pR", 96, 5.9)
        ts(T.ML[:, m + LN:m + 288], T.pR[:, 320:416], -65536.0, None, OP.add, None, "pR", "MS%d" % t, 96, at=8.2)
        mm([(T.pR[:, 128:320], [(dg(3), two(T.RL, t, 7, 1536, 8, 1536)), (sel(0), T.NV[:]), (dg(0), T.ONES[:])])],
           "DG3 RL%d SEL0 NV DG0 ONES" % (t % 2), "pR", LN, 8.6)
        tt(T.pR[:, 128:320], T.pR[:, 128:320], T.KN[:, a::2], OP.min, "pR NM", "pR", LN, 1, 10.1)
        scan(T.RR[:], T.RST[:], T.A[:], OP.add, OP.min, "RST " + names("A", 3), "RR", 1536, 1, 8.6)
        tt(T.MI[:], T.pR[:, 128:320], T.RR[:, 7::8], OP.min, "RR pR", "MI", LN, 1, 10.5)
        ts(T.MJ[:], T.MI[:], 4095, None, OP.bitwise_and, None, "MI", "MJ", LN, at=11.4)
        ts(T.M16[:], T.MJ[:], -1536.0, None, OP.add, None, "MJ", "M16", LN, at=11.9)
        mm([(T.pR[:, 128 + 96 * h:224 + 96 * h], [(rw(2 * h), T.M16[:, 0::2]), (rw(2 * h + 1), T.M16[:, 1::2])]) for h in range(2)],
           names("RW", 4) + " M16", "pR", 96, 12.2)
        ts(T.ML[:, m:m + LN], T.pR[:, 128:320], 1536.0, None, OP.add, None, "pR", "ML%d" % t, LN, at=12.6)

    def rewrite_low(t):
        par = t % 2
        during(t - 1 if t else -0.3)
        ts(T.LG[:, 24 * t:24 * t + 24], land(T, "v", t), 4.0, None, OP.add, None, "", "Lv%d" % t, 24, at=4.9, wait=arrival("v", t),
           **(dict(behind=t - 1) if t else {}))
        lin(two(T.GT, t), T.TB[:, 0:392].indirect(T.LG[:, 24 * t:24 * t + 12]), 1.0, 0.0, names("TB", 4) + " Lv%d" % t, "GT%d" % par, LN, "g", "s", 5.6)
        mm([(T.pU[:, 0:LN], [(dg(7), two(T.KV, t)), (dg(8), T.ONES[:]), (IH, two(T.GT, t))])], "PH0 KV%d GT%d DG7 DG8 ONES" % (par, par), "pU",
           LN, 7.0)
        tt(T.T2[:], T.pU[:, 0:LN], T.KL[:, par::2], OP.min, "pU KL", "T2", LN, 1, 8.4)
        act(T.KL[:, par::2], T.T2[:], AF.Abs, "T2", "KL", LN, 1, 8.8)

    def rewrite(t):
        par, s = t % 2, t + 2
        during(t)
        lin(T.GW[:], T.TC[:, 0:400].indirect(T.QU[:, 36 * s:36 * s + 24]), 1.0, 0.0, names("TC", 10) + " QU%d" % s, "GW", NN, "g", "s", -0.8)
        mm([(T.pU[:, 0:LN], [(dg(7), two(T.KV, t)), (IH, two(T.GT, t)), (dg(1), T.ONES[:]), (rw(3), GU), (rw(1), GJ)]),
            (T.pU[:, LN:NN], [(sel(16), T.NV[:]), (dg(2), T.ONES[:]), (rw(1), GU), (rw(3), GJ)])],
           "PH0 KV%d GT%d GW NV DG1 DG2 DG7 SEL16 RW1 RW3 ONES" % (par, par), "pU", LN, -0.1)
        tt(T.T3[:], T.pU[:, 0:NN], T.KN[:, par::2], OP.min, "pU KA NM", "T3", NN, 1, 1.65)
        act(T.KN[:, par::2], T.T3[:], AF.Abs, "T3", "KA NM", NN, 1, 2.6)

    def ahead(t):
        during(t - 1)
        for k in range(8):
            act(two(T.LLO, t, k, 1536, 8, 1536), T.S[:, 8 * (t % 2) + k::16], AF.Sigmoid, "S", "LL%d_%d" % (t % 2, k), at=8.5, after=["ONES"])
        if t < 5:
            lin(T.HG[:], Sw.indirect(ol(t)), 1.0, 0.0, "S QU%d" % t, "HG", LN, "g", "s", 7.0)

    def h8(t):
        par = t % 2
        during(t - 1)
        mm([(T.pN[:, 0:LN], [(ROT, T.HG[:], 4), (T.BR[:], sg(t, 1728, 1920))])], "PW HG BR SG%db" % par, "pN", LN, 9.0)
        act(two(T.H8, t), T.pN[:, 0:LN], AF.Relu, "pN", "H8%d" % par, LN, 1, 9.6, bias=32.0, scale=8.0)

    def products(t):
        par, m = t % 2, 288 * t
        turn = ROT if t < 5 else IDN
        during(t)
        for i, (a, b, kind) in enumerate(PARTS):
            act(T.LHI[:, 8 * a:8 * b], Sw.indirect(T.ML[:, m + LN + a // 2:m + LN + b // 2]), AF.Sigmoid, "S MS%d" % t, "LH%d" % i, 8 * (b - a), "g",
                0.3 + a / 85, after=["ONES"])
        for i, (a, b, kind) in enumerate(PARTS):
            bank, n = "p" + kind, b - a
            for u in range(2):
                p, at = 1536 * u + 8 * a, 0.3 + (2 * a + u * n) / 90
                left = T.LHI[:, 8 * a:8 * b] if u else two(T.LLO, t, 8 * a, 8 * b, 1, 1536)
                r = "P%d%d" % (i, u)
                tt(T.P[:, p:p + 8 * n], Sw.indirect(T.ML[:, m + 96 * u + a // 2:m + 96 * u + b // 2]), left, OP.mult,
                   "S ML%d " % t + ("LH%d" % i if u else names("LL%d_" % par, 8)), r, 8 * n, "g", at)
                if u == 1 and i >= SCAN_FROM[t]:
                    w = "PS" if i == len(PARTS) - 1 else "PS%d" % i
                    scan(T.PS[:, 8 * a:8 * b], T.RS8[:, 0:8 * n], T.P[:, p:p + 8 * n], OP.mult, OP.add, "RS8 " + r, w, 8 * n, 1, at + 0.7)
                    terms, r = [(turn, T.PS[:, 8 * a + 7:8 * b:8], 4)], w
                else:
                    terms = [(turn, T.P[:, p + k:p + 8 * n:8], 4) for k in range(8)]
                c, d = SPAN[kind]
                if u == 0 and t < 5 and a == c:
                    mm([(T[bank][:, c:d], [(IDN, two(T.H8, t, c, d), 4)])], "PW H8%d" % par, bank, d - c, at - 0.8, stop=False)
                mm([(T[bank][:, a:b], terms)], "PW " + r, bank, n, 1.2 * at + 0.8, start=(u == 0 and t == 5), stop=(u == 1 and (b == d or t == 5)))
            if b == SPAN[kind][1]:
                a, at = SPAN[kind][0], 1.2 * at + 1.2
                if t < 5:
                    act(T.TS[:, LN * t + a:LN * t + b], T[bank][:, a:b], AF.Sigmoid, bank, "TS%d%s" % (t, kind), b - a, 1, at, scale=0.25)
                    send(kind, t, T.TS, "TS%d%s" % (t, kind), at + 0.2)
                else:
                    lin(T.OB[:, 5 * LN + a:5 * LN + b], T[bank][:, a:b], 1.0, 0.0, bank, "OB5" + kind, b - a, 1, "s", at)
                    dma("y", "do" + kind, [(T.yo[:, 5 * LN + a:5 * LN + b], T.OB[:, 5 * LN + a:5 * LN + b])], "OB5" + kind, "", at + 0.2)

    def settle(t):
        during(t)
        a = LN * t
        dma("y", "dt%d" % t, [(T.SL[0:112, :], T.TS[16:128, a:a + LN]), (T.SL[112:128, :], T.TS[0:16, a:a + LN])], "TS%da TS%db A0" % (t, t),
            "SL", 6.8)
        ts(Sw.indirect(ol(t)), T.SL[:], 2.0, -1.0, OP.mult, OP.add, "SL QU%d" % t, "S", LN, "s", at=10.8)
        for kind, (a, b) in SPAN.items():
            tt(T.OB[:, LN * t + a:LN * t + b], T["p" + kind][:, a:b], two(T.H8, t, a, b), OP.subtract, "p%s H8%d" % (kind, t % 2),
               "OB%d%s" % (t, kind), b - a, 1, 8.5 + a / 35)
        for kind, (a, b) in SPAN.items():
            ts(Sw.indirect(T.LG[:, 24 * t + 12 + a // 16:24 * t + 12 + b // 16]), land(T, kind, t), 2.0, -1.0, OP.mult, OP.add,
               "Lv%d" % t, "S", b - a, "s", at=12.8 + a / 256, wait=arrival(kind, t))

    during(-3)
    iota(T.NR[:], [[8, NN]], 0, 1, "NR0 NR1", NN, False)
    dma("y", "dpv", [(T.PVI[0:8, :], T.pv[:])], "", "PVI", 0.0)
    dma("s", "dka", [(T.KI[:], T.ka[:])], "", "KI", 0.0)
    dma("y", "dx", [(T.X[:], T.xa[:])], "", "X", 0.1)
    dma("y", "dn0", [(T.NR[16 * a + 8:16 * a + 16, :], T.nm[8 * a:8 * a + 8, :]) for a in range(4)], "", "NR0", 3.0)
    dma("y", "dn1", [(T.NR[16 * a + 8:16 * a + 16, :], T.nm[8 * a:8 * a + 8, :]) for a in range(4, 8)], "", "NR1", 3.0)
    iota(T.CI[:, 0:1], [[0, 1]], 0, 1, "CI0", 1, False)
    iota(T.IO[:], [[1, 392]], 0, 0, "IO", 392)
    iota(T.GB[:], [[0, 2], [16, 8], [0, 16]], 0, 0, "GB", 256)
    dma("g", "ds0", [(T.S[:], T.s0[:])], "", "S", 12.0, 1400)
    iota(T.UBI[:], [[256, 12]], 0, 0, "UBI", 12)
    iota(T.UN[:], [[-1, 2], [-2, LN]], 192, 0, "UN", NN)
    fill(T.RST[:], 4096, "RST", 1536)
    fill(T.RS8[:], 1, "RS8", 512)
    fill(T.RSZ[:], 1, "RSZ", LN)
    for i, mask in enumerate((15, 112, 16, 31)):
        ts(T.CI[:, i + 1:i + 2], T.CI[:, 0:1], mask, None, OP.bitwise_and, None, "CI0", "CI%d" % (i + 1), 1)
    cp(T.CF[:], T.CI[:], names("CI", 5), "CF", 5)
    act(T.ONES[:], T.IO[:, 0:LN], AF.Sigmoid, "IO", "ONES", at=1.0, bias=30.0, scale=0.0, c=1520)
    for c, src, x, o, w in ((LO, KC, 8.0, OP.is_lt, "LO"), (HI, KC, 8.0, OP.is_ge, "HI"), (L4, KC, 4.0, OP.is_lt, "L4"),
                            (H0, HC, 0.0, OP.is_equal, "H0"), (H1, HC, 16.0, OP.is_equal, "H1")):
        ts(c, src, x, None, o, None, "CF", w, 1)
    ts(T.EQ[:], T.IO[:, 0:16], KC, None, OP.is_equal, None, "IO CF", "EQ", 16)
    ts(CC, GC, LO, -1.0, OP.mult, OP.mult, "CF LO", "CC", 1)
    ts(M4, KC, 12.0, HI, OP.is_lt, OP.mult, "CF HI", "M4", 1)
    ts(R1, LO, L4, 2048.0, OP.subtract, OP.mult, "LO L4", "R1", 1)
    for c, src, x, y, r, w in ((B8C, T.CF[:, 4:5], 16.0, 15.0, "CF", "B8C"),
                               (VS_, HI, -2 * BIG, BIG, "HI", "VS_"), (VB, HI, 897 * BIG, -193 * BIG, "HI", "VB"),
                               (R0, HI, 2752.0, 0.0, "HI", "R0"), (K16, KC, 16.0, 0.0, "CF", "K16"), (G15, GC, 1.0, 15.0, "CF", "G15"),
                               (R2, LO, BIG - 2048, 2048.0, "LO", "R2"), (DL, HI, 4289.0, -193.0, "HI", "DL"),
                               (DN, HI, -198144.0, 131072.0, "HI", "DN"), (D0, KC, -1024.0, 7168.0 + 192.0, "CF", "D0"),
                               (D1, T.EQ[:, 8:9], 2293760.0, 0.0, "EQ", "D1"), (DC, D0, LO, D1, "D0 D1 LO", "DC"),
                               (LS, LO, 1 / BIG, 0.0, "LO", "LS"), (LB, LO, BIG, 0.0, "LO", "LB"), (M4, M4, -1 / BIG, 0.0, "M4", "M4"),
                               (L4, L4, -2.0, 0.0, "L4", "L4")):
        lin(c, src, x, y, r, w)
    ts(T.B8[:], T.IO[:, 0:144], B8C, None, OP.is_equal, None, "IO B8C", "B8", 144)
    ts(T.BLK[:], T.GB[:, 0:128], GC, None, OP.is_equal, None, "GB CF", "BLK", 128)
    for h in range(2):
        ts(T.PH[:, 128 * h:128 * h + 128], T.IO[:, 0:128], PC, None, OP.is_equal, None, "IO CF", "PH%d" % h, 128)
    lin(T.PW[:], T.PH[:], 1.0, 0.0, "PH0 PH1", "PW", 256, 1, "s")
    for j in range(16):
        lin(sel(j), T.BLK[:], T.EQ[:, j:j + 1], 0.0, "BLK EQ", "SEL%d" % j, 128, 0.5, "vs"[j // 8])
    lin(sel(16), sel(0), -1.0, 0.0, "SEL0", "SEL16", 128, 0.5)
    cp(T.PV16[0:8, :], T.PVI[0:8, :], "PVI", "PV16", NN)
    for par in range(2):
        mm([(T.pa[:, 12 * par:12 * par + 12], [(T.B8[0:8, 15 - p:143 - p], T.PV16[0:8, 2 * p + par::32]) for p in range(16)])], "B8 PV16", "pa", 12)
        cp(T.QA[:, 24 * par:24 * par + 12], T.pa[:, 12 * par:12 * par + 12], "pa", "QA%d" % par)
    ts(KAw, T.KI[:], 1.0, None, OP.add, None, "KI", "KA", NN)
    dma("y", "dsp", [(T.KI[32 * i:32 * i + 8, :], T.sp[:, NN * i:NN * i + NN]) for i in range(3)], "", "KI", None)
    ts(T.SP16[0:72, :], T.KI[0:72, :], 512.0, None, OP.add, None, "KI", "SP16", NN)
    ts(NMw, T.NR[:], CC, 65536.0, OP.add, OP.add, "CC NR0 NR1", "NM", NN)
    for par in range(2):
        for k in range(8):
            lin(two(T.XU, par, k, 1536, 8, 1536), T.X[:, par::2], 1.0, 0.0, "X", "XU%d_%d" % (par, k), LN, 0.5, "vg"[par], pool=True)
    lin(rw(0), IH, LO, 0.0, "PH0 LO", "RW0", 128, 0.5)
    lin(rw(1), T.PH[:, 120:248], LO, 0.0, "PH0 PH1 LO", "RW1", 128, 0.5)
    for i, a in enumerate((8, 0)):
        lin(rw(2 + i), T.PH[:, a:a + 128], HI, 0.0, "PH0 PH1 HI", "RW%d" % (2 + i), 128, 0.5)
        lin(T.RF[:, 128 * i:128 * i + 128], T.PH[:, a:a + 128], HI, 0.0, "PH0 PH1 HI", "RF%d" % i, 128, 1, "s")
    ms(T.UB[:], 0.0, "UB", 72)
    for par in range(2):
        ms(T.UB[:, 36 * par:36 * par + 12], float(NN), "UB", 12)
        ts(T.UB[:, 36 * par + 24:36 * par + 36], T.UBI[:], K16, 8.0 * par, OP.add, OP.add, "UBI K16", "UB")
    for s in range(2):
        ts(T.QA[:, 24 * s + 12:24 * s + 24], T.QA[:, 24 * s:24 * s + 12], 3, None, OP.bitwise_and, None, "QA%d" % s, "QB%d" % s)
        lists(s, 12, 36, T.QA[:, 24 * s:24 * s + 24], "QA%d QB%d" % (s, s), 10.0 + 18 * s)
    lin(T.EQN[:], T.EQ[:], -1.0, 0.0, "EQ", "EQN", 16)
    lin(T.EQB[:, 0:4], T.EQ[:, 8:12], -1856.0, R0, "EQ R0", "EQBa", 4)
    lin(T.EQB[:, 4:8], T.EQ[:, 4:8], -1852.0, R1, "EQ R1", "EQBb", 4)
    lin(T.EQB[:, 16:24], T.EQ[:, 0:8], -BIG, R2, "EQ R2", "EQBd", 8)
    lin(T.EQB[:, 8:16], T.EQ[:, 8:16], -1856.0, 0.0, "EQ", "EQBc", 8)
    tt(T.EQB[:, 8:16], T.EQB[:, 8:16], T.EQB[:, 16:24], OP.add, "EQBc EQBd", "EQBc", 8, 2)
    for i, (c, r) in enumerate(((1536.0, ""), (-193.0, ""), (DN, "DN"), (1 / 4096, ""), (LS, "LS"), (DC, "DC"), (LB, "LB"), (M4, "M4 PH1"), (DL, "DL"))):
        lin(dg(i), T.PH[:, 8:136] if i == 7 else IH, c, 0.0, "PH0 " + r, "DG%d" % i, 128, 0.5)
    ts(T.BR[:], T.GB[:, 112:240], GC, L4, OP.is_equal, OP.mult, "GB CF L4", "BR", 128)
    ms(T.RSZ[:, 0::16], 0.0, "RSZ", 12)
    ts(T.CE[:], T.IO[:, 0:144], G15, 8192.0, OP.is_equal, OP.mult, "IO G15", "CE", 144)
    lin(T.CS[:], T.CE[:], 16.0, 0.0, "CE", "CS", 144, 0.5)
    ms(T.RST[:, 0::8], 1.0e12, "RST", LN, 0.5)
    ms(T.RS8[:, 0::8], 0.0, "RS8", 64, 0.5)
    for i, (a, c, r) in enumerate(((0, H0, "H0"), (112, H0, "H0"), (16, H1, "H1"), (0, H1, "H1"))):
        lin(T.MM[:, 128 * i:128 * i + 128], T.PH[:, a:a + 128], c, 0.0, "PH0 PH1 " + r, "MM%d" % i, 128, 0.5)
    for r in range(4):
        lin(T.pU[:, r:NN:4], T.IO[:, r:NN:4], T.EQN[:, 8 + r:9 + r], T.EQB[:, r:r + 1], "IO EQN EQBa", "pU", 96, 1, "s")
    tt(T.KL[:], T.pU[:, 0:NN], KAw, OP.max, "pU KA", "KL", NN)
    for r in range(4):
        lin(T.TB[:, r::4], T.IO[:, r::4], T.EQN[:, 4 + r:5 + r], T.EQB[:, 4 + r:5 + r], "IO EQN EQBb", "TB%d" % r, 98, 1, "s")
    for r in range(8):
        lin(T.TC[:, r:NN:8], T.IO[:, r:NN:8], T.EQN[:, 8 + r:9 + r], T.EQB[:, 8 + r:9 + r], "IO EQN EQBc", "TC%d" % r, 48, 1, "s")
    ts(T.TC[:, NN::2], T.IO[:, 0:8], -7.0, HI, OP.add, OP.mult, "IO HI", "TC8", 8)
    ms(T.TC[:, NN + 1::2], BIG, "TC9", 8)

    def early(t):
        low(t)
        if t > 0:
            rewrite(t - 1)
        choose(t)
        if t < 5:
            rewrite_low(t)

    def late(t):
        high(t)
        lowest(t)

    early(0)
    late(0)
    ahead(0)
    h8(0)
    early(1)
    for t in range(RO):
        if t < 5:
            late(t + 1)
        if t < 4:
            early(t + 2)
        products(t)
        if t < 5:
            ahead(t + 1)
            settle(t)
        if t < 4:
            h8(t + 1)
    during(5)
    n5 = 5 * LN
    dma("y", "do0", [(T.yo[0:112, 0:n5], T.OB[16:128, 0:n5]), (T.yo[112:128, 0:n5], T.OB[0:16, 0:n5])],
        " ".join("OB%d%s" % (i, x) for i in range(5) for x in "ab"), "", 0.0)
    for par in range(2):
        lin(T.YP[:, par::2], T.IO[:, 0:NN].indirect(vl(6 + par)), 1.0, 0.0, "IO QU%d" % (6 + par), "YP%d" % par, LN, "g", "s", 2.0)
    dma("y", "dyp", [(T.yp[:], T.YP[0::16, :])], "YP0 YP1", "", 3.0)

    count = emit(g, T, ops)
    for s in sorted(count):
        g.wait_ge(T.sem[s], count[s])
    g.wait_ge(T.sem.lsent, sent[0])
